import numpy as np
import ml_dtypes


def mxq(x, axis, fmt="e4m3"):
    dtype, down = {"e4m3": (ml_dtypes.float8_e4m3fn, 7), "e5m2": (ml_dtypes.float8_e5m2, 14)}[fmt]
    v = np.moveaxis(np.asarray(x, np.float32).astype(ml_dtypes.bfloat16).astype(np.float64), axis, -1)
    blocks = v.reshape(v.shape[:-1] + (-1, 32))
    amax = np.abs(blocks).max(-1, keepdims=True)
    byte = np.maximum(np.where(amax > 0, np.frexp(amax)[1] - 1 + 127, 0) - down, 1)
    scale = np.exp2(byte - 127.0)
    codes = (blocks / scale).astype(np.float32).astype(dtype).astype(np.float64)
    return np.moveaxis((codes * scale).reshape(v.shape), -1, axis)


WIDE = False


def mx_kscale(k):
    if not WIDE:
        return np.ones(k)
    levels = np.array([10, -10, 5, -5, 0])
    if k % 512:
        return np.exp2(np.random.permutation(np.resize(levels, k // 32))).repeat(32)
    a = np.empty((k // 512, 16))
    for p in range(k // 512):
        a[p, :8] = np.random.permutation(np.resize(levels, 8))
        for g in range(8):
            far = levels[np.abs(levels - a[p, g]) >= 10]
            a[p, g + 8] = far[np.random.randint(len(far))]
    return np.exp2(a.ravel()).repeat(32)


def f64(x):
    return np.asarray(x).astype(np.float64)


def striped(idx):
    return np.tile(idx.reshape(-1, 16).T, (8, 1)).astype(np.uint16)


def unstriped(offs):
    return offs[:16].T.reshape(-1).astype(np.int64)


E2M1 = np.array([0.0, 0.5, 1.0, 1.5, 2.0, 3.0, 4.0, 6.0, -0.0, -0.5, -1.0, -1.5, -2.0, -3.0, -4.0, -6.0])


def pack_fp4(w):
    k, n = w.shape
    w = f64(np.asarray(w, np.float32).astype(ml_dtypes.bfloat16)).reshape(k // 32, 32, n)
    amax = np.abs(w).max(1)
    mant, ex = np.frexp(amax / 6.0)
    byte = np.clip(np.where(amax > 0, np.where(mant > 0.5, ex, ex - 1) + 127, 1), 1, 254)
    scaled = (w * np.exp2(127.0 - byte)[:, None, :]).reshape(k, n).astype(np.float32)
    c = np.ascontiguousarray(scaled.reshape(k // 512, 128, 4, n).transpose(0, 1, 3, 2)).astype(ml_dtypes.float4_e2m1fn).view(np.uint8) & 0xF
    words = (c[..., 0::2] | (c[..., 1::2] << 4)).reshape(k // 512, 128, 2 * n)
    return np.ascontiguousarray(words), np.ascontiguousarray(byte.astype(np.uint8).reshape(k // 512, 16, n))


def unpack_fp4(words, scales):
    g, _, n = scales.shape
    words = np.ascontiguousarray(words).reshape(g, 128, n, 2)
    nib = np.empty((g, 128, n, 4), np.uint8)
    nib[..., 0::2] = words & 0xF
    nib[..., 1::2] = words >> 4
    vals = E2M1[nib] * np.repeat(np.exp2(scales.astype(np.float64) - 127.0), 8, axis=1)[..., None]
    return vals.transpose(0, 1, 3, 2).reshape(g * 512, n)


def relu(v):
    return np.maximum(v, 0.0)


K, T, S, V, H, N = 1024, 2048, 1024, 512, 512, 256


def setup_inputs():
    n = np.random.standard_normal
    s = mx_kscale(K)[:, None]
    u = mx_kscale(H)
    packed_w2 = pack_fp4(n((H, N)) / np.sqrt(2 * H) / u[:, None])
    packed_w3 = pack_fp4(n((H, N)) / np.sqrt(2 * H) / u[:, None])
    return {
        "xT": (n((K, T)) * s).astype(np.float32),
        "w1": (n((K, H)) / np.sqrt(K) / s * u).astype(np.float32),
        "w2_words": packed_w2[0],
        "w2_scales": packed_w2[1],
        "w3_words": packed_w3[0],
        "w3_scales": packed_w3[1],
        "offs": striped(np.random.permutation(T)[:S]),
    }


def reference(xT, w1, w2_words, w2_scales, w3_words, w3_scales, offs):
    xq = mxq(f64(xT)[:, unstriped(offs)], 0, "e4m3")
    h = relu(mxq(f64(w1), 0, "e4m3").T @ xq)
    low = 0.5 * (h[:, :V] + h[:, V:2 * V])
    high = 0.5 * (h[:, :V] - h[:, V:2 * V])
    return unpack_fp4(w2_words, w2_scales).T @ mxq(low, 0, "e4m3") + unpack_fp4(w3_words, w3_scales).T @ mxq(high, 0, "e4m3")

@@ -1,0 +1,199 @@
+from contextlib import ExitStack
+
+import concourse.mybir as mybir
+
+K, T, S, V, H, N = 1024, 2048, 1024, 512, 512, 256
+FLOPS = 2 * K * H * S + 2 * 2 * H * N * V
+
+F32 = mybir.dt.float32
+BF16 = mybir.dt.bfloat16
+U32 = mybir.dt.uint32
+I32 = mybir.dt.int32
+U16 = mybir.dt.uint16
+U8 = mybir.dt.uint8
+FP8X4 = mybir.dt.float8_e4m3fn_x4
+FP4X4 = mybir.dt.float4_e2m1fn_x4
+ACT = mybir.ActivationFunctionType
+ALU = mybir.AluOpType
+
+P = 128
+PACK = 4
+K_PASS = P * PACK
+PASSES = K // K_PASS
+X_LOADS = ((512, 512, 1024), (1024, 512, 256, 256))
+Q_COLS = 512
+X_SHARE = ((12, 12, 13), (12, 10, 8, 6))
+W_LOADS = ((256, 256), (256, 256))
+W_SHARE = ((16, 16), (16, 16))
+HALF = 256
+STEP = 128
+
+
+def tile_picked_haar_relu_e_kernel(
+    tc, xT, w1, w2_words, w2_scales, w3_words, w3_scales, offs, out
+):
+    nc = tc.nc
+    with ExitStack() as ctx:
+        keep = ctx.enter_context(tc.tile_pool(name="keep", bufs=1))
+        psum = ctx.enter_context(tc.psum_pool(name="psum", bufs=1))
+
+        offsets = keep.tile([P, S // 16], U16, name="offsets")
+        x_scales = keep.tile([P, T], U8, name="x_scales", align_bytes=64)
+        nc.gpsimd.memset(x_scales[:].bitcast(I32), 0)
+        w23_scales = keep.tile([P, 2, N], U8, name="w23_scales", align_bytes=64)
+        nc.gpsimd.memset(w23_scales[:].rearrange("p a n -> p (a n)").bitcast(I32), 0)
+        w23_words = keep.tile([P, 2, 2 * N], U8, name="w23_words", align_bytes=64)
+
+        x_words = [keep.tile([P, T], U32, name="x_words%d" % z, align_bytes=64) for z in range(PASSES)]
+        g_words = {}
+        g_scales = {}
+        w_words = [keep.tile([P, H], U32, name="w_words%d" % z, align_bytes=64) for z in range(PASSES)]
+        w_scales = [keep.tile([P, H], U8, name="w_scales%d" % z, align_bytes=64) for z in range(PASSES)]
+
+        def piece(d, c):
+            a = (d * V + c * HALF) // 16
+            return offsets[:, a : a + HALF // 16]
+
+        def gather(window, c, name, tag):
+            dst = keep.tile([P, 2 * HALF], window.dtype, name=name, tag=tag, align_bytes=64)
+            for d in range(2):
+                nc.vector.tensor_copy(dst[:, d * HALF : (d + 1) * HALF], window[:].indirect(piece(d, c)))
+            return dst
+
+        def x_stretch(z, raw, lo, width, col, share):
+            grouped = keep.tile([P, width, PACK], BF16, name="x_bf%d_%d" % (z, col), align_bytes=64)
+            cut = width * share // 16
+            src = raw[:, :, lo : lo + width]
+            for eng, a, b in (("s", 0, cut), ("v", cut, width)):
+                if a == b:
+                    continue
+                o = grouped[:, a:b, :].rearrange("p (c i) t -> p c t i", i=4)
+                s = src[:, :, a:b].rearrange("p t (c i) -> p c t i", i=4)
+                if eng == "s":
+                    nc.scalar.activation(o, s, ACT.Copy)
+                else:
+                    nc.vector.tensor_copy(o, s)
+            nc.vector.quantize_mx(
+                out=x_words[z][:, col : col + width].bitcast(FP8X4),
+                scales=x_scales[4 * z : P, col : col + width],
+                in_=grouped[:].rearrange("p w t -> p (w t)"),
+            )
+
+        first = True
+        for z in range(PASSES):
+            rows = xT[z * K_PASS : (z + 1) * K_PASS, :].rearrange("(p t) w -> p t w", t=PACK)
+            col = 0
+            for n, width in enumerate(X_LOADS[z]):
+                raw = keep.tile([P, PACK, width], F32, name="x_raw%d_%d" % (z, col))
+                nc.sync.dma_start(raw[:], rows[:, :, col : col + width])
+                if first:
+                    nc.sync.dma_start(offsets[:], offs)
+                    first = False
+                for lo in range(0, width, Q_COLS):
+                    x_stretch(z, raw, lo, min(Q_COLS, width), col + lo, X_SHARE[z][n])
+                col = col + width
+            if z == 0:
+                for c in range(2):
+                    g_words[0, c] = gather(x_words[0], c, "g_words0%d" % c, "g_words0%d" % c)
+
+        w_bf = [keep.tile([P, PACK, P, PACK], BF16, name="w_bf%d" % z, tag="w_bf%d" % z, align_bytes=64) for z in range(PASSES)]
+
+        def w_load(z):
+            rows = w1[z * K_PASS : (z + 1) * K_PASS, :].rearrange("(p j) c -> p j c", j=PACK)
+            col = 0
+            for n, width in enumerate(W_LOADS[z]):
+                raw = keep.tile([P, PACK, width], F32, name="w_raw%d_%d" % (z, col))
+                nc.sync.dma_start(raw[:], rows[:, :, col : col + width])
+                m0, ms = col // PACK, width // PACK
+                cut = ms * W_SHARE[z][n] // 16
+                for eng, a, b in (("s", 0, cut), ("v", cut, ms)):
+                    if a == b:
+                        continue
+                    o = w_bf[z][:, :, m0 + a : m0 + b, :].rearrange("p t m j -> p m j t")
+                    s = raw[:, :, PACK * a : PACK * b].rearrange("p j (m t) -> p m j t", t=PACK)
+                    if eng == "s":
+                        nc.scalar.activation(o, s, ACT.Copy)
+                    else:
+                        nc.vector.tensor_copy(o, s)
+                col = col + width
+
+        def w_quant(z):
+            for t in range(PACK):
+                nc.vector.quantize_mx(
+                    out=w_words[z][:, t * P : (t + 1) * P].bitcast(FP8X4),
+                    scales=w_scales[z][:, t * P : (t + 1) * P],
+                    in_=w_bf[z][:, t, :, :].rearrange("p m j -> p (m j)"),
+                )
+
+        banks = [[psum.tile([P, 2 * HALF], F32, name="h%d%d" % (c, t), tag="bank%d" % (PACK * c + t)) for t in range(PACK)] for c in range(2)]
+
+        def first_product(z, c):
+            for t in range(PACK):
+                nc.tensor.matmul_mx(
+                    out=banks[c][t][:],
+                    lhsT=w_words[z][:, t * P : (t + 1) * P].bitcast(FP8X4),
+                    lhsT_scale=w_scales[z][:, t * P : (t + 1) * P],
+                    rhs=g_words[z, c][:].bitcast(FP8X4),
+                    rhs_scale=g_scales[c][4 * z : P, :],
+                    start=(z == 0),
+                    stop=(z == PASSES - 1),
+                )
+
+        g_scales[0] = gather(x_scales, 0, "g_scales0", "g_scales0")
+        g_words[1, 0] = gather(x_words[1], 0, "g_words10", "g_words10")
+        w_load(0)
+        w_quant(0)
+        first_product(0, 0)
+        g_scales[1] = gather(x_scales, 1, "g_scales1", "w_bf0")
+        w_load(1)
+        w_quant(1)
+        first_product(1, 0)
+        g_words[1, 1] = gather(x_words[1], 1, "g_words11", "w_bf1")
+        first_product(0, 1)
+        first_product(1, 1)
+
+        for a, (words, scales) in enumerate(((w2_words, w2_scales), (w3_words, w3_scales))):
+            nc.sync.dma_start(w23_words[:, a, :].bitcast(I32), words[0].bitcast(I32))
+            for q in range(4):
+                nc.sync.dma_start(w23_scales[32 * q : 32 * q + 4, a, :].bitcast(I32), scales[0, 4 * q : 4 * q + 4, :].bitcast(I32))
+
+        out_v = out.rearrange("(m p) v -> p m v", p=P)
+        halves = []
+        for j in range(V // STEP):
+            c, h = divmod(j, HALF // STEP)
+            r = keep.tile([P, 2, PACK, STEP], F32, name="relu%d" % j)
+            for t in range(PACK):
+                src = banks[c][t][:].rearrange("p (d v) -> p d v", d=2)[:, :, h * STEP : (h + 1) * STEP]
+                nc.scalar.activation(r[:, :, t, :], src, ACT.Relu, scale=0.5)
+            halves.append(r)
+
+        for j in range(V // STEP):
+            r = halves[j]
+            a_in = r[:, 0, :, :].rearrange("p t (c i) -> p c t i", i=4)
+            b_in = r[:, 1, :, :].rearrange("p t (c i) -> p c t i", i=4)
+            bands = []
+            for b, op in enumerate((ALU.add, ALU.subtract)):
+                band = keep.tile([P, STEP, PACK], BF16, name="band%d_%d" % (j, b), align_bytes=64)
+                nc.vector.tensor_tensor(band[:].rearrange("p (c i) t -> p c t i", i=4), a_in, b_in, op)
+                bands.append(band)
+            codes = []
+            for b in range(2):
+                words = keep.tile([P, STEP], U32, name="band_words%d_%d" % (j, b), align_bytes=64)
+                scales = keep.tile([P, STEP], U8, name="band_scales%d_%d" % (j, b), align_bytes=64)
+                nc.vector.quantize_mx(out=words[:].bitcast(FP8X4), scales=scales[:], in_=bands[b][:].rearrange("p v t -> p (v t)"))
+                codes.append((words, scales))
+            acc = psum.tile([P, 2 * HALF], F32, name="acc%d" % j, tag="bank%d" % j)
+            for m in range(N // P):
+                for b in range(2):
+                    nc.tensor.matmul_mx(
+                        out=acc[:, m * STEP : (m + 1) * STEP],
+                        lhsT=w23_words[:, b, 2 * P * m : 2 * P * (m + 1)].bitcast(FP4X4),
+                        lhsT_scale=w23_scales[:, b, P * m : P * (m + 1)],
+                        rhs=codes[b][0][:].bitcast(FP8X4),
+                        rhs_scale=codes[b][1][:],
+                        start=(b == 0),
+                        stop=(b == 1),
+                    )
+            res = keep.tile([P, N // P, STEP], F32, name="res%d" % j)
+            nc.scalar.activation(res[:].rearrange("p m v -> p (m v)"), acc[:, 0 : 2 * STEP], ACT.Copy)
+            nc.sync.dma_start(out_v[:, :, j * STEP : (j + 1) * STEP], res[:])

@@ -20,11 +20,11 @@ P = 128
 PACK = 4
 K_PASS = P * PACK
 PASSES = K // K_PASS
-X_LOADS = ((512, 512, 1024), (1024, 512, 256, 256))
+X_LOADS = ((1024, 1024), (1024, 512, 512))
 Q_COLS = 512
-X_SHARE = ((12, 12, 13), (12, 10, 8, 6))
-W_LOADS = ((256, 256), (256, 256))
-W_SHARE = ((16, 16), (16, 16))
+X_SHARE = ((11, 8), (10, 8, 6))
+W_LOADS = ((512,), (512,))
+W_SHARE = ((16,), (9,))
 HALF = 256
 STEP = 128
 
@@ -125,10 +125,8 @@ def tile_picked_haar_relu_e_kernel(
                     in_=w_bf[z][:, t, :, :].rearrange("p m j -> p (m j)"),
                 )
 
-        banks = [[psum.tile([P, 2 * HALF], F32, name="h%d%d" % (c, t), tag="bank%d" % (PACK * c + t)) for t in range(PACK)] for c in range(2)]
-
-        def first_product(z, c):
-            for t in range(PACK):
+        def first_product(banks, z, c, t):
+            if True:
                 nc.tensor.matmul_mx(
                     out=banks[c][t][:],
                     lhsT=w_words[z][:, t * P : (t + 1) * P].bitcast(FP8X4),
@@ -141,16 +139,32 @@ def tile_picked_haar_relu_e_kernel(
 
         g_scales[0] = gather(x_scales, 0, "g_scales0", "g_scales0")
         g_words[1, 0] = gather(x_words[1], 0, "g_words10", "g_words10")
+        g_words[1, 1] = gather(x_words[1], 1, "g_words11", "g_words11")
+        for n in range(4):
+            z = n // 2
+            idle = psum.tile([P, 2 * HALF], F32, name="idle%d" % n, tag="bank%d" % (PACK + n))
+            nc.tensor.matmul_mx(
+                out=idle[:],
+                lhsT=g_words[z, 0][:, 0:P].bitcast(FP8X4),
+                lhsT_scale=g_scales[0][4 * z : P, 0:P],
+                rhs=g_words[z, 0][:].bitcast(FP8X4),
+                rhs_scale=g_scales[0][4 * z : P, :],
+                start=True,
+                stop=True,
+            )
+        banks = [[psum.tile([P, 2 * HALF], F32, name="h%d%d" % (c, t), tag="bank%d" % (PACK * c + t)) for t in range(PACK)] for c in range(2)]
         w_load(0)
         w_quant(0)
-        first_product(0, 0)
-        g_scales[1] = gather(x_scales, 1, "g_scales1", "w_bf0")
+        for t in range(PACK):
+            first_product(banks, 0, 0, t)
         w_load(1)
         w_quant(1)
-        first_product(1, 0)
-        g_words[1, 1] = gather(x_words[1], 1, "g_words11", "w_bf1")
-        first_product(0, 1)
-        first_product(1, 1)
+        for t in range(PACK):
+            first_product(banks, 1, 0, t)
+        g_scales[1] = gather(x_scales, 1, "g_scales1", "w_bf1")
+        for t in range(PACK):
+            first_product(banks, 0, 1, t)
+            first_product(banks, 1, 1, t)
 
         for a, (words, scales) in enumerate(((w2_words, w2_scales), (w3_words, w3_scales))):
             nc.sync.dma_start(w23_words[:, a, :].bitcast(I32), words[0].bitcast(I32))

@@ -20,13 +20,14 @@ P = 128
 PACK = 4
 K_PASS = P * PACK
 PASSES = K // K_PASS
-X_LOADS = ((1024, 1024), (1024, 512, 512))
+X_LOADS = ((1024, 512, 512), (1024, 512, 512))
 Q_COLS = 512
-X_SHARE = ((11, 8), (10, 8, 6))
-W_LOADS = ((512,), (512,))
-W_SHARE = ((16,), (9,))
+X_SHARE = ((11, 9, 7), (9, 8, 6))
+W_SHARE = (16, 12)
+W_QUANT = (4, 2)
 HALF = 256
 STEP = 128
+WARM = 4
 
 
 def tile_picked_haar_relu_e_kernel(
@@ -39,132 +40,131 @@ def tile_picked_haar_relu_e_kernel(
 
         offsets = keep.tile([P, S // 16], U16, name="offsets")
         x_scales = keep.tile([P, T], U8, name="x_scales", align_bytes=64)
-        nc.gpsimd.memset(x_scales[:].bitcast(I32), 0)
+        nc.vector.memset(x_scales[:].bitcast(I32), 0)
         w23_scales = keep.tile([P, 2, N], U8, name="w23_scales", align_bytes=64)
-        nc.gpsimd.memset(w23_scales[:].rearrange("p a n -> p (a n)").bitcast(I32), 0)
+        nc.vector.memset(w23_scales[:].rearrange("p a n -> p (a n)").bitcast(I32), 0)
         w23_words = keep.tile([P, 2, 2 * N], U8, name="w23_words", align_bytes=64)
 
         x_words = [keep.tile([P, T], U32, name="x_words%d" % z, align_bytes=64) for z in range(PASSES)]
-        g_words = {}
-        g_scales = {}
         w_words = [keep.tile([P, H], U32, name="w_words%d" % z, align_bytes=64) for z in range(PASSES)]
         w_scales = [keep.tile([P, H], U8, name="w_scales%d" % z, align_bytes=64) for z in range(PASSES)]
 
-        def piece(d, c):
-            a = (d * V + c * HALF) // 16
-            return offsets[:, a : a + HALF // 16]
-
-        def gather(window, c, name, tag):
-            dst = keep.tile([P, 2 * HALF], window.dtype, name=name, tag=tag, align_bytes=64)
-            for d in range(2):
-                nc.vector.tensor_copy(dst[:, d * HALF : (d + 1) * HALF], window[:].indirect(piece(d, c)))
+        def gather_words(z):
+            dst = keep.tile([P, 2, 2, HALF], U32, name="g_words%d" % z, align_bytes=64)
+            if z == 0:
+                nc.vector.tensor_copy(dst[:].rearrange("p c d v -> p d c v"), x_words[z][:].indirect(offsets[:]))
+                return dst
+            for c in range(2):
+                for d in range(2):
+                    a = (d * V + c * HALF) // 16
+                    nc.vector.tensor_copy(dst[:, c, d, :], x_words[z][:].indirect(offsets[:, a : a + HALF // 16]))
             return dst
+
+        def gather_scales(c, tag):
+            dst = keep.tile([P, 2 * HALF], U8, name="g_scales%d" % c, tag=tag, align_bytes=64)
+            for d in range(2):
+                a = (d * V + c * HALF) // 16
+                nc.vector.tensor_copy(dst[:, d * HALF : (d + 1) * HALF], x_scales[:].indirect(offsets[:, a : a + HALF // 16]))
+            return dst
+
+        def split_cast(views, cut, width):
+            if cut > 0:
+                o, s = views(0, cut)
+                nc.scalar.activation(o, s, ACT.Copy)
+            if cut < width:
+                o, s = views(cut, width)
+                nc.vector.tensor_copy(o, s)
 
         def x_stretch(z, raw, lo, width, col, share):
             grouped = keep.tile([P, width, PACK], BF16, name="x_bf%d_%d" % (z, col), align_bytes=64)
-            cut = width * share // 16
-            src = raw[:, :, lo : lo + width]
-            for eng, a, b in (("s", 0, cut), ("v", cut, width)):
-                if a == b:
-                    continue
-                o = grouped[:, a:b, :].rearrange("p (c i) t -> p c t i", i=4)
-                s = src[:, :, a:b].rearrange("p t (c i) -> p c t i", i=4)
-                if eng == "s":
-                    nc.scalar.activation(o, s, ACT.Copy)
-                else:
-                    nc.vector.tensor_copy(o, s)
+            split_cast(
+                lambda a, b: (
+                    grouped[:, a:b, :].rearrange("p (c i) t -> p c t i", i=4),
+                    raw[:, :, lo + a : lo + b].rearrange("p t (c i) -> p c t i", i=4),
+                ),
+                width * share // 16,
+                width,
+            )
             nc.vector.quantize_mx(
                 out=x_words[z][:, col : col + width].bitcast(FP8X4),
                 scales=x_scales[4 * z : P, col : col + width],
                 in_=grouped[:].rearrange("p w t -> p (w t)"),
             )
 
-        first = True
+        g_words = []
         for z in range(PASSES):
             rows = xT[z * K_PASS : (z + 1) * K_PASS, :].rearrange("(p t) w -> p t w", t=PACK)
             col = 0
             for n, width in enumerate(X_LOADS[z]):
                 raw = keep.tile([P, PACK, width], F32, name="x_raw%d_%d" % (z, col))
                 nc.sync.dma_start(raw[:], rows[:, :, col : col + width])
-                if first:
+                if z == 0 and n == 0:
                     nc.sync.dma_start(offsets[:], offs)
-                    first = False
                 for lo in range(0, width, Q_COLS):
                     x_stretch(z, raw, lo, min(Q_COLS, width), col + lo, X_SHARE[z][n])
                 col = col + width
-            if z == 0:
-                for c in range(2):
-                    g_words[0, c] = gather(x_words[0], c, "g_words0%d" % c, "g_words0%d" % c)
+            if z == PASSES - 1:
+                g_scales = [gather_scales(0, "g_scales0")]
+            g_words.append(gather_words(z))
 
-        w_bf = [keep.tile([P, PACK, P, PACK], BF16, name="w_bf%d" % z, tag="w_bf%d" % z, align_bytes=64) for z in range(PASSES)]
+        def picked(z, c):
+            return g_words[z][:, c, :, :].rearrange("p d v -> p (d v)")
 
-        def w_load(z):
-            rows = w1[z * K_PASS : (z + 1) * K_PASS, :].rearrange("(p j) c -> p j c", j=PACK)
-            col = 0
-            for n, width in enumerate(W_LOADS[z]):
-                raw = keep.tile([P, PACK, width], F32, name="w_raw%d_%d" % (z, col))
-                nc.sync.dma_start(raw[:], rows[:, :, col : col + width])
-                m0, ms = col // PACK, width // PACK
-                cut = ms * W_SHARE[z][n] // 16
-                for eng, a, b in (("s", 0, cut), ("v", cut, ms)):
-                    if a == b:
-                        continue
-                    o = w_bf[z][:, :, m0 + a : m0 + b, :].rearrange("p t m j -> p m j t")
-                    s = raw[:, :, PACK * a : PACK * b].rearrange("p j (m t) -> p m j t", t=PACK)
-                    if eng == "s":
-                        nc.scalar.activation(o, s, ACT.Copy)
-                    else:
-                        nc.vector.tensor_copy(o, s)
-                col = col + width
-
-        def w_quant(z):
-            for t in range(PACK):
-                nc.vector.quantize_mx(
-                    out=w_words[z][:, t * P : (t + 1) * P].bitcast(FP8X4),
-                    scales=w_scales[z][:, t * P : (t + 1) * P],
-                    in_=w_bf[z][:, t, :, :].rearrange("p m j -> p (m j)"),
-                )
-
-        def first_product(banks, z, c, t):
-            if True:
-                nc.tensor.matmul_mx(
-                    out=banks[c][t][:],
-                    lhsT=w_words[z][:, t * P : (t + 1) * P].bitcast(FP8X4),
-                    lhsT_scale=w_scales[z][:, t * P : (t + 1) * P],
-                    rhs=g_words[z, c][:].bitcast(FP8X4),
-                    rhs_scale=g_scales[c][4 * z : P, :],
-                    start=(z == 0),
-                    stop=(z == PASSES - 1),
-                )
-
-        g_scales[0] = gather(x_scales, 0, "g_scales0", "g_scales0")
-        g_words[1, 0] = gather(x_words[1], 0, "g_words10", "g_words10")
-        g_words[1, 1] = gather(x_words[1], 1, "g_words11", "g_words11")
-        for n in range(4):
-            z = n // 2
-            idle = psum.tile([P, 2 * HALF], F32, name="idle%d" % n, tag="bank%d" % (PACK + n))
+        def warm(n, z, c, d, width):
+            idle = psum.tile([P, 2 * HALF], F32, name="idle%d" % n, tag="bank%d" % (PACK + n % PACK))
             nc.tensor.matmul_mx(
-                out=idle[:],
-                lhsT=g_words[z, 0][:, 0:P].bitcast(FP8X4),
+                out=idle[:, 0:width],
+                lhsT=g_words[z][:, c, d, 0:P].bitcast(FP8X4),
                 lhsT_scale=g_scales[0][4 * z : P, 0:P],
-                rhs=g_words[z, 0][:].bitcast(FP8X4),
-                rhs_scale=g_scales[0][4 * z : P, :],
+                rhs=picked(0, 0)[:, 0:width].bitcast(FP8X4),
+                rhs_scale=g_scales[0][:, 0:width],
                 start=True,
                 stop=True,
             )
+
+        for n, args in enumerate(((0, 0, 0, HALF), (0, 0, 0, HALF), (0, 0, 0, 2 * HALF), (1, 0, 0, 2 * HALF), (1, 0, 1, 2 * HALF), (1, 1, 0, 2 * HALF))):
+            warm(n, *args)
         banks = [[psum.tile([P, 2 * HALF], F32, name="h%d%d" % (c, t), tag="bank%d" % (PACK * c + t)) for t in range(PACK)] for c in range(2)]
-        w_load(0)
-        w_quant(0)
+
+        def w_pass(z):
+            raw = keep.tile([P, PACK, H], F32, name="w_raw%d" % z)
+            nc.sync.dma_start(raw[:], w1[z * K_PASS : (z + 1) * K_PASS, :].rearrange("(p j) c -> p j c", j=PACK))
+            dealt = keep.tile([P, PACK, P, PACK], BF16, name="w_bf%d" % z, tag="w_bf%d" % z, align_bytes=64)
+            split_cast(
+                lambda a, b: (
+                    dealt[:, :, a:b, :].rearrange("p t m j -> p m j t"),
+                    raw[:, :, PACK * a : PACK * b].rearrange("p j (m t) -> p m j t", t=PACK),
+                ),
+                P * W_SHARE[z] // 16,
+                P,
+            )
+            for t in range(0, PACK, W_QUANT[z]):
+                cols = slice(t * P, (t + W_QUANT[z]) * P)
+                nc.vector.quantize_mx(
+                    out=w_words[z][:, cols].bitcast(FP8X4),
+                    scales=w_scales[z][:, cols],
+                    in_=dealt[:, t : t + W_QUANT[z], :, :].rearrange("p t m j -> p (t m j)"),
+                )
+
+        def first_product(z, c, t):
+            nc.tensor.matmul_mx(
+                out=banks[c][t][:],
+                lhsT=w_words[z][:, t * P : (t + 1) * P].bitcast(FP8X4),
+                lhsT_scale=w_scales[z][:, t * P : (t + 1) * P],
+                rhs=picked(z, c).bitcast(FP8X4),
+                rhs_scale=g_scales[c][4 * z : P, :],
+                start=(z == 0),
+                stop=(z == PASSES - 1),
+            )
+
+        for z in range(PASSES):
+            w_pass(z)
+            for t in range(PACK):
+                first_product(z, 0, t)
+        g_scales.append(gather_scales(1, "w_bf1"))
         for t in range(PACK):
-            first_product(banks, 0, 0, t)
-        w_load(1)
-        w_quant(1)
-        for t in range(PACK):
-            first_product(banks, 1, 0, t)
-        g_scales[1] = gather(x_scales, 1, "g_scales1", "w_bf1")
-        for t in range(PACK):
-            first_product(banks, 0, 1, t)
-            first_product(banks, 1, 1, t)
+            for z in range(PASSES):
+                first_product(z, 1, t)
 
         for a, (words, scales) in enumerate(((w2_words, w2_scales), (w3_words, w3_scales))):
             nc.sync.dma_start(w23_words[:, a, :].bitcast(I32), words[0].bitcast(I32))
@@ -181,33 +181,56 @@ def tile_picked_haar_relu_e_kernel(
                 nc.scalar.activation(r[:, :, t, :], src, ACT.Relu, scale=0.5)
             halves.append(r)
 
-        for j in range(V // STEP):
-            r = halves[j]
-            a_in = r[:, 0, :, :].rearrange("p t (c i) -> p c t i", i=4)
-            b_in = r[:, 1, :, :].rearrange("p t (c i) -> p c t i", i=4)
-            bands = []
-            for b, op in enumerate((ALU.add, ALU.subtract)):
-                band = keep.tile([P, STEP, PACK], BF16, name="band%d_%d" % (j, b), align_bytes=64)
-                nc.vector.tensor_tensor(band[:].rearrange("p (c i) t -> p c t i", i=4), a_in, b_in, op)
-                bands.append(band)
-            codes = []
-            for b in range(2):
-                words = keep.tile([P, STEP], U32, name="band_words%d_%d" % (j, b), align_bytes=64)
-                scales = keep.tile([P, STEP], U8, name="band_scales%d_%d" % (j, b), align_bytes=64)
-                nc.vector.quantize_mx(out=words[:].bitcast(FP8X4), scales=scales[:], in_=bands[b][:].rearrange("p v t -> p (v t)"))
-                codes.append((words, scales))
-            acc = psum.tile([P, 2 * HALF], F32, name="acc%d" % j, tag="bank%d" % j)
-            for m in range(N // P):
+        def second_product(dst, m, b, words, scales):
+            nc.tensor.matmul_mx(
+                out=dst,
+                lhsT=w23_words[:, b, 2 * P * m : 2 * P * (m + 1)].bitcast(FP4X4),
+                lhsT_scale=w23_scales[:, b, P * m : P * (m + 1)],
+                rhs=words[:, b * STEP : (b + 1) * STEP].bitcast(FP8X4),
+                rhs_scale=scales[:, b * STEP : (b + 1) * STEP],
+                start=(b == 0),
+                stop=(b == 1),
+            )
+
+        steps = V // STEP
+        bands = [keep.tile([P, 2, STEP, PACK], BF16, name="band%d" % j, align_bytes=64) for j in range(steps)]
+
+        def haar(j, b):
+            a_in = halves[j][:, 0, :, :].rearrange("p t (c i) -> p c t i", i=4)
+            b_in = halves[j][:, 1, :, :].rearrange("p t (c i) -> p c t i", i=4)
+            nc.vector.tensor_tensor(bands[j][:, b, :, :].rearrange("p (c i) t -> p c t i", i=4), a_in, b_in, (ALU.add, ALU.subtract)[b])
+
+        def finish(j):
+            words = keep.tile([P, 2 * STEP], U32, name="band_words%d" % j, align_bytes=64)
+            scales = keep.tile([P, 2 * STEP], U8, name="band_scales%d" % j, align_bytes=64)
+            cols = slice(j * STEP, (j + 1) * STEP)
+            band = bands[j]
+            if j < steps - 1:
+                nc.vector.quantize_mx(out=words[:].bitcast(FP8X4), scales=scales[:], in_=band[:].rearrange("p b v t -> p (b v t)"))
+                acc = psum.tile([P, 2 * HALF], F32, name="acc%d" % j, tag="bank%d" % (PACK + j))
+                for m in range(N // P):
+                    for b in range(2):
+                        second_product(acc[:, m * STEP : (m + 1) * STEP], m, b, words, scales)
+                res = keep.tile([P, N // P, STEP], F32, name="res%d" % j)
+                nc.scalar.activation(res[:].rearrange("p m v -> p (m v)"), acc[:, 0 : 2 * STEP], ACT.Copy)
+                nc.sync.dma_start(out_v[:, :, cols], res[:])
+            else:
+                accs = [psum.tile([P, 2 * HALF], F32, name="acc%d_%d" % (j, m), tag="bank%d" % m) for m in range(N // P)]
                 for b in range(2):
-                    nc.tensor.matmul_mx(
-                        out=acc[:, m * STEP : (m + 1) * STEP],
-                        lhsT=w23_words[:, b, 2 * P * m : 2 * P * (m + 1)].bitcast(FP4X4),
-                        lhsT_scale=w23_scales[:, b, P * m : P * (m + 1)],
-                        rhs=codes[b][0][:].bitcast(FP8X4),
-                        rhs_scale=codes[b][1][:],
-                        start=(b == 0),
-                        stop=(b == 1),
-                    )
-            res = keep.tile([P, N // P, STEP], F32, name="res%d" % j)
-            nc.scalar.activation(res[:].rearrange("p m v -> p (m v)"), acc[:, 0 : 2 * STEP], ACT.Copy)
-            nc.sync.dma_start(out_v[:, :, j * STEP : (j + 1) * STEP], res[:])
+                    bc = slice(b * STEP, (b + 1) * STEP)
+                    nc.vector.quantize_mx(out=words[:, bc].bitcast(FP8X4), scales=scales[:, bc], in_=band[:, b, :, :].rearrange("p v t -> p (v t)"))
+                    for m in range(N // P):
+                        second_product(accs[m][:, 0:STEP], m, b, words, scales)
+                res0 = keep.tile([P, STEP], F32, name="res_last0")
+                nc.scalar.activation(res0[:], accs[0][:, 0:STEP], ACT.Copy)
+                nc.scalar.dma_start(out_v[:, 0, cols], res0[:])
+                res1 = keep.tile([P, STEP], F32, name="res_last1")
+                nc.vector.tensor_copy(res1[:], accs[1][:, 0:STEP])
+                nc.sync.dma_start(out_v[:, 1, cols], res1[:])
+
+        for j in range(steps):
+            haar(j, 0)
+            if j > 0:
+                finish(j - 1)
+            haar(j, 1)
+        finish(steps - 1)

@@ -20,11 +20,11 @@ P = 128
 PACK = 4
 K_PASS = P * PACK
 PASSES = K // K_PASS
-X_LOADS = ((1024, 512, 512), (1024, 512, 512))
+X_LOADS = ((1024, 1024), (1024, 512, 512))
 Q_COLS = 512
-X_SHARE = ((11, 9, 7), (9, 8, 6))
-W_SHARE = (16, 12)
-W_QUANT = (4, 2)
+X_SHARE = ((11, 8), (10, 8, 6))
+W_SHARE = (16, 9)
+W_QUANT = (2, 2)
 HALF = 256
 STEP = 128
 WARM = 4
@@ -50,14 +50,14 @@ def tile_picked_haar_relu_e_kernel(
         w_scales = [keep.tile([P, H], U8, name="w_scales%d" % z, align_bytes=64) for z in range(PASSES)]
 
         def gather_words(z):
-            dst = keep.tile([P, 2, 2, HALF], U32, name="g_words%d" % z, align_bytes=64)
+            dst = keep.tile([P, S], U32, name="g_words%d" % z, align_bytes=64)
             if z == 0:
-                nc.vector.tensor_copy(dst[:].rearrange("p c d v -> p d c v"), x_words[z][:].indirect(offsets[:]))
+                nc.vector.tensor_copy(dst[:], x_words[z][:].indirect(offsets[:]))
                 return dst
             for c in range(2):
                 for d in range(2):
-                    a = (d * V + c * HALF) // 16
-                    nc.vector.tensor_copy(dst[:, c, d, :], x_words[z][:].indirect(offsets[:, a : a + HALF // 16]))
+                    a = d * V + c * HALF
+                    nc.vector.tensor_copy(dst[:, a : a + HALF], x_words[z][:].indirect(offsets[:, a // 16 : (a + HALF) // 16]))
             return dst
 
         def gather_scales(c, tag):
@@ -67,13 +67,19 @@ def tile_picked_haar_relu_e_kernel(
                 nc.vector.tensor_copy(dst[:, d * HALF : (d + 1) * HALF], x_scales[:].indirect(offsets[:, a : a + HALF // 16]))
             return dst
 
-        def split_cast(views, cut, width):
+        def split_cast(views, cut, width, halve=False):
             if cut > 0:
                 o, s = views(0, cut)
-                nc.scalar.activation(o, s, ACT.Copy)
+                if halve:
+                    nc.scalar.activation(o, s, ACT.Copy, scale=0.5)
+                else:
+                    nc.scalar.activation(o, s, ACT.Copy)
             if cut < width:
                 o, s = views(cut, width)
-                nc.vector.tensor_copy(o, s)
+                if halve:
+                    nc.vector.tensor_scalar(o, s, 0.5, None, ALU.mult)
+                else:
+                    nc.vector.tensor_copy(o, s)
 
         def x_stretch(z, raw, lo, width, col, share):
             grouped = keep.tile([P, width, PACK], BF16, name="x_bf%d_%d" % (z, col), align_bytes=64)
@@ -107,24 +113,20 @@ def tile_picked_haar_relu_e_kernel(
                 g_scales = [gather_scales(0, "g_scales0")]
             g_words.append(gather_words(z))
 
-        def picked(z, c):
-            return g_words[z][:, c, :, :].rearrange("p d v -> p (d v)")
-
-        def warm(n, z, c, d, width):
-            idle = psum.tile([P, 2 * HALF], F32, name="idle%d" % n, tag="bank%d" % (PACK + n % PACK))
+        def warm(n, lhsT, lhsT_scale):
+            idle = psum.tile([P, PACK * STEP], F32, name="idle%d" % n, tag="bank%d" % (PACK + n % PACK))
             nc.tensor.matmul_mx(
-                out=idle[:, 0:width],
-                lhsT=g_words[z][:, c, d, 0:P].bitcast(FP8X4),
-                lhsT_scale=g_scales[0][4 * z : P, 0:P],
-                rhs=picked(0, 0)[:, 0:width].bitcast(FP8X4),
-                rhs_scale=g_scales[0][:, 0:width],
+                out=idle[:],
+                lhsT=lhsT.bitcast(FP8X4),
+                lhsT_scale=lhsT_scale,
+                rhs=g_words[0][:, 0 : 2 * HALF].bitcast(FP8X4),
+                rhs_scale=g_scales[0][:],
                 start=True,
                 stop=True,
             )
 
-        for n, args in enumerate(((0, 0, 0, HALF), (0, 0, 0, HALF), (0, 0, 0, 2 * HALF), (1, 0, 0, 2 * HALF), (1, 0, 1, 2 * HALF), (1, 1, 0, 2 * HALF))):
-            warm(n, *args)
-        banks = [[psum.tile([P, 2 * HALF], F32, name="h%d%d" % (c, t), tag="bank%d" % (PACK * c + t)) for t in range(PACK)] for c in range(2)]
+        for n, a in enumerate((V, HALF, V + HALF)):
+            warm(n, g_words[1][:, a : a + P], g_scales[0][4:P, 0:P])
 
         def w_pass(z):
             raw = keep.tile([P, PACK, H], F32, name="w_raw%d" % z)
@@ -137,7 +139,11 @@ def tile_picked_haar_relu_e_kernel(
                 ),
                 P * W_SHARE[z] // 16,
                 P,
+                True,
             )
+            return dealt
+
+        def w_quant(z, dealt):
             for t in range(0, PACK, W_QUANT[z]):
                 cols = slice(t * P, (t + W_QUANT[z]) * P)
                 nc.vector.quantize_mx(
@@ -146,25 +152,40 @@ def tile_picked_haar_relu_e_kernel(
                     in_=dealt[:, t : t + W_QUANT[z], :, :].rearrange("p t m j -> p (t m j)"),
                 )
 
-        def first_product(z, c, t):
+        steps = V // STEP
+        dealt = [w_pass(z) for z in range(PASSES)]
+        w_quant(0, dealt[0])
+        for n in range(2):
+            cols = slice(2 * n * P, (2 * n + 1) * P)
+            warm(3 + n, w_words[0][:, cols], w_scales[0][:, cols])
+        banks = [[psum.tile([P, PACK, STEP], F32, name="h%d%d" % (j, d), tag="bank%d" % (2 * j + d)) for d in range(2)] for j in range(steps)]
+
+        def first_product(z, j, d, t):
+            c, h = divmod(j, HALF // STEP)
+            a = d * V + j * STEP
+            b = d * HALF + h * STEP
             nc.tensor.matmul_mx(
-                out=banks[c][t][:],
+                out=banks[j][d][:, t, :],
                 lhsT=w_words[z][:, t * P : (t + 1) * P].bitcast(FP8X4),
                 lhsT_scale=w_scales[z][:, t * P : (t + 1) * P],
-                rhs=picked(z, c).bitcast(FP8X4),
-                rhs_scale=g_scales[c][4 * z : P, :],
+                rhs=g_words[z][:, a : a + STEP].bitcast(FP8X4),
+                rhs_scale=g_scales[c][4 * z : P, b : b + STEP],
                 start=(z == 0),
                 stop=(z == PASSES - 1),
             )
 
-        for z in range(PASSES):
-            w_pass(z)
-            for t in range(PACK):
-                first_product(z, 0, t)
+        w_quant(1, dealt[1])
         g_scales.append(gather_scales(1, "w_bf1"))
-        for t in range(PACK):
-            for z in range(PASSES):
-                first_product(z, 1, t)
+        halves = []
+        for j in range(steps):
+            r = keep.tile([P, STEP, PACK], F32, name="relu%d" % j)
+            for d in (1, 0):
+                for t in range(PACK):
+                    for z in range(PASSES):
+                        first_product(z, j, d, t)
+                if d == 1:
+                    nc.scalar.activation(r[:], banks[j][d][:].rearrange("p t v -> p v t"), ACT.Relu)
+            halves.append(r)
 
         for a, (words, scales) in enumerate(((w2_words, w2_scales), (w3_words, w3_scales))):
             nc.sync.dma_start(w23_words[:, a, :].bitcast(I32), words[0].bitcast(I32))
@@ -172,14 +193,6 @@ def tile_picked_haar_relu_e_kernel(
                 nc.sync.dma_start(w23_scales[32 * q : 32 * q + 4, a, :].bitcast(I32), scales[0, 4 * q : 4 * q + 4, :].bitcast(I32))
 
         out_v = out.rearrange("(m p) v -> p m v", p=P)
-        halves = []
-        for j in range(V // STEP):
-            c, h = divmod(j, HALF // STEP)
-            r = keep.tile([P, 2, PACK, STEP], F32, name="relu%d" % j)
-            for t in range(PACK):
-                src = banks[c][t][:].rearrange("p (d v) -> p d v", d=2)[:, :, h * STEP : (h + 1) * STEP]
-                nc.scalar.activation(r[:, :, t, :], src, ACT.Relu, scale=0.5)
-            halves.append(r)
 
         def second_product(dst, m, b, words, scales):
             nc.tensor.matmul_mx(
@@ -192,13 +205,19 @@ def tile_picked_haar_relu_e_kernel(
                 stop=(b == 1),
             )
 
-        steps = V // STEP
-        bands = [keep.tile([P, 2, STEP, PACK], BF16, name="band%d" % j, align_bytes=64) for j in range(steps)]
+        bands = [keep.tile([P, 2, STEP * PACK], BF16, name="band%d" % j, align_bytes=64) for j in range(steps)]
 
         def haar(j, b):
-            a_in = halves[j][:, 0, :, :].rearrange("p t (c i) -> p c t i", i=4)
-            b_in = halves[j][:, 1, :, :].rearrange("p t (c i) -> p c t i", i=4)
-            nc.vector.tensor_tensor(bands[j][:, b, :, :].rearrange("p (c i) t -> p c t i", i=4), a_in, b_in, (ALU.add, ALU.subtract)[b])
+            nc.vector.scalar_tensor_tensor(
+                bands[j][:, b, :].rearrange("p (v t) -> p v t", t=PACK),
+                banks[j][0][:].rearrange("p t v -> p v t"),
+                0.0,
+                halves[j][:],
+                ALU.max,
+                (ALU.add, ALU.subtract)[b],
+            )
+
+        res_first = keep.tile([P, N // P, 2 * STEP], F32, name="res_first")
 
         def finish(j):
             words = keep.tile([P, 2 * STEP], U32, name="band_words%d" % j, align_bytes=64)
@@ -206,19 +225,24 @@ def tile_picked_haar_relu_e_kernel(
             cols = slice(j * STEP, (j + 1) * STEP)
             band = bands[j]
             if j < steps - 1:
-                nc.vector.quantize_mx(out=words[:].bitcast(FP8X4), scales=scales[:], in_=band[:].rearrange("p b v t -> p (b v t)"))
-                acc = psum.tile([P, 2 * HALF], F32, name="acc%d" % j, tag="bank%d" % (PACK + j))
+                nc.vector.quantize_mx(out=words[:].bitcast(FP8X4), scales=scales[:], in_=band[:].rearrange("p b w -> p (b w)"))
+                acc = psum.tile([P, N // P, 2 * STEP], F32, name="acc%d" % j, tag="bank%d" % (2 * j + 1))
                 for m in range(N // P):
                     for b in range(2):
-                        second_product(acc[:, m * STEP : (m + 1) * STEP], m, b, words, scales)
-                res = keep.tile([P, N // P, STEP], F32, name="res%d" % j)
-                nc.scalar.activation(res[:].rearrange("p m v -> p (m v)"), acc[:, 0 : 2 * STEP], ACT.Copy)
-                nc.sync.dma_start(out_v[:, :, cols], res[:])
+                        second_product(acc[:, m, 0:STEP], m, b, words, scales)
+                if j < 2:
+                    nc.scalar.activation(res_first[:, :, cols], acc[:, :, 0:STEP], ACT.Copy)
+                    if j == 1:
+                        nc.sync.dma_start(out_v[:, :, 0 : 2 * STEP], res_first[:])
+                else:
+                    res = keep.tile([P, N // P, STEP], F32, name="res%d" % j)
+                    nc.scalar.activation(res[:], acc[:, :, 0:STEP], ACT.Copy)
+                    nc.sync.dma_start(out_v[:, :, cols], res[:])
             else:
-                accs = [psum.tile([P, 2 * HALF], F32, name="acc%d_%d" % (j, m), tag="bank%d" % m) for m in range(N // P)]
+                accs = [psum.tile([P, 2 * HALF], F32, name="acc%d_%d" % (j, m), tag="bank%d" % (2 * m)) for m in range(N // P)]
                 for b in range(2):
                     bc = slice(b * STEP, (b + 1) * STEP)
-                    nc.vector.quantize_mx(out=words[:, bc].bitcast(FP8X4), scales=scales[:, bc], in_=band[:, b, :, :].rearrange("p v t -> p (v t)"))
+                    nc.vector.quantize_mx(out=words[:, bc].bitcast(FP8X4), scales=scales[:, bc], in_=band[:, b, :])
                     for m in range(N // P):
                         second_product(accs[m][:, 0:STEP], m, b, words, scales)
                 res0 = keep.tile([P, STEP], F32, name="res_last0")

@@ -20,14 +20,16 @@ P = 128
 PACK = 4
 K_PASS = P * PACK
 PASSES = K // K_PASS
-X_LOADS = ((1024, 1024), (1024, 512, 512))
-Q_COLS = 512
-X_SHARE = ((11, 8), (10, 8, 6))
-W_SHARE = (16, 9)
-W_QUANT = (2, 2)
-HALF = 256
+LIST_ROWS = 16
+SCALE_ROWS = 4
+HALF = V // 2
 STEP = 128
-WARM = 4
+STEPS = V // STEP
+
+X_LOADS = ((1024, 1024), (1024, 512, 512))
+X_STRETCH = 512
+X_ON_SCALAR = ((11, 7), (9, 8, 6))
+W_ON_SCALAR = (16, 8)
 
 
 def tile_picked_haar_relu_e_kernel(
@@ -38,7 +40,8 @@ def tile_picked_haar_relu_e_kernel(
         keep = ctx.enter_context(tc.tile_pool(name="keep", bufs=1))
         psum = ctx.enter_context(tc.psum_pool(name="psum", bufs=1))
 
-        offsets = keep.tile([P, S // 16], U16, name="offsets")
+        offsets = keep.tile([P, S // LIST_ROWS], U16, name="offsets")
+
         x_scales = keep.tile([P, T], U8, name="x_scales", align_bytes=64)
         nc.vector.memset(x_scales[:].bitcast(I32), 0)
         w23_scales = keep.tile([P, 2, N], U8, name="w23_scales", align_bytes=64)
@@ -49,55 +52,46 @@ def tile_picked_haar_relu_e_kernel(
         w_words = [keep.tile([P, H], U32, name="w_words%d" % z, align_bytes=64) for z in range(PASSES)]
         w_scales = [keep.tile([P, H], U8, name="w_scales%d" % z, align_bytes=64) for z in range(PASSES)]
 
+        def entries(d, c):
+            first = d * V + c * HALF
+            return offsets[:, first // LIST_ROWS : (first + HALF) // LIST_ROWS]
+
         def gather_words(z):
-            dst = keep.tile([P, S], U32, name="g_words%d" % z, align_bytes=64)
-            if z == 0:
-                nc.vector.tensor_copy(dst[:], x_words[z][:].indirect(offsets[:]))
-                return dst
+            picked = keep.tile([P, S], U32, name="picked_words%d" % z, align_bytes=64)
+            if z < PASSES - 1:
+                nc.vector.tensor_copy(picked[:], x_words[z][:].indirect(offsets[:]))
+                return picked
             for c in range(2):
                 for d in range(2):
-                    a = d * V + c * HALF
-                    nc.vector.tensor_copy(dst[:, a : a + HALF], x_words[z][:].indirect(offsets[:, a // 16 : (a + HALF) // 16]))
-            return dst
+                    first = d * V + c * HALF
+                    nc.vector.tensor_copy(picked[:, first : first + HALF], x_words[z][:].indirect(entries(d, c)))
+            return picked
 
         def gather_scales(c, tag):
-            dst = keep.tile([P, 2 * HALF], U8, name="g_scales%d" % c, tag=tag, align_bytes=64)
+            picked = keep.tile([P, 2 * HALF], U8, name="picked_scales%d" % c, tag=tag, align_bytes=64)
             for d in range(2):
-                a = (d * V + c * HALF) // 16
-                nc.vector.tensor_copy(dst[:, d * HALF : (d + 1) * HALF], x_scales[:].indirect(offsets[:, a : a + HALF // 16]))
-            return dst
+                nc.vector.tensor_copy(picked[:, d * HALF : (d + 1) * HALF], x_scales[:].indirect(entries(d, c)))
+            return picked
 
-        def split_cast(views, cut, width, halve=False):
-            if cut > 0:
-                o, s = views(0, cut)
-                if halve:
-                    nc.scalar.activation(o, s, ACT.Copy, scale=0.5)
-                else:
-                    nc.scalar.activation(o, s, ACT.Copy)
-            if cut < width:
-                o, s = views(cut, width)
-                if halve:
-                    nc.vector.tensor_scalar(o, s, 0.5, None, ALU.mult)
-                else:
-                    nc.vector.tensor_copy(o, s)
+        def quantise_x(z, raw, first, col, sixteenths):
+            grouped = keep.tile([P, X_STRETCH, PACK], BF16, name="x_bf%d_%d" % (z, col), align_bytes=64)
 
-        def x_stretch(z, raw, lo, width, col, share):
-            grouped = keep.tile([P, width, PACK], BF16, name="x_bf%d_%d" % (z, col), align_bytes=64)
-            split_cast(
-                lambda a, b: (
+            def views(a, b):
+                return (
                     grouped[:, a:b, :].rearrange("p (c i) t -> p c t i", i=4),
-                    raw[:, :, lo + a : lo + b].rearrange("p t (c i) -> p c t i", i=4),
-                ),
-                width * share // 16,
-                width,
-            )
+                    raw[:, :, first + a : first + b].rearrange("p t (c i) -> p c t i", i=4),
+                )
+
+            cut = X_STRETCH * sixteenths // 16
+            nc.scalar.activation(*views(0, cut), ACT.Copy)
+            nc.vector.tensor_copy(*views(cut, X_STRETCH))
             nc.vector.quantize_mx(
-                out=x_words[z][:, col : col + width].bitcast(FP8X4),
-                scales=x_scales[4 * z : P, col : col + width],
+                out=x_words[z][:, col : col + X_STRETCH].bitcast(FP8X4),
+                scales=x_scales[SCALE_ROWS * z : P, col : col + X_STRETCH],
                 in_=grouped[:].rearrange("p w t -> p (w t)"),
             )
 
-        g_words = []
+        picked_words = []
         for z in range(PASSES):
             rows = xT[z * K_PASS : (z + 1) * K_PASS, :].rearrange("(p t) w -> p t w", t=PACK)
             col = 0
@@ -106,93 +100,113 @@ def tile_picked_haar_relu_e_kernel(
                 nc.sync.dma_start(raw[:], rows[:, :, col : col + width])
                 if z == 0 and n == 0:
                     nc.sync.dma_start(offsets[:], offs)
-                for lo in range(0, width, Q_COLS):
-                    x_stretch(z, raw, lo, min(Q_COLS, width), col + lo, X_SHARE[z][n])
+                for first in range(0, width, X_STRETCH):
+                    quantise_x(z, raw, first, col + first, X_ON_SCALAR[z][n])
                 col = col + width
             if z == PASSES - 1:
-                g_scales = [gather_scales(0, "g_scales0")]
-            g_words.append(gather_words(z))
+                picked_scales = [gather_scales(0, "picked_scales0")]
+            picked_words.append(gather_words(z))
 
-        def warm(n, lhsT, lhsT_scale):
-            idle = psum.tile([P, PACK * STEP], F32, name="idle%d" % n, tag="bank%d" % (PACK + n % PACK))
+        def warm_up(n, lhsT, lhsT_scale):
+            idle = psum.tile([P, PACK * STEP], F32, name="idle%d" % n, tag="bank%d" % (STEPS + n % STEPS))
             nc.tensor.matmul_mx(
                 out=idle[:],
                 lhsT=lhsT.bitcast(FP8X4),
                 lhsT_scale=lhsT_scale,
-                rhs=g_words[0][:, 0 : 2 * HALF].bitcast(FP8X4),
-                rhs_scale=g_scales[0][:],
+                rhs=picked_words[0][:, 0 : 2 * HALF].bitcast(FP8X4),
+                rhs_scale=picked_scales[0][:],
                 start=True,
                 stop=True,
             )
 
-        for n, a in enumerate((V, HALF, V + HALF)):
-            warm(n, g_words[1][:, a : a + P], g_scales[0][4:P, 0:P])
+        for n, first in enumerate((V, HALF, V + HALF)):
+            warm_up(n, picked_words[1][:, first : first + P], picked_scales[0][SCALE_ROWS:P, 0:P])
 
-        def w_pass(z):
+        def cast_w(z):
             raw = keep.tile([P, PACK, H], F32, name="w_raw%d" % z)
             nc.sync.dma_start(raw[:], w1[z * K_PASS : (z + 1) * K_PASS, :].rearrange("(p j) c -> p j c", j=PACK))
             dealt = keep.tile([P, PACK, P, PACK], BF16, name="w_bf%d" % z, tag="w_bf%d" % z, align_bytes=64)
-            split_cast(
-                lambda a, b: (
+
+            def views(a, b):
+                return (
                     dealt[:, :, a:b, :].rearrange("p t m j -> p m j t"),
                     raw[:, :, PACK * a : PACK * b].rearrange("p j (m t) -> p m j t", t=PACK),
-                ),
-                P * W_SHARE[z] // 16,
-                P,
-                True,
-            )
+                )
+
+            cut = P * W_ON_SCALAR[z] // 16
+            nc.scalar.activation(*views(0, cut), ACT.Copy, scale=0.5)
+            if cut < P:
+                nc.vector.tensor_scalar(*views(cut, P), 0.5, None, ALU.mult)
             return dealt
 
-        def w_quant(z, dealt):
-            for t in range(0, PACK, W_QUANT[z]):
-                cols = slice(t * P, (t + W_QUANT[z]) * P)
+        def quantise_w(z, dealt):
+            for t in range(0, PACK, 2):
+                cols = slice(t * P, (t + 2) * P)
                 nc.vector.quantize_mx(
                     out=w_words[z][:, cols].bitcast(FP8X4),
                     scales=w_scales[z][:, cols],
-                    in_=dealt[:, t : t + W_QUANT[z], :, :].rearrange("p t m j -> p (t m j)"),
+                    in_=dealt[:, t : t + 2, :, :].rearrange("p t m j -> p (t m j)"),
                 )
 
-        steps = V // STEP
-        dealt = [w_pass(z) for z in range(PASSES)]
-        w_quant(0, dealt[0])
+        w_dealt = [cast_w(z) for z in range(PASSES)]
+        quantise_w(0, w_dealt[0])
         for n in range(2):
             cols = slice(2 * n * P, (2 * n + 1) * P)
-            warm(3 + n, w_words[0][:, cols], w_scales[0][:, cols])
-        banks = [[psum.tile([P, PACK, STEP], F32, name="h%d%d" % (j, d), tag="bank%d" % (2 * j + d)) for d in range(2)] for j in range(steps)]
+            warm_up(3 + n, w_words[0][:, cols], w_scales[0][:, cols])
+
+        banks = [
+            [psum.tile([P, PACK, STEP], F32, name="h%d%d" % (j, d), tag="bank%d" % (2 * j + d)) for d in range(2)]
+            for j in range(STEPS)
+        ]
 
         def first_product(z, j, d, t):
-            c, h = divmod(j, HALF // STEP)
-            a = d * V + j * STEP
-            b = d * HALF + h * STEP
+            c, within = divmod(j * STEP, HALF)
+            word_col = d * V + j * STEP
+            scale_col = d * HALF + within
             nc.tensor.matmul_mx(
                 out=banks[j][d][:, t, :],
                 lhsT=w_words[z][:, t * P : (t + 1) * P].bitcast(FP8X4),
                 lhsT_scale=w_scales[z][:, t * P : (t + 1) * P],
-                rhs=g_words[z][:, a : a + STEP].bitcast(FP8X4),
-                rhs_scale=g_scales[c][4 * z : P, b : b + STEP],
+                rhs=picked_words[z][:, word_col : word_col + STEP].bitcast(FP8X4),
+                rhs_scale=picked_scales[c][SCALE_ROWS * z : P, scale_col : scale_col + STEP],
                 start=(z == 0),
                 stop=(z == PASSES - 1),
             )
 
-        w_quant(1, dealt[1])
-        g_scales.append(gather_scales(1, "w_bf1"))
-        halves = []
-        for j in range(steps):
-            r = keep.tile([P, STEP, PACK], F32, name="relu%d" % j)
+        quantise_w(1, w_dealt[1])
+        picked_scales.append(gather_scales(1, "w_bf1"))
+
+        relu1 = []
+        for j in range(STEPS):
+            rectified = keep.tile([P, STEP, PACK], F32, name="relu1_%d" % j)
             for d in (1, 0):
                 for t in range(PACK):
                     for z in range(PASSES):
                         first_product(z, j, d, t)
                 if d == 1:
-                    nc.scalar.activation(r[:], banks[j][d][:].rearrange("p t v -> p v t"), ACT.Relu)
-            halves.append(r)
+                    nc.scalar.activation(rectified[:], banks[j][d][:].rearrange("p t v -> p v t"), ACT.Relu)
+            relu1.append(rectified)
 
-        for a, (words, scales) in enumerate(((w2_words, w2_scales), (w3_words, w3_scales))):
-            nc.sync.dma_start(w23_words[:, a, :].bitcast(I32), words[0].bitcast(I32))
-            for q in range(4):
-                nc.sync.dma_start(w23_scales[32 * q : 32 * q + 4, a, :].bitcast(I32), scales[0, 4 * q : 4 * q + 4, :].bitcast(I32))
+        for b, (words, scales) in enumerate(((w2_words, w2_scales), (w3_words, w3_scales))):
+            nc.sync.dma_start(w23_words[:, b, :].bitcast(I32), words[0].bitcast(I32))
+            for q in range(P // 32):
+                nc.sync.dma_start(
+                    w23_scales[32 * q : 32 * q + SCALE_ROWS, b, :].bitcast(I32),
+                    scales[0, SCALE_ROWS * q : SCALE_ROWS * (q + 1), :].bitcast(I32),
+                )
 
-        out_v = out.rearrange("(m p) v -> p m v", p=P)
+        out_rows = out.rearrange("(m p) v -> p m v", p=P)
+        bands = [keep.tile([P, 2, STEP * PACK], BF16, name="band%d" % j, align_bytes=64) for j in range(STEPS)]
+
+        def haar(j, b):
+            nc.vector.scalar_tensor_tensor(
+                bands[j][:, b, :].rearrange("p (v t) -> p v t", t=PACK),
+                banks[j][0][:].rearrange("p t v -> p v t"),
+                0.0,
+                relu1[j][:],
+                ALU.max,
+                (ALU.add, ALU.subtract)[b],
+            )
 
         def second_product(dst, m, b, words, scales):
             nc.tensor.matmul_mx(
@@ -205,56 +219,55 @@ def tile_picked_haar_relu_e_kernel(
                 stop=(b == 1),
             )
 
-        bands = [keep.tile([P, 2, STEP * PACK], BF16, name="band%d" % j, align_bytes=64) for j in range(steps)]
-
-        def haar(j, b):
-            nc.vector.scalar_tensor_tensor(
-                bands[j][:, b, :].rearrange("p (v t) -> p v t", t=PACK),
-                banks[j][0][:].rearrange("p t v -> p v t"),
-                0.0,
-                halves[j][:],
-                ALU.max,
-                (ALU.add, ALU.subtract)[b],
-            )
-
-        res_first = keep.tile([P, N // P, 2 * STEP], F32, name="res_first")
-
-        def finish(j):
+        def band_codes(j):
             words = keep.tile([P, 2 * STEP], U32, name="band_words%d" % j, align_bytes=64)
             scales = keep.tile([P, 2 * STEP], U8, name="band_scales%d" % j, align_bytes=64)
-            cols = slice(j * STEP, (j + 1) * STEP)
-            band = bands[j]
-            if j < steps - 1:
-                nc.vector.quantize_mx(out=words[:].bitcast(FP8X4), scales=scales[:], in_=band[:].rearrange("p b w -> p (b w)"))
-                acc = psum.tile([P, N // P, 2 * STEP], F32, name="acc%d" % j, tag="bank%d" % (2 * j + 1))
-                for m in range(N // P):
-                    for b in range(2):
-                        second_product(acc[:, m, 0:STEP], m, b, words, scales)
-                if j < 2:
-                    nc.scalar.activation(res_first[:, :, cols], acc[:, :, 0:STEP], ACT.Copy)
-                    if j == 1:
-                        nc.sync.dma_start(out_v[:, :, 0 : 2 * STEP], res_first[:])
-                else:
-                    res = keep.tile([P, N // P, STEP], F32, name="res%d" % j)
-                    nc.scalar.activation(res[:], acc[:, :, 0:STEP], ACT.Copy)
-                    nc.sync.dma_start(out_v[:, :, cols], res[:])
-            else:
-                accs = [psum.tile([P, 2 * HALF], F32, name="acc%d_%d" % (j, m), tag="bank%d" % (2 * m)) for m in range(N // P)]
-                for b in range(2):
-                    bc = slice(b * STEP, (b + 1) * STEP)
-                    nc.vector.quantize_mx(out=words[:, bc].bitcast(FP8X4), scales=scales[:, bc], in_=band[:, b, :])
-                    for m in range(N // P):
-                        second_product(accs[m][:, 0:STEP], m, b, words, scales)
-                res0 = keep.tile([P, STEP], F32, name="res_last0")
-                nc.scalar.activation(res0[:], accs[0][:, 0:STEP], ACT.Copy)
-                nc.scalar.dma_start(out_v[:, 0, cols], res0[:])
-                res1 = keep.tile([P, STEP], F32, name="res_last1")
-                nc.vector.tensor_copy(res1[:], accs[1][:, 0:STEP])
-                nc.sync.dma_start(out_v[:, 1, cols], res1[:])
+            return words, scales
 
-        for j in range(steps):
+        def multiply_bands(j, acc):
+            words, scales = band_codes(j)
+            nc.vector.quantize_mx(out=words[:].bitcast(FP8X4), scales=scales[:], in_=bands[j][:].rearrange("p b w -> p (b w)"))
+            for m in range(N // P):
+                for b in range(2):
+                    second_product(acc[:, m, :], m, b, words, scales)
+
+        acc_early = psum.tile([P, N // P, 2 * STEP], F32, name="acc_early", tag="bank%d" % (2 * STEPS - 1))
+        res_early = keep.tile([P, N // P, 2 * STEP], F32, name="res_early")
+
+        def finish(j):
+            cols = slice(j * STEP, (j + 1) * STEP)
+            if j < 2:
+                multiply_bands(j, acc_early[:, :, cols])
+                if j == 1:
+                    nc.scalar.activation(res_early[:], acc_early[:], ACT.Copy)
+                    nc.sync.dma_start(out_rows[:, :, 0 : 2 * STEP], res_early[:])
+            else:
+                acc = psum.tile([P, N // P, 2 * STEP], F32, name="acc%d" % j, tag="bank%d" % (2 * j + 1))
+                multiply_bands(j, acc[:, :, 0:STEP])
+                res = keep.tile([P, N // P, STEP], F32, name="res%d" % j)
+                nc.scalar.activation(res[:], acc[:, :, 0:STEP], ACT.Copy)
+                nc.sync.dma_start(out_rows[:, :, cols], res[:])
+
+        def finish_last():
+            j = STEPS - 1
+            cols = slice(j * STEP, (j + 1) * STEP)
+            words, scales = band_codes(j)
+            accs = [psum.tile([P, PACK * STEP], F32, name="acc_last%d" % m, tag="bank%d" % (2 * m)) for m in range(N // P)]
+            for b in range(2):
+                band_cols = slice(b * STEP, (b + 1) * STEP)
+                nc.vector.quantize_mx(out=words[:, band_cols].bitcast(FP8X4), scales=scales[:, band_cols], in_=bands[j][:, b, :])
+                for m in range(N // P):
+                    second_product(accs[m][:, 0:STEP], m, b, words, scales)
+            res_scalar = keep.tile([P, STEP], F32, name="res_last0")
+            nc.scalar.activation(res_scalar[:], accs[0][:, 0:STEP], ACT.Copy)
+            nc.scalar.dma_start(out_rows[:, 0, cols], res_scalar[:])
+            res_vector = keep.tile([P, STEP], F32, name="res_last1")
+            nc.vector.tensor_copy(res_vector[:], accs[1][:, 0:STEP])
+            nc.sync.dma_start(out_rows[:, 1, cols], res_vector[:])
+
+        for j in range(STEPS):
             haar(j, 0)
             if j > 0:
                 finish(j - 1)
             haar(j, 1)
-        finish(steps - 1)
+        finish_last()

@@ -26,10 +26,9 @@ HALF = V // 2
 STEP = 128
 STEPS = V // STEP
 
-X_LOADS = ((1024, 1024), (1024, 512, 512))
-X_STRETCH = 512
-X_ON_SCALAR = ((11, 7), (9, 8, 6))
-W_ON_SCALAR = (16, 8)
+X_LOADS = (((1024, 16), (1024, 5)), ((1024, 16), (1024, 5)), ((1024, 16), (1024, 5)), ((1024, 16), (512, 0), (512, 5)))
+W_ON_SCALAR = (10, 7)
+EARLY = 2
 
 
 def tile_picked_haar_relu_e_kernel(
@@ -42,88 +41,83 @@ def tile_picked_haar_relu_e_kernel(
 
         offsets = keep.tile([P, S // LIST_ROWS], U16, name="offsets")
 
-        x_scales = keep.tile([P, T], U8, name="x_scales", align_bytes=64)
-        nc.vector.memset(x_scales[:].bitcast(I32), 0)
         w23_scales = keep.tile([P, 2, N], U8, name="w23_scales", align_bytes=64)
         nc.vector.memset(w23_scales[:].rearrange("p a n -> p (a n)").bitcast(I32), 0)
         w23_words = keep.tile([P, 2, 2 * N], U8, name="w23_words", align_bytes=64)
 
-        x_words = [keep.tile([P, T], U32, name="x_words%d" % z, align_bytes=64) for z in range(PASSES)]
+        x_words = [keep.tile([P, S], U32, name="x_words%d" % z, align_bytes=64) for z in range(PASSES)]
+        x_scales = [keep.tile([P, S], U8, name="x_scales%d" % z, align_bytes=64) for z in range(PASSES)]
         w_words = [keep.tile([P, H], U32, name="w_words%d" % z, align_bytes=64) for z in range(PASSES)]
         w_scales = [keep.tile([P, H], U8, name="w_scales%d" % z, align_bytes=64) for z in range(PASSES)]
+        woven0 = keep.tile([P, S * 2], U32, name="woven0", align_bytes=64)
+        picked1 = keep.tile([P, 2, S], U32, name="picked1", align_bytes=64)
 
-        def entries(d, c):
-            first = d * V + c * HALF
-            return offsets[:, first // LIST_ROWS : (first + HALF) // LIST_ROWS]
-
-        def gather_words(z):
-            picked = keep.tile([P, S], U32, name="picked_words%d" % z, align_bytes=64)
-            if z < PASSES - 1:
-                nc.vector.tensor_copy(picked[:], x_words[z][:].indirect(offsets[:]))
-                return picked
-            for c in range(2):
-                for d in range(2):
-                    first = d * V + c * HALF
-                    nc.vector.tensor_copy(picked[:, first : first + HALF], x_words[z][:].indirect(entries(d, c)))
-            return picked
-
-        def gather_scales(c, tag):
-            picked = keep.tile([P, 2 * HALF], U8, name="picked_scales%d" % c, tag=tag, align_bytes=64)
-            for d in range(2):
-                nc.vector.tensor_copy(picked[:, d * HALF : (d + 1) * HALF], x_scales[:].indirect(entries(d, c)))
-            return picked
-
-        def quantise_x(z, raw, first, col, sixteenths):
-            grouped = keep.tile([P, X_STRETCH, PACK], BF16, name="x_bf%d_%d" % (z, col), align_bytes=64)
-
-            def views(a, b):
-                return (
-                    grouped[:, a:b, :].rearrange("p (c i) t -> p c t i", i=4),
-                    raw[:, :, first + a : first + b].rearrange("p t (c i) -> p c t i", i=4),
-                )
-
-            cut = X_STRETCH * sixteenths // 16
-            nc.scalar.activation(*views(0, cut), ACT.Copy)
-            nc.vector.tensor_copy(*views(cut, X_STRETCH))
-            nc.vector.quantize_mx(
-                out=x_words[z][:, col : col + X_STRETCH].bitcast(FP8X4),
-                scales=x_scales[SCALE_ROWS * z : P, col : col + X_STRETCH],
-                in_=grouped[:].rearrange("p w t -> p (w t)"),
-            )
-
-        picked_words = []
-        for z in range(PASSES):
+        def load_pair(z, u):
             rows = xT[z * K_PASS : (z + 1) * K_PASS, :].rearrange("(p t) w -> p t w", t=PACK)
+            pairs = keep.tile([P, T * 2], BF16, name="pairs%d%d" % (z, u), align_bytes=64)
             col = 0
-            for n, width in enumerate(X_LOADS[z]):
-                raw = keep.tile([P, PACK, width], F32, name="x_raw%d_%d" % (z, col))
-                nc.sync.dma_start(raw[:], rows[:, :, col : col + width])
-                if z == 0 and n == 0:
+            for width, sixteenths in X_LOADS[2 * z + u]:
+                raw = keep.tile([P, 2, width], F32, name="x_raw%d%d_%d" % (z, u, col))
+                nc.sync.dma_start(raw[:], rows[:, 2 * u : 2 * u + 2, col : col + width])
+                if z == 0 and u == 0 and col == 0:
                     nc.sync.dma_start(offsets[:], offs)
-                for first in range(0, width, X_STRETCH):
-                    quantise_x(z, raw, first, col + first, X_ON_SCALAR[z][n])
-                col = col + width
-            if z == PASSES - 1:
-                picked_scales = [gather_scales(0, "picked_scales0")]
-            picked_words.append(gather_words(z))
 
-        def warm_up(n, lhsT, lhsT_scale):
-            idle = psum.tile([P, PACK * STEP], F32, name="idle%d" % n, tag="bank%d" % (STEPS + n % STEPS))
-            nc.tensor.matmul_mx(
-                out=idle[:],
-                lhsT=lhsT.bitcast(FP8X4),
-                lhsT_scale=lhsT_scale,
-                rhs=picked_words[0][:, 0 : 2 * HALF].bitcast(FP8X4),
-                rhs_scale=picked_scales[0][:],
-                start=True,
-                stop=True,
+                def views(a, b):
+                    return (
+                        pairs[:, 2 * (col + a) : 2 * (col + b)].rearrange("p (c i e) -> p c e i", i=4, e=2),
+                        raw[:, :, a:b].rearrange("p e (c i) -> p c e i", i=4),
+                    )
+
+                cut = width * sixteenths // 16
+                if cut > 0:
+                    nc.scalar.activation(*views(0, cut), ACT.Copy)
+                if cut < width:
+                    nc.vector.tensor_copy(*views(cut, width))
+                col = col + width
+            return pairs
+
+        def gather(dst, pairs, first, count):
+            nc.vector.tensor_copy(
+                dst, pairs[:].bitcast(U32).indirect(offsets[:, first // LIST_ROWS : (first + count) // LIST_ROWS])
             )
 
-        for n, first in enumerate((V, HALF, V + HALF)):
-            warm_up(n, picked_words[1][:, first : first + P], picked_scales[0][SCALE_ROWS:P, 0:P])
+        def quantise_x(z, first, count, woven):
+            nc.vector.quantize_mx(
+                out=x_words[z][:, first : first + count].bitcast(FP8X4),
+                scales=x_scales[z][:, first : first + count],
+                in_=woven.bitcast(BF16),
+            )
+
+        woven0_view = woven0[:].rearrange("p (s u) -> p s u", u=2)
+        gather(woven0_view[:, :, 0], load_pair(0, 0), 0, S)
+        pairs = load_pair(0, 1)
+        for d in range(2):
+            gather(woven0_view[:, d * V : (d + 1) * V, 1], pairs, d * V, V)
+        for d in range(2):
+            quantise_x(0, d * V, V, woven0[:, 2 * d * V : 2 * (d + 1) * V])
+        gather(picked1[:, 0, :], load_pair(1, 0), 0, S)
+        pairs = load_pair(1, 1)
+        for c in range(2):
+            for d in (1, 0):
+                first = d * V + c * HALF
+                gather(picked1[:, 1, first : first + HALF], pairs, first, HALF)
+
+        def weave(c, tag):
+            woven = keep.tile([P, 2, 2 * HALF], U32, name="woven1_%d" % c, tag=tag, align_bytes=64)
+            for d in (1, 0):
+                first = d * V + c * HALF
+                nc.scalar.copy(
+                    woven[:, d, :].rearrange("p (c i u) -> p c u i", i=4, u=2),
+                    picked1[:, :, first : first + HALF].rearrange("p u (c i) -> p c u i", i=4),
+                )
+            return woven
+
+        def quantise_late(c, woven):
+            for d in (1, 0):
+                quantise_x(1, d * V + c * HALF, HALF, woven[:, d, :])
 
         def cast_w(z):
-            raw = keep.tile([P, PACK, H], F32, name="w_raw%d" % z)
+            raw = keep.tile([P, PACK, H], F32, name="w_raw%d" % z, tag="w_raw%d" % z, align_bytes=64)
             nc.sync.dma_start(raw[:], w1[z * K_PASS : (z + 1) * K_PASS, :].rearrange("(p j) c -> p j c", j=PACK))
             dealt = keep.tile([P, PACK, P, PACK], BF16, name="w_bf%d" % z, tag="w_bf%d" % z, align_bytes=64)
 
@@ -135,8 +129,7 @@ def tile_picked_haar_relu_e_kernel(
 
             cut = P * W_ON_SCALAR[z] // 16
             nc.scalar.activation(*views(0, cut), ACT.Copy, scale=0.5)
-            if cut < P:
-                nc.vector.tensor_scalar(*views(cut, P), 0.5, None, ALU.mult)
+            nc.vector.tensor_scalar(*views(cut, P), 0.5, None, ALU.mult)
             return dealt
 
         def quantise_w(z, dealt):
@@ -148,44 +141,60 @@ def tile_picked_haar_relu_e_kernel(
                     in_=dealt[:, t : t + 2, :, :].rearrange("p t m j -> p (t m j)"),
                 )
 
-        w_dealt = [cast_w(z) for z in range(PASSES)]
-        quantise_w(0, w_dealt[0])
-        for n in range(2):
-            cols = slice(2 * n * P, (2 * n + 1) * P)
-            warm_up(3 + n, w_words[0][:, cols], w_scales[0][:, cols])
-
-        banks = [
-            [psum.tile([P, PACK, STEP], F32, name="h%d%d" % (j, d), tag="bank%d" % (2 * j + d)) for d in range(2)]
-            for j in range(STEPS)
-        ]
-
-        def first_product(z, j, d, t):
-            c, within = divmod(j * STEP, HALF)
-            word_col = d * V + j * STEP
-            scale_col = d * HALF + within
+        def first_product(z, j, d, t, opens):
+            cols = slice(d * V + j * STEP, d * V + (j + 1) * STEP)
             nc.tensor.matmul_mx(
                 out=banks[j][d][:, t, :],
                 lhsT=w_words[z][:, t * P : (t + 1) * P].bitcast(FP8X4),
                 lhsT_scale=w_scales[z][:, t * P : (t + 1) * P],
-                rhs=picked_words[z][:, word_col : word_col + STEP].bitcast(FP8X4),
-                rhs_scale=picked_scales[c][SCALE_ROWS * z : P, scale_col : scale_col + STEP],
-                start=(z == 0),
-                stop=(z == PASSES - 1),
+                rhs=x_words[z][:, cols].bitcast(FP8X4),
+                rhs_scale=x_scales[z][:, cols],
+                start=(opens and t == 0),
+                stop=(not opens and t == PACK - 1),
             )
 
-        quantise_w(1, w_dealt[1])
-        picked_scales.append(gather_scales(1, "w_bf1"))
-
         relu1 = []
-        for j in range(STEPS):
+
+        def rectify(j):
             rectified = keep.tile([P, STEP, PACK], F32, name="relu1_%d" % j)
+            nc.scalar.activation(rectified[:], banks[j][1][:].rearrange("p t v -> p v t"), ACT.Relu)
+            relu1.append(rectified)
+
+        quantise_late(0, weave(0, "woven1_0"))
+        for n, first in enumerate((V, 0, 0)):
+            idle = psum.tile([P, PACK * STEP], F32, name="idle%d" % n, tag="bank%d" % (STEPS + n))
+            nc.tensor.matmul_mx(
+                out=idle[:],
+                lhsT=x_words[1][:, first : first + P].bitcast(FP8X4),
+                lhsT_scale=x_scales[1][:, first : first + P],
+                rhs=x_words[0][:, 0:V].bitcast(FP8X4),
+                rhs_scale=x_scales[0][:, 0:V],
+                start=True,
+                stop=True,
+            )
+        banks = [
+            [psum.tile([P, PACK, STEP], F32, name="h%d%d" % (j, d), tag="bank%d" % (2 * j + d)) for d in range(2)]
+            for j in range(STEPS)
+        ]
+        quantise_w(0, cast_w(0))
+        for j in range(EARLY):
             for d in (1, 0):
                 for t in range(PACK):
-                    for z in range(PASSES):
-                        first_product(z, j, d, t)
+                    first_product(0, j, d, t, True)
+        quantise_w(1, cast_w(1))
+        quantise_late(1, weave(1, "w_raw1"))
+        for d in (1, 0):
+            for t in range(2):
+                first_product(1, 0, d, t, False)
+        for j in range(STEPS):
+            for d in (1, 0):
+                for t in range(2 if j == 0 else 0, PACK):
+                    first_product(1, j, d, t, j >= EARLY)
+                if j >= EARLY:
+                    for t in range(PACK):
+                        first_product(0, j, d, t, False)
                 if d == 1:
-                    nc.scalar.activation(rectified[:], banks[j][d][:].rearrange("p t v -> p v t"), ACT.Relu)
-            relu1.append(rectified)
+                    rectify(j)
 
         for b, (words, scales) in enumerate(((w2_words, w2_scales), (w3_words, w3_scales))):
             nc.sync.dma_start(w23_words[:, b, :].bitcast(I32), words[0].bitcast(I32))

@@ -26,7 +26,7 @@ HALF = V // 2
 STEP = 128
 STEPS = V // STEP
 
-X_LOADS = (((1024, 16), (1024, 5)), ((1024, 16), (1024, 5)), ((1024, 16), (1024, 5)), ((1024, 16), (512, 0), (512, 5)))
+X_LOADS = (((1024, 16), (1024, 5)), ((1024, 16), (1024, 5)), ((1024, 16), (1024, 10)), ((1024, 16), (512, 0), (512, 5)))
 W_ON_SCALAR = (10, 7)
 EARLY = 2
 
@@ -45,19 +45,18 @@ def tile_picked_haar_relu_e_kernel(
         nc.vector.memset(w23_scales[:].rearrange("p a n -> p (a n)").bitcast(I32), 0)
         w23_words = keep.tile([P, 2, 2 * N], U8, name="w23_words", align_bytes=64)
 
-        x_words = [keep.tile([P, S], U32, name="x_words%d" % z, align_bytes=64) for z in range(PASSES)]
-        x_scales = [keep.tile([P, S], U8, name="x_scales%d" % z, align_bytes=64) for z in range(PASSES)]
+        x_words = {}
+        x_scales = {}
         w_words = [keep.tile([P, H], U32, name="w_words%d" % z, align_bytes=64) for z in range(PASSES)]
         w_scales = [keep.tile([P, H], U8, name="w_scales%d" % z, align_bytes=64) for z in range(PASSES)]
-        woven0 = keep.tile([P, S * 2], U32, name="woven0", align_bytes=64)
-        picked1 = keep.tile([P, 2, S], U32, name="picked1", align_bytes=64)
+        picked = [keep.tile([P, 2, S], U32, name="picked%d" % z, align_bytes=64) for z in range(PASSES)]
 
         def load_pair(z, u):
             rows = xT[z * K_PASS : (z + 1) * K_PASS, :].rearrange("(p t) w -> p t w", t=PACK)
             pairs = keep.tile([P, T * 2], BF16, name="pairs%d%d" % (z, u), align_bytes=64)
             col = 0
             for width, sixteenths in X_LOADS[2 * z + u]:
-                raw = keep.tile([P, 2, width], F32, name="x_raw%d%d_%d" % (z, u, col))
+                raw = keep.tile([P, 2, width], F32, name="x_raw%d%d_%d" % (z, u, col), tag="x_raw%d%d_%d" % (z, u, col), align_bytes=64)
                 nc.sync.dma_start(raw[:], rows[:, 2 * u : 2 * u + 2, col : col + width])
                 if z == 0 and u == 0 and col == 0:
                     nc.sync.dma_start(offsets[:], offs)
@@ -81,40 +80,46 @@ def tile_picked_haar_relu_e_kernel(
                 dst, pairs[:].bitcast(U32).indirect(offsets[:, first // LIST_ROWS : (first + count) // LIST_ROWS])
             )
 
-        def quantise_x(z, first, count, woven):
-            nc.vector.quantize_mx(
-                out=x_words[z][:, first : first + count].bitcast(FP8X4),
-                scales=x_scales[z][:, first : first + count],
-                in_=woven.bitcast(BF16),
-            )
+        def weave(z, c, tag):
+            woven = keep.tile([P, 2 * 2 * HALF], U32, name="woven%d%d" % (z, c), tag=tag, align_bytes=64)
+            for d in (1, 0):
+                first = d * V + c * HALF
+                dst = woven[:, 2 * d * HALF : 2 * (d + 1) * HALF]
+                src = picked[z][:, :, first : first + HALF]
+                if z == 0 and c == 0:
+                    nc.vector.tensor_copy(
+                        dst.bitcast(I32).rearrange("p (c i u) -> p c u i", i=4, u=2),
+                        src.bitcast(I32).rearrange("p u (c i) -> p c u i", i=4),
+                    )
+                else:
+                    nc.scalar.copy(
+                        dst.rearrange("p (c i u) -> p c u i", i=4, u=2), src.rearrange("p u (c i) -> p c u i", i=4)
+                    )
+            return woven
 
-        woven0_view = woven0[:].rearrange("p (s u) -> p s u", u=2)
-        gather(woven0_view[:, :, 0], load_pair(0, 0), 0, S)
+        def quantise_x(z, c, woven, tag, calls):
+            x_words[z, c] = keep.tile([P, 2 * HALF], U32, name="x_words%d%d" % (z, c), tag=tag, align_bytes=64)
+            x_scales[z, c] = keep.tile([P, 2 * HALF], U8, name="x_scales%d%d" % (z, c), align_bytes=64)
+            width = 2 * HALF // calls
+            for first in reversed(range(0, 2 * HALF, width)):
+                nc.vector.quantize_mx(
+                    out=x_words[z, c][:, first : first + width].bitcast(FP8X4),
+                    scales=x_scales[z, c][:, first : first + width],
+                    in_=woven[:, 2 * first : 2 * (first + width)].bitcast(BF16),
+                )
+
+        gather(picked[0][:, 0, :], load_pair(0, 0), 0, S)
         pairs = load_pair(0, 1)
-        for d in range(2):
-            gather(woven0_view[:, d * V : (d + 1) * V, 1], pairs, d * V, V)
-        for d in range(2):
-            quantise_x(0, d * V, V, woven0[:, 2 * d * V : 2 * (d + 1) * V])
-        gather(picked1[:, 0, :], load_pair(1, 0), 0, S)
+        for d in (1, 0):
+            gather(picked[0][:, 1, d * V : (d + 1) * V], pairs, d * V, V)
+        quantise_x(0, 0, weave(0, 0, "woven00"), "x_words00", 1)
+        gather(picked[1][:, 0, :], load_pair(1, 0), 0, S)
         pairs = load_pair(1, 1)
+        woven01 = weave(0, 1, "x_raw11_1536")
         for c in range(2):
             for d in (1, 0):
                 first = d * V + c * HALF
-                gather(picked1[:, 1, first : first + HALF], pairs, first, HALF)
-
-        def weave(c, tag):
-            woven = keep.tile([P, 2, 2 * HALF], U32, name="woven1_%d" % c, tag=tag, align_bytes=64)
-            for d in (1, 0):
-                first = d * V + c * HALF
-                nc.scalar.copy(
-                    woven[:, d, :].rearrange("p (c i u) -> p c u i", i=4, u=2),
-                    picked1[:, :, first : first + HALF].rearrange("p u (c i) -> p c u i", i=4),
-                )
-            return woven
-
-        def quantise_late(c, woven):
-            for d in (1, 0):
-                quantise_x(1, d * V + c * HALF, HALF, woven[:, d, :])
+                gather(picked[1][:, 1, first : first + HALF], pairs, first, HALF)
 
         def cast_w(z):
             raw = keep.tile([P, PACK, H], F32, name="w_raw%d" % z, tag="w_raw%d" % z, align_bytes=64)
@@ -142,13 +147,14 @@ def tile_picked_haar_relu_e_kernel(
                 )
 
         def first_product(z, j, d, t, opens):
-            cols = slice(d * V + j * STEP, d * V + (j + 1) * STEP)
+            c, within = divmod(j * STEP, HALF)
+            cols = slice(d * HALF + within, d * HALF + within + STEP)
             nc.tensor.matmul_mx(
                 out=banks[j][d][:, t, :],
                 lhsT=w_words[z][:, t * P : (t + 1) * P].bitcast(FP8X4),
                 lhsT_scale=w_scales[z][:, t * P : (t + 1) * P],
-                rhs=x_words[z][:, cols].bitcast(FP8X4),
-                rhs_scale=x_scales[z][:, cols],
+                rhs=x_words[z, c][:, cols].bitcast(FP8X4),
+                rhs_scale=x_scales[z, c][:, cols],
                 start=(opens and t == 0),
                 stop=(not opens and t == PACK - 1),
             )
@@ -160,15 +166,15 @@ def tile_picked_haar_relu_e_kernel(
             nc.scalar.activation(rectified[:], banks[j][1][:].rearrange("p t v -> p v t"), ACT.Relu)
             relu1.append(rectified)
 
-        quantise_late(0, weave(0, "woven1_0"))
-        for n, first in enumerate((V, 0, 0)):
+        quantise_x(1, 0, weave(1, 0, "woven10"), "x_words10", 2)
+        for n, first in enumerate((HALF, 0, 0)):
             idle = psum.tile([P, PACK * STEP], F32, name="idle%d" % n, tag="bank%d" % (STEPS + n))
             nc.tensor.matmul_mx(
                 out=idle[:],
-                lhsT=x_words[1][:, first : first + P].bitcast(FP8X4),
-                lhsT_scale=x_scales[1][:, first : first + P],
-                rhs=x_words[0][:, 0:V].bitcast(FP8X4),
-                rhs_scale=x_scales[0][:, 0:V],
+                lhsT=x_words[1, 0][:, first : first + P].bitcast(FP8X4),
+                lhsT_scale=x_scales[1, 0][:, first : first + P],
+                rhs=x_words[0, 0][:].bitcast(FP8X4),
+                rhs_scale=x_scales[0, 0][:],
                 start=True,
                 stop=True,
             )
@@ -182,17 +188,18 @@ def tile_picked_haar_relu_e_kernel(
                 for t in range(PACK):
                     first_product(0, j, d, t, True)
         quantise_w(1, cast_w(1))
-        quantise_late(1, weave(1, "w_raw1"))
+        quantise_x(0, 1, woven01, "w_bf1", 1)
+        quantise_x(1, 1, weave(1, 1, "w_raw1"), "x_words11", 2)
         for d in (1, 0):
             for t in range(2):
                 first_product(1, 0, d, t, False)
         for j in range(STEPS):
             for d in (1, 0):
-                for t in range(2 if j == 0 else 0, PACK):
-                    first_product(1, j, d, t, j >= EARLY)
                 if j >= EARLY:
                     for t in range(PACK):
-                        first_product(0, j, d, t, False)
+                        first_product(0, j, d, t, True)
+                for t in range(2 if j == 0 else 0, PACK):
+                    first_product(1, j, d, t, False)
                 if d == 1:
                     rectify(j)
 

@@ -26,9 +26,8 @@ HALF = V // 2
 STEP = 128
 STEPS = V // STEP
 
-X_LOADS = (((1024, 16), (1024, 5)), ((1024, 16), (1024, 5)), ((1024, 16), (1024, 10)), ((1024, 16), (512, 0), (512, 5)))
-W_ON_SCALAR = (10, 7)
-EARLY = 2
+X_LOADS = (((1024, 16), (1024, 5)), ((1536, 6), (512, 5)), ((1152, 16), (896, 3)), ((1024, 16), (512, 0), (512, 5)))
+W_ON_SCALAR = (87, 53)
 
 
 def tile_picked_haar_relu_e_kernel(
@@ -80,81 +79,113 @@ def tile_picked_haar_relu_e_kernel(
                 dst, pairs[:].bitcast(U32).indirect(offsets[:, first // LIST_ROWS : (first + count) // LIST_ROWS])
             )
 
-        def weave(z, c, tag):
-            woven = keep.tile([P, 2 * 2 * HALF], U32, name="woven%d%d" % (z, c), tag=tag, align_bytes=64)
-            for d in (1, 0):
-                first = d * V + c * HALF
-                dst = woven[:, 2 * d * HALF : 2 * (d + 1) * HALF]
-                src = picked[z][:, :, first : first + HALF]
-                if z == 0 and c == 0:
-                    nc.vector.tensor_copy(
-                        dst.bitcast(I32).rearrange("p (c i u) -> p c u i", i=4, u=2),
-                        src.bitcast(I32).rearrange("p u (c i) -> p c u i", i=4),
-                    )
-                else:
-                    nc.scalar.copy(
-                        dst.rearrange("p (c i u) -> p c u i", i=4, u=2), src.rearrange("p u (c i) -> p c u i", i=4)
-                    )
-            return woven
+        def weave(z, c, d, dst, on_scalar):
+            first = d * V + c * HALF
+            src = picked[z][:, :, first : first + HALF]
+            if on_scalar:
+                nc.scalar.copy(dst.rearrange("p (c i u) -> p c u i", i=4, u=2), src.rearrange("p u (c i) -> p c u i", i=4))
+            else:
+                nc.vector.tensor_copy(
+                    dst.bitcast(I32).rearrange("p (c i u) -> p c u i", i=4, u=2),
+                    src.bitcast(I32).rearrange("p u (c i) -> p c u i", i=4),
+                )
 
-        def quantise_x(z, c, woven, tag, calls):
+        def woven_tile(name, pieces, tag):
+            return keep.tile([P, pieces * 2 * HALF], U32, name=name, tag=tag, align_bytes=64)
+
+        def codes(z, c, tag):
             x_words[z, c] = keep.tile([P, 2 * HALF], U32, name="x_words%d%d" % (z, c), tag=tag, align_bytes=64)
             x_scales[z, c] = keep.tile([P, 2 * HALF], U8, name="x_scales%d%d" % (z, c), align_bytes=64)
-            width = 2 * HALF // calls
-            for first in reversed(range(0, 2 * HALF, width)):
-                nc.vector.quantize_mx(
-                    out=x_words[z, c][:, first : first + width].bitcast(FP8X4),
-                    scales=x_scales[z, c][:, first : first + width],
-                    in_=woven[:, 2 * first : 2 * (first + width)].bitcast(BF16),
-                )
+
+        def quantise_x(z, c, first, woven):
+            width = woven.shape[1] // 2
+            nc.vector.quantize_mx(
+                out=x_words[z, c][:, first : first + width].bitcast(FP8X4),
+                scales=x_scales[z, c][:, first : first + width],
+                in_=woven.bitcast(BF16),
+            )
+
+        def quantise_piece(d, woven, tag):
+            words = keep.tile([P, HALF], U32, name="x_words01%d" % d, tag=tag, align_bytes=64)
+            scales = keep.tile([P, HALF], U8, name="x_scales01%d" % d, align_bytes=64)
+            nc.vector.quantize_mx(out=words[:].bitcast(FP8X4), scales=scales[:], in_=woven.bitcast(BF16))
+            pieces01[d] = (words, scales)
+
+        pieces01 = {}
+
+        def late_half(c, tag):
+            woven = woven_tile("woven1%d" % c, 2, tag)
+            codes(1, c, "x_words1%d" % c)
+            for d in (1, 0):
+                weave(1, c, d, woven[:, 2 * d * HALF : 2 * (d + 1) * HALF], True)
+            for d in (1, 0):
+                quantise_x(1, c, d * HALF, woven[:, 2 * d * HALF : 2 * (d + 1) * HALF])
 
         gather(picked[0][:, 0, :], load_pair(0, 0), 0, S)
         pairs = load_pair(0, 1)
         for d in (1, 0):
             gather(picked[0][:, 1, d * V : (d + 1) * V], pairs, d * V, V)
-        quantise_x(0, 0, weave(0, 0, "woven00"), "x_words00", 1)
-        gather(picked[1][:, 0, :], load_pair(1, 0), 0, S)
+        woven011 = woven_tile("woven011", 1, "woven011")
+        weave(0, 1, 1, woven011[:], False)
+        woven00 = woven_tile("woven00", 2, "woven00")
+        for d in (1, 0):
+            weave(0, 0, d, woven00[:, 2 * d * HALF : 2 * (d + 1) * HALF], False)
+        quantise_piece(1, woven011[:], "x_words011")
+        pairs = load_pair(1, 0)
+        codes(0, 0, "x_raw10_0")
+        quantise_x(0, 0, 0, woven00[:])
+        gather(picked[1][:, 0, :], pairs, 0, S)
         pairs = load_pair(1, 1)
-        woven01 = weave(0, 1, "x_raw11_1536")
+        woven010 = woven_tile("woven010", 1, "x_raw11_1536")
+        weave(0, 1, 0, woven010[:], True)
         for c in range(2):
             for d in (1, 0):
                 first = d * V + c * HALF
                 gather(picked[1][:, 1, first : first + HALF], pairs, first, HALF)
 
+        w_raw = keep.tile([P, PASSES, PACK, H], F32, name="w_raw", tag="w_raw", align_bytes=64)
+        dealt = keep.tile([P, PASSES, PACK, P, PACK], BF16, name="w_bf", tag="w_bf", align_bytes=64)
+
         def cast_w(z):
-            raw = keep.tile([P, PACK, H], F32, name="w_raw%d" % z, tag="w_raw%d" % z, align_bytes=64)
-            nc.sync.dma_start(raw[:], w1[z * K_PASS : (z + 1) * K_PASS, :].rearrange("(p j) c -> p j c", j=PACK))
-            dealt = keep.tile([P, PACK, P, PACK], BF16, name="w_bf%d" % z, tag="w_bf%d" % z, align_bytes=64)
+            nc.sync.dma_start(w_raw[:, z], w1[z * K_PASS : (z + 1) * K_PASS, :].rearrange("(p j) c -> p j c", j=PACK))
 
             def views(a, b):
                 return (
-                    dealt[:, :, a:b, :].rearrange("p t m j -> p m j t"),
-                    raw[:, :, PACK * a : PACK * b].rearrange("p j (m t) -> p m j t", t=PACK),
+                    dealt[:, z, :, a:b, :].rearrange("p t m j -> p m j t"),
+                    w_raw[:, z, :, PACK * a : PACK * b].rearrange("p j (m t) -> p m j t", t=PACK),
                 )
 
-            cut = P * W_ON_SCALAR[z] // 16
+            cut = W_ON_SCALAR[z]
             nc.scalar.activation(*views(0, cut), ACT.Copy, scale=0.5)
-            nc.vector.tensor_scalar(*views(cut, P), 0.5, None, ALU.mult)
-            return dealt
+            if z == PASSES - 1:
+                nc.vector.tensor_scalar(
+                    dealt[:, :, :, P - 1, :].rearrange("p z t j -> p z j t"), w_raw[:, :, :, H - PACK : H], 0.5, None, ALU.mult
+                )
+            nc.vector.tensor_scalar(*views(cut, P - 1), 0.5, None, ALU.mult)
 
-        def quantise_w(z, dealt):
+        def quantise_w(z):
             for t in range(0, PACK, 2):
                 cols = slice(t * P, (t + 2) * P)
                 nc.vector.quantize_mx(
                     out=w_words[z][:, cols].bitcast(FP8X4),
                     scales=w_scales[z][:, cols],
-                    in_=dealt[:, t : t + 2, :, :].rearrange("p t m j -> p (t m j)"),
+                    in_=dealt[:, z, t : t + 2, :, :].rearrange("p t m j -> p (t m j)"),
                 )
 
         def first_product(z, j, d, t, opens):
             c, within = divmod(j * STEP, HALF)
-            cols = slice(d * HALF + within, d * HALF + within + STEP)
+            if (z, c) == (0, 1):
+                words, scales = pieces01[d]
+                cols = slice(within, within + STEP)
+            else:
+                words, scales = x_words[z, c], x_scales[z, c]
+                cols = slice(d * HALF + within, d * HALF + within + STEP)
             nc.tensor.matmul_mx(
                 out=banks[j][d][:, t, :],
                 lhsT=w_words[z][:, t * P : (t + 1) * P].bitcast(FP8X4),
                 lhsT_scale=w_scales[z][:, t * P : (t + 1) * P],
-                rhs=x_words[z, c][:, cols].bitcast(FP8X4),
-                rhs_scale=x_scales[z, c][:, cols],
+                rhs=words[:, cols].bitcast(FP8X4),
+                rhs_scale=scales[:, cols],
                 start=(opens and t == 0),
                 stop=(not opens and t == PACK - 1),
             )
@@ -166,7 +197,7 @@ def tile_picked_haar_relu_e_kernel(
             nc.scalar.activation(rectified[:], banks[j][1][:].rearrange("p t v -> p v t"), ACT.Relu)
             relu1.append(rectified)
 
-        quantise_x(1, 0, weave(1, 0, "woven10"), "x_words10", 2)
+        late_half(0, "woven10")
         for n, first in enumerate((HALF, 0, 0)):
             idle = psum.tile([P, PACK * STEP], F32, name="idle%d" % n, tag="bank%d" % (STEPS + n))
             nc.tensor.matmul_mx(
@@ -182,24 +213,22 @@ def tile_picked_haar_relu_e_kernel(
             [psum.tile([P, PACK, STEP], F32, name="h%d%d" % (j, d), tag="bank%d" % (2 * j + d)) for d in range(2)]
             for j in range(STEPS)
         ]
-        quantise_w(0, cast_w(0))
-        for j in range(EARLY):
-            for d in (1, 0):
-                for t in range(PACK):
-                    first_product(0, j, d, t, True)
-        quantise_w(1, cast_w(1))
-        quantise_x(0, 1, woven01, "w_bf1", 1)
-        quantise_x(1, 1, weave(1, 1, "w_raw1"), "x_words11", 2)
+        for z in range(PASSES):
+            cast_w(z)
+        quantise_w(0)
+        quantise_w(1)
+        woven11 = woven_tile("woven11", 2, "w_raw")
+        codes(1, 1, "x_words11")
         for d in (1, 0):
-            for t in range(2):
-                first_product(1, 0, d, t, False)
+            weave(1, 1, d, woven11[:, 2 * d * HALF : 2 * (d + 1) * HALF], True)
+        quantise_x(1, 1, HALF, woven11[:, 2 * HALF : 4 * HALF])
+        quantise_piece(0, woven010[:], "w_bf")
+        quantise_x(1, 1, 0, woven11[:, 0 : 2 * HALF])
         for j in range(STEPS):
             for d in (1, 0):
-                if j >= EARLY:
+                for z in range(PASSES):
                     for t in range(PACK):
-                        first_product(0, j, d, t, True)
-                for t in range(2 if j == 0 else 0, PACK):
-                    first_product(1, j, d, t, False)
+                        first_product(z, j, d, t, z == 0)
                 if d == 1:
                     rectify(j)
 

@@ -22,11 +22,18 @@ K_PASS = P * PACK
 PASSES = K // K_PASS
 LIST_ROWS = 16
 SCALE_ROWS = 4
+LINE = 4
 HALF = V // 2
 STEP = 128
 STEPS = V // STEP
+WARM_UPS = 3
 
-X_LOADS = (((1024, 16), (1024, 5)), ((1536, 6), (512, 5)), ((1152, 16), (896, 3)), ((1024, 16), (512, 0), (512, 5)))
+X_LOADS = (
+    ((1024, 16), (1024, 5)),
+    ((1536, 6), (512, 5)),
+    ((1152, 16), (896, 3)),
+    ((1024, 16), (512, 0), (512, 5)),
+)
 W_ON_SCALAR = (87, 53)
 
 
@@ -44,26 +51,28 @@ def tile_picked_haar_relu_e_kernel(
         nc.vector.memset(w23_scales[:].rearrange("p a n -> p (a n)").bitcast(I32), 0)
         w23_words = keep.tile([P, 2, 2 * N], U8, name="w23_words", align_bytes=64)
 
-        x_words = {}
-        x_scales = {}
         w_words = [keep.tile([P, H], U32, name="w_words%d" % z, align_bytes=64) for z in range(PASSES)]
         w_scales = [keep.tile([P, H], U8, name="w_scales%d" % z, align_bytes=64) for z in range(PASSES)]
         picked = [keep.tile([P, 2, S], U32, name="picked%d" % z, align_bytes=64) for z in range(PASSES)]
+        x_codes = {}
 
-        def load_pair(z, u):
+        def raw_tag(z, u, n):
+            return "x_raw%d%d_%d" % (z, u, n)
+
+        def load_duos(z, u):
             rows = xT[z * K_PASS : (z + 1) * K_PASS, :].rearrange("(p t) w -> p t w", t=PACK)
-            pairs = keep.tile([P, T * 2], BF16, name="pairs%d%d" % (z, u), align_bytes=64)
+            duos = keep.tile([P, T * 2], BF16, name="duos%d%d" % (z, u), align_bytes=64)
             col = 0
-            for width, sixteenths in X_LOADS[2 * z + u]:
-                raw = keep.tile([P, 2, width], F32, name="x_raw%d%d_%d" % (z, u, col), tag="x_raw%d%d_%d" % (z, u, col), align_bytes=64)
+            for n, (width, sixteenths) in enumerate(X_LOADS[2 * z + u]):
+                raw = keep.tile([P, 2, width], F32, name=raw_tag(z, u, n), tag=raw_tag(z, u, n), align_bytes=64)
                 nc.sync.dma_start(raw[:], rows[:, 2 * u : 2 * u + 2, col : col + width])
-                if z == 0 and u == 0 and col == 0:
+                if (z, u, n) == (0, 0, 0):
                     nc.sync.dma_start(offsets[:], offs)
 
                 def views(a, b):
                     return (
-                        pairs[:, 2 * (col + a) : 2 * (col + b)].rearrange("p (c i e) -> p c e i", i=4, e=2),
-                        raw[:, :, a:b].rearrange("p e (c i) -> p c e i", i=4),
+                        duos[:, 2 * (col + a) : 2 * (col + b)].rearrange("p (c i e) -> p c e i", i=LINE, e=2),
+                        raw[:, :, a:b].rearrange("p e (c i) -> p c e i", i=LINE),
                     )
 
                 cut = width * sixteenths // 16
@@ -72,165 +81,136 @@ def tile_picked_haar_relu_e_kernel(
                 if cut < width:
                     nc.vector.tensor_copy(*views(cut, width))
                 col = col + width
-            return pairs
+            return duos[:].bitcast(U32)
 
-        def gather(dst, pairs, first, count):
-            nc.vector.tensor_copy(
-                dst, pairs[:].bitcast(U32).indirect(offsets[:, first // LIST_ROWS : (first + count) // LIST_ROWS])
-            )
+        def gather(z, u, window, first, count):
+            entries = offsets[:, first // LIST_ROWS : (first + count) // LIST_ROWS]
+            nc.vector.tensor_copy(picked[z][:, u, first : first + count], window.indirect(entries))
 
-        def weave(z, c, d, dst, on_scalar):
-            first = d * V + c * HALF
-            src = picked[z][:, :, first : first + HALF]
-            if on_scalar:
-                nc.scalar.copy(dst.rearrange("p (c i u) -> p c u i", i=4, u=2), src.rearrange("p u (c i) -> p c u i", i=4))
-            else:
-                nc.vector.tensor_copy(
-                    dst.bitcast(I32).rearrange("p (c i u) -> p c u i", i=4, u=2),
-                    src.bitcast(I32).rearrange("p u (c i) -> p c u i", i=4),
-                )
+        def weave(z, c, pieces, on_scalar, tag):
+            woven = keep.tile([P, len(pieces) * 2 * HALF], U32, name="woven%d%d%d" % (z, c, pieces[0]), tag=tag, align_bytes=64)
+            for n in reversed(range(len(pieces))):
+                first = pieces[n] * V + c * HALF
+                src = picked[z][:, :, first : first + HALF]
+                dst = woven[:, 2 * n * HALF : 2 * (n + 1) * HALF]
+                if on_scalar:
+                    nc.scalar.copy(
+                        dst.rearrange("p (c i u) -> p c u i", i=LINE, u=2), src.rearrange("p u (c i) -> p c u i", i=LINE)
+                    )
+                else:
+                    nc.vector.tensor_copy(
+                        dst.bitcast(I32).rearrange("p (c i u) -> p c u i", i=LINE, u=2),
+                        src.bitcast(I32).rearrange("p u (c i) -> p c u i", i=LINE),
+                    )
+            return woven
 
-        def woven_tile(name, pieces, tag):
-            return keep.tile([P, pieces * 2 * HALF], U32, name=name, tag=tag, align_bytes=64)
+        def code_tiles(z, c, pieces, tag):
+            name = "%d%d%d" % (z, c, pieces[0])
+            words = keep.tile([P, len(pieces) * HALF], U32, name="x_words" + name, tag=tag, align_bytes=64)
+            scales = keep.tile([P, len(pieces) * HALF], U8, name="x_scales" + name, align_bytes=64)
+            for n, d in enumerate(pieces):
+                x_codes[z, c, d] = (words[:, n * HALF : (n + 1) * HALF], scales[:, n * HALF : (n + 1) * HALF])
+            return words[:], scales[:]
 
-        def codes(z, c, tag):
-            x_words[z, c] = keep.tile([P, 2 * HALF], U32, name="x_words%d%d" % (z, c), tag=tag, align_bytes=64)
-            x_scales[z, c] = keep.tile([P, 2 * HALF], U8, name="x_scales%d%d" % (z, c), align_bytes=64)
+        def quantise(codes, values):
+            nc.vector.quantize_mx(out=codes[0].bitcast(FP8X4), scales=codes[1], in_=values)
 
-        def quantise_x(z, c, first, woven):
-            width = woven.shape[1] // 2
-            nc.vector.quantize_mx(
-                out=x_words[z, c][:, first : first + width].bitcast(FP8X4),
-                scales=x_scales[z, c][:, first : first + width],
-                in_=woven.bitcast(BF16),
-            )
+        def piece_of(woven, d):
+            return woven[:, 2 * d * HALF : 2 * (d + 1) * HALF].bitcast(BF16)
 
-        def quantise_piece(d, woven, tag):
-            words = keep.tile([P, HALF], U32, name="x_words01%d" % d, tag=tag, align_bytes=64)
-            scales = keep.tile([P, HALF], U8, name="x_scales01%d" % d, align_bytes=64)
-            nc.vector.quantize_mx(out=words[:].bitcast(FP8X4), scales=scales[:], in_=woven.bitcast(BF16))
-            pieces01[d] = (words, scales)
-
-        pieces01 = {}
-
-        def late_half(c, tag):
-            woven = woven_tile("woven1%d" % c, 2, tag)
-            codes(1, c, "x_words1%d" % c)
-            for d in (1, 0):
-                weave(1, c, d, woven[:, 2 * d * HALF : 2 * (d + 1) * HALF], True)
-            for d in (1, 0):
-                quantise_x(1, c, d * HALF, woven[:, 2 * d * HALF : 2 * (d + 1) * HALF])
-
-        gather(picked[0][:, 0, :], load_pair(0, 0), 0, S)
-        pairs = load_pair(0, 1)
+        gather(0, 0, load_duos(0, 0), 0, S)
+        window = load_duos(0, 1)
         for d in (1, 0):
-            gather(picked[0][:, 1, d * V : (d + 1) * V], pairs, d * V, V)
-        woven011 = woven_tile("woven011", 1, "woven011")
-        weave(0, 1, 1, woven011[:], False)
-        woven00 = woven_tile("woven00", 2, "woven00")
-        for d in (1, 0):
-            weave(0, 0, d, woven00[:, 2 * d * HALF : 2 * (d + 1) * HALF], False)
-        quantise_piece(1, woven011[:], "x_words011")
-        pairs = load_pair(1, 0)
-        codes(0, 0, "x_raw10_0")
-        quantise_x(0, 0, 0, woven00[:])
-        gather(picked[1][:, 0, :], pairs, 0, S)
-        pairs = load_pair(1, 1)
-        woven010 = woven_tile("woven010", 1, "x_raw11_1536")
-        weave(0, 1, 0, woven010[:], True)
+            gather(0, 1, window, d * V, V)
+        woven011 = weave(0, 1, (1,), False, "woven011")
+        woven00 = weave(0, 0, (0, 1), False, "woven00")
+        quantise(code_tiles(0, 1, (1,), "x_words011"), woven011[:].bitcast(BF16))
+        window = load_duos(1, 0)
+        codes00 = code_tiles(0, 0, (0, 1), raw_tag(1, 0, 0))
+        quantise(codes00, woven00[:].bitcast(BF16))
+        gather(1, 0, window, 0, S)
+        window = load_duos(1, 1)
+        woven010 = weave(0, 1, (0,), True, raw_tag(1, 1, 2))
         for c in range(2):
             for d in (1, 0):
-                first = d * V + c * HALF
-                gather(picked[1][:, 1, first : first + HALF], pairs, first, HALF)
+                gather(1, 1, window, d * V + c * HALF, HALF)
 
         w_raw = keep.tile([P, PASSES, PACK, H], F32, name="w_raw", tag="w_raw", align_bytes=64)
-        dealt = keep.tile([P, PASSES, PACK, P, PACK], BF16, name="w_bf", tag="w_bf", align_bytes=64)
+        w_dealt = keep.tile([P, PASSES, PACK, P, PACK], BF16, name="w_dealt", tag="w_dealt", align_bytes=64)
 
-        def cast_w(z):
-            nc.sync.dma_start(w_raw[:, z], w1[z * K_PASS : (z + 1) * K_PASS, :].rearrange("(p j) c -> p j c", j=PACK))
+        woven10 = weave(1, 0, (0, 1), True, "woven10")
+        code_tiles(1, 0, (0, 1), "x_words10")
+        for d in (1, 0):
+            quantise(x_codes[1, 0, d], piece_of(woven10, d))
 
-            def views(a, b):
-                return (
-                    dealt[:, z, :, a:b, :].rearrange("p t m j -> p m j t"),
-                    w_raw[:, z, :, PACK * a : PACK * b].rearrange("p j (m t) -> p m j t", t=PACK),
-                )
-
-            cut = W_ON_SCALAR[z]
-            nc.scalar.activation(*views(0, cut), ACT.Copy, scale=0.5)
-            if z == PASSES - 1:
-                nc.vector.tensor_scalar(
-                    dealt[:, :, :, P - 1, :].rearrange("p z t j -> p z j t"), w_raw[:, :, :, H - PACK : H], 0.5, None, ALU.mult
-                )
-            nc.vector.tensor_scalar(*views(cut, P - 1), 0.5, None, ALU.mult)
-
-        def quantise_w(z):
-            for t in range(0, PACK, 2):
-                cols = slice(t * P, (t + 2) * P)
-                nc.vector.quantize_mx(
-                    out=w_words[z][:, cols].bitcast(FP8X4),
-                    scales=w_scales[z][:, cols],
-                    in_=dealt[:, z, t : t + 2, :, :].rearrange("p t m j -> p (t m j)"),
-                )
-
-        def first_product(z, j, d, t, opens):
-            c, within = divmod(j * STEP, HALF)
-            if (z, c) == (0, 1):
-                words, scales = pieces01[d]
-                cols = slice(within, within + STEP)
-            else:
-                words, scales = x_words[z, c], x_scales[z, c]
-                cols = slice(d * HALF + within, d * HALF + within + STEP)
-            nc.tensor.matmul_mx(
-                out=banks[j][d][:, t, :],
-                lhsT=w_words[z][:, t * P : (t + 1) * P].bitcast(FP8X4),
-                lhsT_scale=w_scales[z][:, t * P : (t + 1) * P],
-                rhs=words[:, cols].bitcast(FP8X4),
-                rhs_scale=scales[:, cols],
-                start=(opens and t == 0),
-                stop=(not opens and t == PACK - 1),
-            )
-
-        relu1 = []
-
-        def rectify(j):
-            rectified = keep.tile([P, STEP, PACK], F32, name="relu1_%d" % j)
-            nc.scalar.activation(rectified[:], banks[j][1][:].rearrange("p t v -> p v t"), ACT.Relu)
-            relu1.append(rectified)
-
-        late_half(0, "woven10")
-        for n, first in enumerate((HALF, 0, 0)):
+        for n, d in zip(range(WARM_UPS), (1, 0, 0)):
             idle = psum.tile([P, PACK * STEP], F32, name="idle%d" % n, tag="bank%d" % (STEPS + n))
             nc.tensor.matmul_mx(
                 out=idle[:],
-                lhsT=x_words[1, 0][:, first : first + P].bitcast(FP8X4),
-                lhsT_scale=x_scales[1, 0][:, first : first + P],
-                rhs=x_words[0, 0][:].bitcast(FP8X4),
-                rhs_scale=x_scales[0, 0][:],
+                lhsT=x_codes[1, 0, d][0][:, 0:P].bitcast(FP8X4),
+                lhsT_scale=x_codes[1, 0, d][1][:, 0:P],
+                rhs=codes00[0].bitcast(FP8X4),
+                rhs_scale=codes00[1],
                 start=True,
                 stop=True,
             )
+
         banks = [
             [psum.tile([P, PACK, STEP], F32, name="h%d%d" % (j, d), tag="bank%d" % (2 * j + d)) for d in range(2)]
             for j in range(STEPS)
         ]
+
         for z in range(PASSES):
-            cast_w(z)
-        quantise_w(0)
-        quantise_w(1)
-        woven11 = woven_tile("woven11", 2, "w_raw")
-        codes(1, 1, "x_words11")
-        for d in (1, 0):
-            weave(1, 1, d, woven11[:, 2 * d * HALF : 2 * (d + 1) * HALF], True)
-        quantise_x(1, 1, HALF, woven11[:, 2 * HALF : 4 * HALF])
-        quantise_piece(0, woven010[:], "w_bf")
-        quantise_x(1, 1, 0, woven11[:, 0 : 2 * HALF])
+            nc.sync.dma_start(w_raw[:, z], w1[z * K_PASS : (z + 1) * K_PASS, :].rearrange("(p j) c -> p j c", j=PACK))
+
+            def views(a, b):
+                return (
+                    w_dealt[:, z, :, a:b, :].rearrange("p t m j -> p m j t"),
+                    w_raw[:, z, :, PACK * a : PACK * b].rearrange("p j (m t) -> p m j t", t=PACK),
+                )
+
+            nc.scalar.activation(*views(0, W_ON_SCALAR[z]), ACT.Copy, scale=0.5)
+            if z == PASSES - 1:
+                nc.vector.tensor_scalar(
+                    w_dealt[:, :, :, P - 1, :].rearrange("p z t j -> p z j t"), w_raw[:, :, :, H - PACK : H], 0.5, None, ALU.mult
+                )
+            nc.vector.tensor_scalar(*views(W_ON_SCALAR[z], P - 1), 0.5, None, ALU.mult)
+        for z in range(PASSES):
+            for t in range(0, PACK, 2):
+                cols = slice(t * P, (t + 2) * P)
+                quantise((w_words[z][:, cols], w_scales[z][:, cols]), w_dealt[:, z, t : t + 2, :, :].rearrange("p t m j -> p (t m j)"))
+
+        woven11 = weave(1, 1, (0, 1), True, "w_raw")
+        code_tiles(1, 1, (0, 1), "x_words11")
+        quantise(x_codes[1, 1, 1], piece_of(woven11, 1))
+        quantise(code_tiles(0, 1, (0,), "w_dealt"), woven010[:].bitcast(BF16))
+        quantise(x_codes[1, 1, 0], piece_of(woven11, 0))
+
+        def parts_of(split):
+            count = 2 if split else 1
+            return [slice(n * STEP // count, (n + 1) * STEP // count) for n in range(count)]
+
+        relu1 = []
         for j in range(STEPS):
+            c, within = divmod(j * STEP, HALF)
             for d in (1, 0):
                 for z in range(PASSES):
+                    words, scales = x_codes[z, c, d]
                     for t in range(PACK):
-                        first_product(z, j, d, t, z == 0)
+                        nc.tensor.matmul_mx(
+                            out=banks[j][d][:, t, :],
+                            lhsT=w_words[z][:, t * P : (t + 1) * P].bitcast(FP8X4),
+                            lhsT_scale=w_scales[z][:, t * P : (t + 1) * P],
+                            rhs=words[:, within : within + STEP].bitcast(FP8X4),
+                            rhs_scale=scales[:, within : within + STEP],
+                            start=(z == 0 and t == 0),
+                            stop=(z == PASSES - 1 and t == PACK - 1),
+                        )
                 if d == 1:
-                    rectify(j)
+                    rectified = keep.tile([P, STEP, PACK], F32, name="relu1_%d" % j)
+                    for pairs in parts_of(j == 0):
+                        nc.scalar.activation(rectified[:, pairs, :], banks[j][1][:, :, pairs].rearrange("p t v -> p v t"), ACT.Relu)
+                    relu1.append(rectified)
 
         for b, (words, scales) in enumerate(((w2_words, w2_scales), (w3_words, w3_scales))):
             nc.sync.dma_start(w23_words[:, b, :].bitcast(I32), words[0].bitcast(I32))
@@ -244,14 +224,15 @@ def tile_picked_haar_relu_e_kernel(
         bands = [keep.tile([P, 2, STEP * PACK], BF16, name="band%d" % j, align_bytes=64) for j in range(STEPS)]
 
         def haar(j, b):
-            nc.vector.scalar_tensor_tensor(
-                bands[j][:, b, :].rearrange("p (v t) -> p v t", t=PACK),
-                banks[j][0][:].rearrange("p t v -> p v t"),
-                0.0,
-                relu1[j][:],
-                ALU.max,
-                (ALU.add, ALU.subtract)[b],
-            )
+            for pairs in parts_of(j == 0 and b == 0):
+                nc.vector.scalar_tensor_tensor(
+                    bands[j][:, b, :].rearrange("p (v t) -> p v t", t=PACK)[:, pairs, :],
+                    banks[j][0][:, :, pairs].rearrange("p t v -> p v t"),
+                    0.0,
+                    relu1[j][:, pairs, :],
+                    ALU.max,
+                    (ALU.add, ALU.subtract)[b],
+                )
 
         def second_product(dst, m, b, words, scales):
             nc.tensor.matmul_mx(

@@ -31,10 +31,10 @@ WARM_UPS = 3
 X_LOADS = (
     ((1024, 16), (1024, 5)),
     ((1536, 6), (512, 5)),
-    ((1152, 16), (896, 3)),
-    ((1024, 16), (512, 0), (512, 5)),
+    ((768, 16), (768, 10), (512, 4)),
+    ((768, 16), (768, 10), (512, 4)),
 )
-W_ON_SCALAR = (87, 53)
+W_ON_SCALAR = (100, 53)
 
 
 def tile_picked_haar_relu_e_kernel(
@@ -93,16 +93,30 @@ def tile_picked_haar_relu_e_kernel(
                 first = pieces[n] * V + c * HALF
                 src = picked[z][:, :, first : first + HALF]
                 dst = woven[:, 2 * n * HALF : 2 * (n + 1) * HALF]
-                if on_scalar:
-                    nc.scalar.copy(
-                        dst.rearrange("p (c i u) -> p c u i", i=LINE, u=2), src.rearrange("p u (c i) -> p c u i", i=LINE)
-                    )
+                if on_scalar == "gpsimd":
+                    nc.gpsimd.tensor_copy(dst.rearrange("p (e u) -> p e u", u=2), src.rearrange("p u e -> p e u"))
+                elif on_scalar:
+                    nc.scalar.copy(dst.rearrange("p (e u) -> p e u", u=2), src.rearrange("p u e -> p e u"))
                 else:
                     nc.vector.tensor_copy(
                         dst.bitcast(I32).rearrange("p (c i u) -> p c u i", i=LINE, u=2),
                         src.bitcast(I32).rearrange("p u (c i) -> p c u i", i=LINE),
                     )
             return woven
+
+        def weave_piece(d, tag):
+            woven = keep.tile([P, 2 * V], U32, name="woven0%d" % d, tag=tag, align_bytes=64)
+            src = picked[0][:, :, d * V : (d + 1) * V]
+            nc.gpsimd.tensor_copy(woven[:].rearrange("p (e u) -> p e u", u=2), src.rearrange("p u e -> p e u"))
+            return woven
+
+        def quantise_piece(d, woven):
+            words = keep.tile([P, V], U32, name="x_words0%d" % d, align_bytes=64)
+            scales = keep.tile([P, V], U8, name="x_scales0%d" % d, align_bytes=64)
+            for c in range(2):
+                x_codes[0, c, d] = (words[:, c * HALF : (c + 1) * HALF], scales[:, c * HALF : (c + 1) * HALF])
+            quantise((words[:], scales[:]), woven[:].bitcast(BF16))
+            return words[:], scales[:]
 
         def code_tiles(z, c, pieces, tag):
             name = "%d%d%d" % (z, c, pieces[0])
@@ -122,15 +136,14 @@ def tile_picked_haar_relu_e_kernel(
         window = load_duos(0, 1)
         for d in (1, 0):
             gather(0, 1, window, d * V, V)
-        woven011 = weave(0, 1, (1,), False, "woven011")
-        woven00 = weave(0, 0, (0, 1), False, "woven00")
-        quantise(code_tiles(0, 1, (1,), "x_words011"), woven011[:].bitcast(BF16))
+        woven01 = [weave(0, c, (1,), "gpsimd", "woven0%d1" % c) for c in range(2)]
         window = load_duos(1, 0)
-        codes00 = code_tiles(0, 0, (0, 1), raw_tag(1, 0, 0))
-        quantise(codes00, woven00[:].bitcast(BF16))
+        for c in range(2):
+            quantise(code_tiles(0, c, (1,), "x_words0%d1" % c), woven01[c][:].bitcast(BF16))
         gather(1, 0, window, 0, S)
+        woven00 = weave_piece(0, raw_tag(1, 0, 2))
+        codes00 = quantise_piece(0, woven00)
         window = load_duos(1, 1)
-        woven010 = weave(0, 1, (0,), True, raw_tag(1, 1, 2))
         for c in range(2):
             for d in (1, 0):
                 gather(1, 1, window, d * V + c * HALF, HALF)
@@ -138,7 +151,7 @@ def tile_picked_haar_relu_e_kernel(
         w_raw = keep.tile([P, PASSES, PACK, H], F32, name="w_raw", tag="w_raw", align_bytes=64)
         w_dealt = keep.tile([P, PASSES, PACK, P, PACK], BF16, name="w_dealt", tag="w_dealt", align_bytes=64)
 
-        woven10 = weave(1, 0, (0, 1), True, "woven10")
+        woven10 = weave(1, 0, (0, 1), "gpsimd", "woven10")
         code_tiles(1, 0, (0, 1), "x_words10")
         for d in (1, 0):
             quantise(x_codes[1, 0, d], piece_of(woven10, d))
@@ -183,7 +196,6 @@ def tile_picked_haar_relu_e_kernel(
         woven11 = weave(1, 1, (0, 1), True, "w_raw")
         code_tiles(1, 1, (0, 1), "x_words11")
         quantise(x_codes[1, 1, 1], piece_of(woven11, 1))
-        quantise(code_tiles(0, 1, (0,), "w_dealt"), woven010[:].bitcast(BF16))
         quantise(x_codes[1, 1, 0], piece_of(woven11, 0))
 
         def parts_of(split):
@@ -194,7 +206,8 @@ def tile_picked_haar_relu_e_kernel(
         for j in range(STEPS):
             c, within = divmod(j * STEP, HALF)
             for d in (1, 0):
-                for z in range(PASSES):
+                order = (0, 1) if c == 0 else (1, 0)
+                for z in order:
                     words, scales = x_codes[z, c, d]
                     for t in range(PACK):
                         nc.tensor.matmul_mx(
@@ -203,8 +216,8 @@ def tile_picked_haar_relu_e_kernel(
                             lhsT_scale=w_scales[z][:, t * P : (t + 1) * P],
                             rhs=words[:, within : within + STEP].bitcast(FP8X4),
                             rhs_scale=scales[:, within : within + STEP],
-                            start=(z == 0 and t == 0),
-                            stop=(z == PASSES - 1 and t == PACK - 1),
+                            start=(z == order[0] and t == 0),
+                            stop=(z == order[1] and t == PACK - 1),
                         )
                 if d == 1:
                     rectified = keep.tile([P, STEP, PACK], F32, name="relu1_%d" % j)

@@ -27,14 +27,15 @@ HALF = V // 2
 STEP = 128
 STEPS = V // STEP
 WARM_UPS = 3
+LEAD = 40
 
 X_LOADS = (
+    ((2048, 6),),
     ((1024, 16), (1024, 5)),
-    ((1536, 6), (512, 5)),
-    ((768, 16), (768, 10), (512, 4)),
-    ((768, 16), (768, 10), (512, 4)),
+    ((1024, 16), (1024, 4)),
+    ((1024, 16), (512, 0), (512, 5)),
 )
-W_ON_SCALAR = (100, 53)
+W_ON_SCALAR = (87, 53)
 
 
 def tile_picked_haar_relu_e_kernel(
@@ -138,11 +139,16 @@ def tile_picked_haar_relu_e_kernel(
             gather(0, 1, window, d * V, V)
         woven01 = [weave(0, c, (1,), "gpsimd", "woven0%d1" % c) for c in range(2)]
         window = load_duos(1, 0)
+        codes00 = (
+            keep.tile([P, V], U32, name="x_words01", align_bytes=64)[:],
+            keep.tile([P, V], U8, name="x_scales01", align_bytes=64)[:],
+        )
         for c in range(2):
-            quantise(code_tiles(0, c, (1,), "x_words0%d1" % c), woven01[c][:].bitcast(BF16))
+            x_codes[0, c, 1] = (codes00[0][:, c * HALF : (c + 1) * HALF], codes00[1][:, c * HALF : (c + 1) * HALF])
+            quantise(x_codes[0, c, 1], woven01[c][:].bitcast(BF16))
         gather(1, 0, window, 0, S)
-        woven00 = weave_piece(0, raw_tag(1, 0, 2))
-        codes00 = quantise_piece(0, woven00)
+        woven00 = weave_piece(0, raw_tag(1, 0, 1))
+        quantise(code_tiles(0, 0, (0,), "x_words000"), piece_of(woven00, 0))
         window = load_duos(1, 1)
         for c in range(2):
             for d in (1, 0):
@@ -151,7 +157,7 @@ def tile_picked_haar_relu_e_kernel(
         w_raw = keep.tile([P, PASSES, PACK, H], F32, name="w_raw", tag="w_raw", align_bytes=64)
         w_dealt = keep.tile([P, PASSES, PACK, P, PACK], BF16, name="w_dealt", tag="w_dealt", align_bytes=64)
 
-        woven10 = weave(1, 0, (0, 1), "gpsimd", "woven10")
+        woven10 = weave(1, 0, (0, 1), True, "woven10")
         code_tiles(1, 0, (0, 1), "x_words10")
         for d in (1, 0):
             quantise(x_codes[1, 0, d], piece_of(woven10, d))
@@ -189,24 +195,24 @@ def tile_picked_haar_relu_e_kernel(
                 )
             nc.vector.tensor_scalar(*views(W_ON_SCALAR[z], P - 1), 0.5, None, ALU.mult)
         for z in range(PASSES):
-            for t in range(0, PACK, 2):
-                cols = slice(t * P, (t + 2) * P)
-                quantise((w_words[z][:, cols], w_scales[z][:, cols]), w_dealt[:, z, t : t + 2, :, :].rearrange("p t m j -> p (t m j)"))
+            for first, last in ((0, 2), (2, 4)) if z == 0 else ((0, 2), (2, 3), (3, 4)):
+                cols = slice(first * P, last * P)
+                quantise((w_words[z][:, cols], w_scales[z][:, cols]), w_dealt[:, z, first:last, :, :].rearrange("p t m j -> p (t m j)"))
 
         woven11 = weave(1, 1, (0, 1), True, "w_raw")
         code_tiles(1, 1, (0, 1), "x_words11")
         quantise(x_codes[1, 1, 1], piece_of(woven11, 1))
+        quantise(code_tiles(0, 1, (0,), "w_dealt"), piece_of(woven00, 1))
         quantise(x_codes[1, 1, 0], piece_of(woven11, 0))
 
         def parts_of(split):
-            count = 2 if split else 1
-            return [slice(n * STEP // count, (n + 1) * STEP // count) for n in range(count)]
+            return [slice(0, LEAD), slice(LEAD, STEP)] if split else [slice(0, STEP)]
 
         relu1 = []
         for j in range(STEPS):
             c, within = divmod(j * STEP, HALF)
             for d in (1, 0):
-                order = (0, 1) if c == 0 else (1, 0)
+                order = (0, 1)
                 for z in order:
                     words, scales = x_codes[z, c, d]
                     for t in range(PACK):
@@ -236,8 +242,8 @@ def tile_picked_haar_relu_e_kernel(
         out_rows = out.rearrange("(m p) v -> p m v", p=P)
         bands = [keep.tile([P, 2, STEP * PACK], BF16, name="band%d" % j, align_bytes=64) for j in range(STEPS)]
 
-        def haar(j, b):
-            for pairs in parts_of(j == 0 and b == 0):
+        def haar(j, b, parts):
+            for pairs in parts:
                 nc.vector.scalar_tensor_tensor(
                     bands[j][:, b, :].rearrange("p (v t) -> p v t", t=PACK)[:, pairs, :],
                     banks[j][0][:, :, pairs].rearrange("p t v -> p v t"),
@@ -304,9 +310,11 @@ def tile_picked_haar_relu_e_kernel(
             nc.vector.tensor_copy(res_vector[:], accs[1][:, 0:STEP])
             nc.sync.dma_start(out_rows[:, 1, cols], res_vector[:])
 
-        for j in range(STEPS):
-            haar(j, 0)
-            if j > 0:
-                finish(j - 1)
-            haar(j, 1)
+        for pairs in parts_of(True):
+            haar(0, 0, [pairs])
+            haar(0, 1, [pairs])
+        for j in range(1, STEPS):
+            haar(j, 0, parts_of(False))
+            finish(j - 1)
+            haar(j, 1, parts_of(False))
         finish_last()

@@ -26,16 +26,10 @@ LINE = 4
 HALF = V // 2
 STEP = 128
 STEPS = V // STEP
-WARM_UPS = 3
 LEAD = 40
-
-X_LOADS = (
-    ((2048, 6),),
-    ((1024, 16), (1024, 5)),
-    ((1024, 16), (1024, 4)),
-    ((1024, 16), (512, 0), (512, 5)),
-)
-W_ON_SCALAR = (87, 53)
+W_ON_SCALAR = (30, 40)
+ON_VECTOR = 608
+EARLY_STEPS = 2
 
 
 def tile_picked_haar_relu_e_kernel(
@@ -54,177 +48,127 @@ def tile_picked_haar_relu_e_kernel(
 
         w_words = [keep.tile([P, H], U32, name="w_words%d" % z, align_bytes=64) for z in range(PASSES)]
         w_scales = [keep.tile([P, H], U8, name="w_scales%d" % z, align_bytes=64) for z in range(PASSES)]
-        picked = [keep.tile([P, 2, S], U32, name="picked%d" % z, align_bytes=64) for z in range(PASSES)]
         x_codes = {}
 
-        def raw_tag(z, u, n):
-            return "x_raw%d%d_%d" % (z, u, n)
-
-        def load_duos(z, u):
+        def load_row(z, t):
             rows = xT[z * K_PASS : (z + 1) * K_PASS, :].rearrange("(p t) w -> p t w", t=PACK)
-            duos = keep.tile([P, T * 2], BF16, name="duos%d%d" % (z, u), align_bytes=64)
-            col = 0
-            for n, (width, sixteenths) in enumerate(X_LOADS[2 * z + u]):
-                raw = keep.tile([P, 2, width], F32, name=raw_tag(z, u, n), tag=raw_tag(z, u, n), align_bytes=64)
-                nc.sync.dma_start(raw[:], rows[:, 2 * u : 2 * u + 2, col : col + width])
-                if (z, u, n) == (0, 0, 0):
-                    nc.sync.dma_start(offsets[:], offs)
+            row = keep.tile([P, T], F32, name="x_row%d%d" % (z, t), tag="x_row%d%d" % (z, t), align_bytes=64)
+            nc.sync.dma_start(row[:], rows[:, t, :])
+            if (z, t) == (0, 0):
+                nc.sync.dma_start(offsets[:], offs)
+            return row
 
-                def views(a, b):
-                    return (
-                        duos[:, 2 * (col + a) : 2 * (col + b)].rearrange("p (c i e) -> p c e i", i=LINE, e=2),
-                        raw[:, :, a:b].rearrange("p e (c i) -> p c e i", i=LINE),
-                    )
+        def picked(row, first, count):
+            return row[:].indirect(offsets[:, first // LIST_ROWS : (first + count) // LIST_ROWS])
 
-                cut = width * sixteenths // 16
-                if cut > 0:
-                    nc.scalar.activation(*views(0, cut), ACT.Copy)
-                if cut < width:
-                    nc.vector.tensor_copy(*views(cut, width))
-                col = col + width
-            return duos[:].bitcast(U32)
-
-        def gather(z, u, window, first, count):
-            entries = offsets[:, first // LIST_ROWS : (first + count) // LIST_ROWS]
-            nc.vector.tensor_copy(picked[z][:, u, first : first + count], window.indirect(entries))
-
-        def weave(z, c, pieces, on_scalar, tag):
-            woven = keep.tile([P, len(pieces) * 2 * HALF], U32, name="woven%d%d%d" % (z, c, pieces[0]), tag=tag, align_bytes=64)
-            for n in reversed(range(len(pieces))):
-                first = pieces[n] * V + c * HALF
-                src = picked[z][:, :, first : first + HALF]
-                dst = woven[:, 2 * n * HALF : 2 * (n + 1) * HALF]
-                if on_scalar == "gpsimd":
-                    nc.gpsimd.tensor_copy(dst.rearrange("p (e u) -> p e u", u=2), src.rearrange("p u e -> p e u"))
-                elif on_scalar:
-                    nc.scalar.copy(dst.rearrange("p (e u) -> p e u", u=2), src.rearrange("p u e -> p e u"))
-                else:
-                    nc.vector.tensor_copy(
-                        dst.bitcast(I32).rearrange("p (c i u) -> p c u i", i=LINE, u=2),
-                        src.bitcast(I32).rearrange("p u (c i) -> p c u i", i=LINE),
-                    )
-            return woven
-
-        def weave_piece(d, tag):
-            woven = keep.tile([P, 2 * V], U32, name="woven0%d" % d, tag=tag, align_bytes=64)
-            src = picked[0][:, :, d * V : (d + 1) * V]
-            nc.gpsimd.tensor_copy(woven[:].rearrange("p (e u) -> p e u", u=2), src.rearrange("p u e -> p e u"))
-            return woven
-
-        def quantise_piece(d, woven):
-            words = keep.tile([P, V], U32, name="x_words0%d" % d, align_bytes=64)
-            scales = keep.tile([P, V], U8, name="x_scales0%d" % d, align_bytes=64)
-            for c in range(2):
-                x_codes[0, c, d] = (words[:, c * HALF : (c + 1) * HALF], scales[:, c * HALF : (c + 1) * HALF])
-            quantise((words[:], scales[:]), woven[:].bitcast(BF16))
-            return words[:], scales[:]
-
-        def code_tiles(z, c, pieces, tag):
-            name = "%d%d%d" % (z, c, pieces[0])
-            words = keep.tile([P, len(pieces) * HALF], U32, name="x_words" + name, tag=tag, align_bytes=64)
-            scales = keep.tile([P, len(pieces) * HALF], U8, name="x_scales" + name, align_bytes=64)
-            for n, d in enumerate(pieces):
-                x_codes[z, c, d] = (words[:, n * HALF : (n + 1) * HALF], scales[:, n * HALF : (n + 1) * HALF])
-            return words[:], scales[:]
+        def weave_views(woven, planes):
+            return (
+                woven.rearrange("p (c i) t -> p c t i", i=LINE),
+                planes.rearrange("p t (c i) -> p c t i", i=LINE),
+            )
 
         def quantise(codes, values):
             nc.vector.quantize_mx(out=codes[0].bitcast(FP8X4), scales=codes[1], in_=values)
 
-        def piece_of(woven, d):
-            return woven[:, 2 * d * HALF : 2 * (d + 1) * HALF].bitcast(BF16)
+        def code_tiles(name, width, tag):
+            words = keep.tile([P, width], U32, name="x_words" + name, tag=tag, align_bytes=64)
+            scales = keep.tile([P, width], U8, name="x_scales" + name, align_bytes=64)
+            return words, scales
 
-        gather(0, 0, load_duos(0, 0), 0, S)
-        window = load_duos(0, 1)
-        for d in (1, 0):
-            gather(0, 1, window, d * V, V)
-        woven01 = [weave(0, c, (1,), "gpsimd", "woven0%d1" % c) for c in range(2)]
-        window = load_duos(1, 0)
-        codes00 = (
-            keep.tile([P, V], U32, name="x_words01", align_bytes=64)[:],
-            keep.tile([P, V], U8, name="x_scales01", align_bytes=64)[:],
-        )
-        for c in range(2):
-            x_codes[0, c, 1] = (codes00[0][:, c * HALF : (c + 1) * HALF], codes00[1][:, c * HALF : (c + 1) * HALF])
-            quantise(x_codes[0, c, 1], woven01[c][:].bitcast(BF16))
-        gather(1, 0, window, 0, S)
-        woven00 = weave_piece(0, raw_tag(1, 0, 1))
-        quantise(code_tiles(0, 0, (0,), "x_words000"), piece_of(woven00, 0))
-        window = load_duos(1, 1)
-        for c in range(2):
-            for d in (1, 0):
-                gather(1, 1, window, d * V + c * HALF, HALF)
+        def load_and_quantise_w(z, groups):
+            w_raw = keep.tile([P, PACK, H], F32, name="w_raw%d" % z, tag="w_raw%d" % z, align_bytes=64)
+            w_dealt = keep.tile([P, PACK, P, PACK], BF16, name="w_dealt%d" % z, tag="w_dealt%d" % z, align_bytes=64)
+            nc.sync.dma_start(w_raw[:], w1[z * K_PASS : (z + 1) * K_PASS, :].rearrange("(p j) c -> p j c", j=PACK))
 
-        w_raw = keep.tile([P, PASSES, PACK, H], F32, name="w_raw", tag="w_raw", align_bytes=64)
-        w_dealt = keep.tile([P, PASSES, PACK, P, PACK], BF16, name="w_dealt", tag="w_dealt", align_bytes=64)
+            def views(a, b):
+                return (
+                    w_dealt[:, :, a:b, :].rearrange("p t m j -> p m j t"),
+                    w_raw[:, :, PACK * a : PACK * b].rearrange("p j (m t) -> p m j t", t=PACK),
+                )
 
-        woven10 = weave(1, 0, (0, 1), True, "woven10")
-        code_tiles(1, 0, (0, 1), "x_words10")
-        for d in (1, 0):
-            quantise(x_codes[1, 0, d], piece_of(woven10, d))
+            nc.scalar.activation(*views(0, W_ON_SCALAR[z]), ACT.Copy, scale=0.5)
+            nc.vector.tensor_scalar(*views(W_ON_SCALAR[z], P), 0.5, None, ALU.mult)
+            for first, last in groups:
+                cols = slice(first * P, last * P)
+                quantise((w_words[z][:, cols], w_scales[z][:, cols]), w_dealt[:, first:last, :, :].rearrange("p t m j -> p (t m j)"))
 
-        for n, d in zip(range(WARM_UPS), (1, 0, 0)):
-            idle = psum.tile([P, PACK * STEP], F32, name="idle%d" % n, tag="bank%d" % (STEPS + n))
-            nc.tensor.matmul_mx(
-                out=idle[:],
-                lhsT=x_codes[1, 0, d][0][:, 0:P].bitcast(FP8X4),
-                lhsT_scale=x_codes[1, 0, d][1][:, 0:P],
-                rhs=codes00[0].bitcast(FP8X4),
-                rhs_scale=codes00[1],
-                start=True,
-                stop=True,
-            )
+        planes0 = keep.tile([P, PACK, S], BF16, name="planes0", align_bytes=64)
+        woven0 = [keep.tile([P, V, PACK], BF16, name="woven0%d" % d, align_bytes=64) for d in range(2)]
+        for t in range(PACK):
+            row = load_row(0, t)
+            nc.vector.tensor_copy(planes0[:, t, 0:ON_VECTOR], picked(row, 0, ON_VECTOR))
+            nc.scalar.activation(planes0[:, t, ON_VECTOR:S], picked(row, ON_VECTOR, S - ON_VECTOR), ACT.Copy)
+            if t % 2 == 1:
+                for d in (1, 0):
+                    nc.gpsimd.tensor_copy(
+                        woven0[d][:, :, t - 1 : t + 1], planes0[:, t - 1 : t + 1, d * V : (d + 1) * V].rearrange("p t e -> p e t")
+                    )
+
+        def quantise_pass0(d, tag):
+            words, scales = code_tiles("0%d" % d, V, tag)
+            quantise((words[:], scales[:]), woven0[d][:].rearrange("p e t -> p (e t)"))
+            for c in range(2):
+                x_codes[0, c, d] = (words[:, c * HALF : (c + 1) * HALF], scales[:, c * HALF : (c + 1) * HALF])
 
         banks = [
             [psum.tile([P, PACK, STEP], F32, name="h%d%d" % (j, d), tag="bank%d" % (2 * j + d)) for d in range(2)]
             for j in range(STEPS)
         ]
 
-        for z in range(PASSES):
-            nc.sync.dma_start(w_raw[:, z], w1[z * K_PASS : (z + 1) * K_PASS, :].rearrange("(p j) c -> p j c", j=PACK))
-
-            def views(a, b):
-                return (
-                    w_dealt[:, z, :, a:b, :].rearrange("p t m j -> p m j t"),
-                    w_raw[:, z, :, PACK * a : PACK * b].rearrange("p j (m t) -> p m j t", t=PACK),
+        def first_product(z, j, d):
+            c, within = divmod(j * STEP, HALF)
+            words, scales = x_codes[z, c, d]
+            order = (0, 1) if j < EARLY_STEPS else (1, 0)
+            for t in range(PACK):
+                nc.tensor.matmul_mx(
+                    out=banks[j][d][:, t, :],
+                    lhsT=w_words[z][:, t * P : (t + 1) * P].bitcast(FP8X4),
+                    lhsT_scale=w_scales[z][:, t * P : (t + 1) * P],
+                    rhs=words[:, within : within + STEP].bitcast(FP8X4),
+                    rhs_scale=scales[:, within : within + STEP],
+                    start=(z == order[0] and t == 0),
+                    stop=(z == order[1] and t == PACK - 1),
                 )
 
-            nc.scalar.activation(*views(0, W_ON_SCALAR[z]), ACT.Copy, scale=0.5)
-            if z == PASSES - 1:
-                nc.vector.tensor_scalar(
-                    w_dealt[:, :, :, P - 1, :].rearrange("p z t j -> p z j t"), w_raw[:, :, :, H - PACK : H], 0.5, None, ALU.mult
-                )
-            nc.vector.tensor_scalar(*views(W_ON_SCALAR[z], P - 1), 0.5, None, ALU.mult)
-        for z in range(PASSES):
-            for first, last in ((0, 2), (2, 4)) if z == 0 else ((0, 2), (2, 3), (3, 4)):
-                cols = slice(first * P, last * P)
-                quantise((w_words[z][:, cols], w_scales[z][:, cols]), w_dealt[:, z, first:last, :, :].rearrange("p t m j -> p (t m j)"))
+        woven1 = [[keep.tile([P, HALF, PACK], BF16, name="woven1%d%d" % (c, d), align_bytes=64) for d in range(2)] for c in range(2)]
+        planes1 = [keep.tile([P, PACK, HALF], BF16, name="planes1%d" % d, align_bytes=64) for d in range(2)]
+        for t in range(PACK):
+            row = load_row(1, t)
+            for d in (1, 0):
+                nc.vector.tensor_copy(woven1[0][d][:, :, t], picked(row, d * V, HALF))
+                nc.scalar.activation(planes1[d][:, t, :], picked(row, d * V + HALF, HALF), ACT.Copy)
+            if t == 1:
+                nc.scalar.activation(woven1[1][1][:, :, 0:2], planes1[1][:, 0:2, :].rearrange("p t e -> p e t"), ACT.Copy)
+                for d in (1, 0):
+                    quantise_pass0(d, "x_row11" if d == 1 else "x_row10")
 
-        woven11 = weave(1, 1, (0, 1), True, "w_raw")
-        code_tiles(1, 1, (0, 1), "x_words11")
-        quantise(x_codes[1, 1, 1], piece_of(woven11, 1))
-        quantise(code_tiles(0, 1, (0,), "w_dealt"), piece_of(woven00, 1))
-        quantise(x_codes[1, 1, 0], piece_of(woven11, 0))
+        def quantise_pass1(c, d, woven, tag):
+            words, scales = code_tiles("1%d%d" % (c, d), HALF, tag)
+            x_codes[1, c, d] = (words[:], scales[:])
+            quantise(x_codes[1, c, d], woven[:].rearrange("p e t -> p (e t)"))
+
+        for d in (1, 0):
+            quantise_pass1(0, d, woven1[0][d], "x_words10%d" % d)
+        nc.scalar.activation(woven1[1][1][:, :, 2:PACK], planes1[1][:, 2:PACK, :].rearrange("p t e -> p e t"), ACT.Copy)
+        load_and_quantise_w(0, ((0, 2), (2, 4)))
+        for j in range(EARLY_STEPS):
+            for d in (1, 0):
+                first_product(0, j, d)
+        late = keep.tile([P, HALF, PACK], BF16, name="late", tag="w_raw0", align_bytes=64)
+        nc.scalar.activation(*weave_views(late[:], planes1[0][:]), ACT.Copy)
+        quantise_pass1(1, 1, woven1[1][1], "w_dealt0")
+        load_and_quantise_w(1, ((0, 2), (2, 3), (3, 4)))
+        quantise_pass1(1, 0, late, "w_dealt1")
 
         def parts_of(split):
             return [slice(0, LEAD), slice(LEAD, STEP)] if split else [slice(0, STEP)]
 
         relu1 = []
         for j in range(STEPS):
-            c, within = divmod(j * STEP, HALF)
             for d in (1, 0):
-                order = (0, 1)
-                for z in order:
-                    words, scales = x_codes[z, c, d]
-                    for t in range(PACK):
-                        nc.tensor.matmul_mx(
-                            out=banks[j][d][:, t, :],
-                            lhsT=w_words[z][:, t * P : (t + 1) * P].bitcast(FP8X4),
-                            lhsT_scale=w_scales[z][:, t * P : (t + 1) * P],
-                            rhs=words[:, within : within + STEP].bitcast(FP8X4),
-                            rhs_scale=scales[:, within : within + STEP],
-                            start=(z == order[0] and t == 0),
-                            stop=(z == order[1] and t == PACK - 1),
-                        )
+                first_product(1, j, d)
+                if j >= EARLY_STEPS:
+                    first_product(0, j, d)
                 if d == 1:
                     rectified = keep.tile([P, STEP, PACK], F32, name="relu1_%d" % j)
                     for pairs in parts_of(j == 0):

@@ -27,9 +27,8 @@ HALF = V // 2
 STEP = 128
 STEPS = V // STEP
 LEAD = 40
-W_ON_SCALAR = (30, 40)
-ON_VECTOR = 608
-EARLY_STEPS = 2
+W_ON_SCALAR = (32, 42)
+EARLY = ((0, 1), (0, 0), (1, 1), (1, 0))
 
 
 def tile_picked_haar_relu_e_kernel(
@@ -75,7 +74,7 @@ def tile_picked_haar_relu_e_kernel(
             scales = keep.tile([P, width], U8, name="x_scales" + name, align_bytes=64)
             return words, scales
 
-        def load_and_quantise_w(z, groups):
+        def cast_w(z):
             w_raw = keep.tile([P, PACK, H], F32, name="w_raw%d" % z, tag="w_raw%d" % z, align_bytes=64)
             w_dealt = keep.tile([P, PACK, P, PACK], BF16, name="w_dealt%d" % z, tag="w_dealt%d" % z, align_bytes=64)
             nc.sync.dma_start(w_raw[:], w1[z * K_PASS : (z + 1) * K_PASS, :].rearrange("(p j) c -> p j c", j=PACK))
@@ -88,27 +87,29 @@ def tile_picked_haar_relu_e_kernel(
 
             nc.scalar.activation(*views(0, W_ON_SCALAR[z]), ACT.Copy, scale=0.5)
             nc.vector.tensor_scalar(*views(W_ON_SCALAR[z], P), 0.5, None, ALU.mult)
+            return w_dealt
+
+        def quantise_w(z, w_dealt, groups):
             for first, last in groups:
                 cols = slice(first * P, last * P)
                 quantise((w_words[z][:, cols], w_scales[z][:, cols]), w_dealt[:, first:last, :, :].rearrange("p t m j -> p (t m j)"))
 
-        planes0 = keep.tile([P, PACK, S], BF16, name="planes0", align_bytes=64)
-        woven0 = [keep.tile([P, V, PACK], BF16, name="woven0%d" % d, align_bytes=64) for d in range(2)]
+        planes0 = keep.tile([P, PACK, V], BF16, name="planes0", align_bytes=64)
+        woven0 = keep.tile([P, S, PACK], BF16, name="woven0", align_bytes=64)
         for t in range(PACK):
             row = load_row(0, t)
-            nc.vector.tensor_copy(planes0[:, t, 0:ON_VECTOR], picked(row, 0, ON_VECTOR))
-            nc.scalar.activation(planes0[:, t, ON_VECTOR:S], picked(row, ON_VECTOR, S - ON_VECTOR), ACT.Copy)
+            nc.vector.tensor_copy(woven0[:, 0:V, t], picked(row, 0, V))
+            nc.scalar.activation(planes0[:, t, :], picked(row, V, V), ACT.Copy)
             if t % 2 == 1:
-                for d in (1, 0):
-                    nc.gpsimd.tensor_copy(
-                        woven0[d][:, :, t - 1 : t + 1], planes0[:, t - 1 : t + 1, d * V : (d + 1) * V].rearrange("p t e -> p e t")
-                    )
+                nc.gpsimd.tensor_copy(woven0[:, V:S, t - 1 : t + 1], planes0[:, t - 1 : t + 1, :].rearrange("p t e -> p e t"))
 
-        def quantise_pass0(d, tag):
-            words, scales = code_tiles("0%d" % d, V, tag)
-            quantise((words[:], scales[:]), woven0[d][:].rearrange("p e t -> p (e t)"))
-            for c in range(2):
-                x_codes[0, c, d] = (words[:, c * HALF : (c + 1) * HALF], scales[:, c * HALF : (c + 1) * HALF])
+        def quantise_pass0(tag):
+            words, scales = code_tiles("0", S, tag)
+            quantise((words[:], scales[:]), woven0[:].rearrange("p e t -> p (e t)"))
+            for d in range(2):
+                for c in range(2):
+                    cols = slice(d * V + c * HALF, d * V + (c + 1) * HALF)
+                    x_codes[0, c, d] = (words[:, cols], scales[:, cols])
 
         banks = [
             [psum.tile([P, PACK, STEP], F32, name="h%d%d" % (j, d), tag="bank%d" % (2 * j + d)) for d in range(2)]
@@ -118,7 +119,7 @@ def tile_picked_haar_relu_e_kernel(
         def first_product(z, j, d):
             c, within = divmod(j * STEP, HALF)
             words, scales = x_codes[z, c, d]
-            order = (0, 1) if j < EARLY_STEPS else (1, 0)
+            order = (0, 1) if (j, d) in EARLY else (1, 0)
             for t in range(PACK):
                 nc.tensor.matmul_mx(
                     out=banks[j][d][:, t, :],
@@ -130,17 +131,18 @@ def tile_picked_haar_relu_e_kernel(
                     stop=(z == order[1] and t == PACK - 1),
                 )
 
-        woven1 = [[keep.tile([P, HALF, PACK], BF16, name="woven1%d%d" % (c, d), align_bytes=64) for d in range(2)] for c in range(2)]
+        woven1 = [[keep.tile([P, HALF, PACK], BF16, name="woven1%d%d" % (c, d), align_bytes=64) for d in range(2)] for c in range(1)]
+        woven1.append([None, keep.tile([P, HALF, PACK], BF16, name="woven111", align_bytes=64)])
         planes1 = [keep.tile([P, PACK, HALF], BF16, name="planes1%d" % d, align_bytes=64) for d in range(2)]
         for t in range(PACK):
             row = load_row(1, t)
             for d in (1, 0):
                 nc.vector.tensor_copy(woven1[0][d][:, :, t], picked(row, d * V, HALF))
                 nc.scalar.activation(planes1[d][:, t, :], picked(row, d * V + HALF, HALF), ACT.Copy)
+            if t == 0:
+                quantise_pass0("x_row10")
             if t == 1:
-                nc.scalar.activation(woven1[1][1][:, :, 0:2], planes1[1][:, 0:2, :].rearrange("p t e -> p e t"), ACT.Copy)
-                for d in (1, 0):
-                    quantise_pass0(d, "x_row11" if d == 1 else "x_row10")
+                nc.gpsimd.tensor_copy(woven1[1][1][:, :, 0:2], planes1[1][:, 0:2, :].rearrange("p t e -> p e t"))
 
         def quantise_pass1(c, d, woven, tag):
             words, scales = code_tiles("1%d%d" % (c, d), HALF, tag)
@@ -150,15 +152,16 @@ def tile_picked_haar_relu_e_kernel(
         for d in (1, 0):
             quantise_pass1(0, d, woven1[0][d], "x_words10%d" % d)
         nc.scalar.activation(woven1[1][1][:, :, 2:PACK], planes1[1][:, 2:PACK, :].rearrange("p t e -> p e t"), ACT.Copy)
-        load_and_quantise_w(0, ((0, 2), (2, 4)))
-        for j in range(EARLY_STEPS):
-            for d in (1, 0):
-                first_product(0, j, d)
-        late = keep.tile([P, HALF, PACK], BF16, name="late", tag="w_raw0", align_bytes=64)
+        quantise_w(0, cast_w(0), ((0, 2), (2, 4)))
+        for j, d in EARLY:
+            first_product(0, j, d)
+        quantise_w(1, cast_w(1), ((0, 2), (2, 3), (3, 4)))
+        late = keep.tile([P, HALF, PACK], BF16, name="late", tag="w_raw1", align_bytes=64)
         nc.scalar.activation(*weave_views(late[:], planes1[0][:]), ACT.Copy)
-        quantise_pass1(1, 1, woven1[1][1], "w_dealt0")
-        load_and_quantise_w(1, ((0, 2), (2, 3), (3, 4)))
-        quantise_pass1(1, 0, late, "w_dealt1")
+        words, scales = code_tiles("11", V, "w_dealt1")
+        for d, woven in ((1, woven1[1][1]), (0, late)):
+            x_codes[1, 1, d] = (words[:, d * HALF : (d + 1) * HALF], scales[:, d * HALF : (d + 1) * HALF])
+            quantise(x_codes[1, 1, d], woven[:].rearrange("p e t -> p (e t)"))
 
         def parts_of(split):
             return [slice(0, LEAD), slice(LEAD, STEP)] if split else [slice(0, STEP)]
@@ -167,7 +170,7 @@ def tile_picked_haar_relu_e_kernel(
         for j in range(STEPS):
             for d in (1, 0):
                 first_product(1, j, d)
-                if j >= EARLY_STEPS:
+                if (j, d) not in EARLY:
                     first_product(0, j, d)
                 if d == 1:
                     rectified = keep.tile([P, STEP, PACK], F32, name="relu1_%d" % j)

@@ -27,7 +27,7 @@ HALF = V // 2
 STEP = 128
 STEPS = V // STEP
 LEAD = 40
-W_ON_SCALAR = (32, 42)
+W_ON_SCALAR = (50, 42)
 EARLY = ((0, 1), (0, 0), (1, 1), (1, 0))
 
 
@@ -79,14 +79,15 @@ def tile_picked_haar_relu_e_kernel(
             w_dealt = keep.tile([P, PACK, P, PACK], BF16, name="w_dealt%d" % z, tag="w_dealt%d" % z, align_bytes=64)
             nc.sync.dma_start(w_raw[:], w1[z * K_PASS : (z + 1) * K_PASS, :].rearrange("(p j) c -> p j c", j=PACK))
 
-            def views(a, b):
+            def views(a, b, tiles):
                 return (
-                    w_dealt[:, :, a:b, :].rearrange("p t m j -> p m j t"),
-                    w_raw[:, :, PACK * a : PACK * b].rearrange("p j (m t) -> p m j t", t=PACK),
+                    w_dealt[:, tiles, a:b, :].rearrange("p t m j -> p m j t"),
+                    w_raw[:, :, PACK * a : PACK * b].rearrange("p j (m t) -> p m j t", t=PACK)[:, :, :, tiles],
                 )
 
-            nc.scalar.activation(*views(0, W_ON_SCALAR[z]), ACT.Copy, scale=0.5)
-            nc.vector.tensor_scalar(*views(W_ON_SCALAR[z], P), 0.5, None, ALU.mult)
+            for tiles in (slice(0, 2), slice(2, 4)):
+                nc.scalar.activation(*views(0, W_ON_SCALAR[z], tiles), ACT.Copy, scale=0.5)
+                nc.vector.tensor_scalar(*views(W_ON_SCALAR[z], P, tiles), 0.5, None, ALU.mult)
             return w_dealt
 
         def quantise_w(z, w_dealt, groups):
@@ -138,11 +139,15 @@ def tile_picked_haar_relu_e_kernel(
             row = load_row(1, t)
             for d in (1, 0):
                 nc.vector.tensor_copy(woven1[0][d][:, :, t], picked(row, d * V, HALF))
-                nc.scalar.activation(planes1[d][:, t, :], picked(row, d * V + HALF, HALF), ACT.Copy)
+                for first, count in ((0, STEP), (STEP, STEP)) if (t, d) == (PACK - 1, 1) else ((0, HALF),):
+                    part = slice(first, first + count)
+                    nc.scalar.activation(planes1[d][:, t, part], picked(row, d * V + HALF + first, count), ACT.Copy)
+                    if t % 2 == 1 and d == 1:
+                        nc.gpsimd.tensor_copy(
+                            woven1[1][1][:, part, t - 1 : t + 1], planes1[1][:, t - 1 : t + 1, part].rearrange("p t e -> p e t")
+                        )
             if t == 0:
                 quantise_pass0("x_row10")
-            if t == 1:
-                nc.gpsimd.tensor_copy(woven1[1][1][:, :, 0:2], planes1[1][:, 0:2, :].rearrange("p t e -> p e t"))
 
         def quantise_pass1(c, d, woven, tag):
             words, scales = code_tiles("1%d%d" % (c, d), HALF, tag)
@@ -151,17 +156,25 @@ def tile_picked_haar_relu_e_kernel(
 
         for d in (1, 0):
             quantise_pass1(0, d, woven1[0][d], "x_words10%d" % d)
-        nc.scalar.activation(woven1[1][1][:, :, 2:PACK], planes1[1][:, 2:PACK, :].rearrange("p t e -> p e t"), ACT.Copy)
         quantise_w(0, cast_w(0), ((0, 2), (2, 4)))
         for j, d in EARLY:
             first_product(0, j, d)
+
+        def weave_late(n):
+            late = keep.tile([P, STEP, PACK], BF16, name="late%d" % n, tag="w_raw%d" % n, align_bytes=64)
+            nc.scalar.activation(*weave_views(late[:], planes1[0][:, :, n * STEP : (n + 1) * STEP]), ACT.Copy)
+            return late
+
+        lates = [weave_late(0)]
         quantise_w(1, cast_w(1), ((0, 2), (2, 3), (3, 4)))
-        late = keep.tile([P, HALF, PACK], BF16, name="late", tag="w_raw1", align_bytes=64)
-        nc.scalar.activation(*weave_views(late[:], planes1[0][:]), ACT.Copy)
+        lates.append(weave_late(1))
         words, scales = code_tiles("11", V, "w_dealt1")
-        for d, woven in ((1, woven1[1][1]), (0, late)):
+        for d in range(2):
             x_codes[1, 1, d] = (words[:, d * HALF : (d + 1) * HALF], scales[:, d * HALF : (d + 1) * HALF])
-            quantise(x_codes[1, 1, d], woven[:].rearrange("p e t -> p (e t)"))
+        quantise(x_codes[1, 1, 1], woven1[1][1][:].rearrange("p e t -> p (e t)"))
+        for n, late in enumerate(lates):
+            cols = slice(n * STEP, (n + 1) * STEP)
+            quantise((words[:, cols], scales[:, cols]), late[:].rearrange("p e t -> p (e t)"))
 
         def parts_of(split):
             return [slice(0, LEAD), slice(LEAD, STEP)] if split else [slice(0, STEP)]

@@ -1,6 +1,7 @@
 from contextlib import ExitStack
 
 import concourse.mybir as mybir
+from concourse.masks import make_identity
 
 K, T, S, V, H, N = 1024, 2048, 1024, 512, 512, 256
 FLOPS = 2 * K * H * S + 2 * 2 * H * N * V
@@ -26,9 +27,10 @@ LINE = 4
 HALF = V // 2
 STEP = 128
 STEPS = V // STEP
+TURNED = 2
 LEAD = 40
-W_ON_SCALAR = (50, 42)
-EARLY = ((0, 1), (0, 0), (1, 1), (1, 0))
+W_ON_SCALAR = (42, 42)
+EARLY = ((0, 1), (0, 0), (1, 1), (1, 0), (2, 1), (2, 0), (3, 1), (3, 0))
 
 
 def tile_picked_haar_relu_e_kernel(
@@ -40,12 +42,14 @@ def tile_picked_haar_relu_e_kernel(
         psum = ctx.enter_context(tc.psum_pool(name="psum", bufs=1))
 
         offsets = keep.tile([P, S // LIST_ROWS], U16, name="offsets")
+        identity = keep.tile([P, P], F32, name="identity")
+        make_identity(nc, identity[:])
 
         w23_scales = keep.tile([P, 2, N], U8, name="w23_scales", align_bytes=64)
         nc.vector.memset(w23_scales[:].rearrange("p a n -> p (a n)").bitcast(I32), 0)
         w23_words = keep.tile([P, 2, 2 * N], U8, name="w23_words", align_bytes=64)
 
-        w_words = [keep.tile([P, H], U32, name="w_words%d" % z, align_bytes=64) for z in range(PASSES)]
+        w_words = {}
         w_scales = [keep.tile([P, H], U8, name="w_scales%d" % z, align_bytes=64) for z in range(PASSES)]
         x_codes = {}
 
@@ -90,10 +94,13 @@ def tile_picked_haar_relu_e_kernel(
                 nc.vector.tensor_scalar(*views(W_ON_SCALAR[z], P, tiles), 0.5, None, ALU.mult)
             return w_dealt
 
-        def quantise_w(z, w_dealt, groups):
+        def quantise_w(z, w_dealt, groups, tag):
+            w_words[z] = keep.tile([P, H], U32, name="w_words%d" % z, tag=tag, align_bytes=64)
             for first, last in groups:
                 cols = slice(first * P, last * P)
                 quantise((w_words[z][:, cols], w_scales[z][:, cols]), w_dealt[:, first:last, :, :].rearrange("p t m j -> p (t m j)"))
+
+        w_dealt0 = cast_w(0)
 
         planes0 = keep.tile([P, PACK, V], BF16, name="planes0", align_bytes=64)
         woven0 = keep.tile([P, S, PACK], BF16, name="woven0", align_bytes=64)
@@ -104,13 +111,12 @@ def tile_picked_haar_relu_e_kernel(
             if t % 2 == 1:
                 nc.gpsimd.tensor_copy(woven0[:, V:S, t - 1 : t + 1], planes0[:, t - 1 : t + 1, :].rearrange("p t e -> p e t"))
 
-        def quantise_pass0(tag):
-            words, scales = code_tiles("0", S, tag)
-            quantise((words[:], scales[:]), woven0[:].rearrange("p e t -> p (e t)"))
-            for d in range(2):
-                for c in range(2):
-                    cols = slice(d * V + c * HALF, d * V + (c + 1) * HALF)
-                    x_codes[0, c, d] = (words[:, cols], scales[:, cols])
+        def quantise_pass0(d, tag):
+            words, scales = code_tiles("0%d" % d, V, tag)
+            quantise((words[:], scales[:]), woven0[:, d * V : (d + 1) * V, :].rearrange("p e t -> p (e t)"))
+            for c in range(2):
+                cols = slice(c * HALF, (c + 1) * HALF)
+                x_codes[0, c, d] = (words[:, cols], scales[:, cols])
 
         banks = [
             [psum.tile([P, PACK, STEP], F32, name="h%d%d" % (j, d), tag="bank%d" % (2 * j + d)) for d in range(2)]
@@ -120,14 +126,27 @@ def tile_picked_haar_relu_e_kernel(
         def first_product(z, j, d):
             c, within = divmod(j * STEP, HALF)
             words, scales = x_codes[z, c, d]
+            patch_words = words[:, within : within + STEP].bitcast(FP8X4)
+            patch_scales = scales[:, within : within + STEP]
             order = (0, 1) if (j, d) in EARLY else (1, 0)
+            if j == TURNED:
+                nc.tensor.matmul_mx(
+                    out=banks[j][d][:].rearrange("p t m -> p (t m)"),
+                    lhsT=patch_words,
+                    lhsT_scale=patch_scales,
+                    rhs=w_words[z][:].bitcast(FP8X4),
+                    rhs_scale=w_scales[z][:],
+                    start=(z == order[0]),
+                    stop=(z == order[1]),
+                )
+                return
             for t in range(PACK):
                 nc.tensor.matmul_mx(
                     out=banks[j][d][:, t, :],
                     lhsT=w_words[z][:, t * P : (t + 1) * P].bitcast(FP8X4),
                     lhsT_scale=w_scales[z][:, t * P : (t + 1) * P],
-                    rhs=words[:, within : within + STEP].bitcast(FP8X4),
-                    rhs_scale=scales[:, within : within + STEP],
+                    rhs=patch_words,
+                    rhs_scale=patch_scales,
                     start=(z == order[0] and t == 0),
                     stop=(z == order[1] and t == PACK - 1),
                 )
@@ -146,8 +165,12 @@ def tile_picked_haar_relu_e_kernel(
                         nc.gpsimd.tensor_copy(
                             woven1[1][1][:, part, t - 1 : t + 1], planes1[1][:, t - 1 : t + 1, part].rearrange("p t e -> p e t")
                         )
-            if t == 0:
-                quantise_pass0("x_row10")
+            if t < 2:
+                quantise_pass0(t, "x_row1%d" % t)
+            if t == 2:
+                quantise_w(0, w_dealt0, ((0, 2), (2, 4)), "x_row12")
+                for j, d in EARLY:
+                    first_product(0, j, d)
 
         def quantise_pass1(c, d, woven, tag):
             words, scales = code_tiles("1%d%d" % (c, d), HALF, tag)
@@ -156,17 +179,14 @@ def tile_picked_haar_relu_e_kernel(
 
         for d in (1, 0):
             quantise_pass1(0, d, woven1[0][d], "x_words10%d" % d)
-        quantise_w(0, cast_w(0), ((0, 2), (2, 4)))
-        for j, d in EARLY:
-            first_product(0, j, d)
 
         def weave_late(n):
-            late = keep.tile([P, STEP, PACK], BF16, name="late%d" % n, tag="w_raw%d" % n, align_bytes=64)
+            late = keep.tile([P, STEP, PACK], BF16, name="late%d" % n, tag=("late0", "w_raw1")[n], align_bytes=64)
             nc.scalar.activation(*weave_views(late[:], planes1[0][:, :, n * STEP : (n + 1) * STEP]), ACT.Copy)
             return late
 
         lates = [weave_late(0)]
-        quantise_w(1, cast_w(1), ((0, 2), (2, 3), (3, 4)))
+        quantise_w(1, cast_w(1), ((0, 2), (2, 3), (3, 4)), "w_words1")
         lates.append(weave_late(1))
         words, scales = code_tiles("11", V, "w_dealt1")
         for d in range(2):
@@ -179,17 +199,19 @@ def tile_picked_haar_relu_e_kernel(
         def parts_of(split):
             return [slice(0, LEAD), slice(LEAD, STEP)] if split else [slice(0, STEP)]
 
-        relu1 = []
+        rectified = {}
         for j in range(STEPS):
             for d in (1, 0):
                 first_product(1, j, d)
                 if (j, d) not in EARLY:
                     first_product(0, j, d)
-                if d == 1:
-                    rectified = keep.tile([P, STEP, PACK], F32, name="relu1_%d" % j)
+                if j == TURNED:
+                    rectified[j, d] = keep.tile([P, PACK, P], F32, name="relu%d%d" % (j, d))
+                    nc.scalar.activation(rectified[j, d][:], banks[j][d][:], ACT.Relu)
+                elif d == 1:
+                    rectified[j, d] = keep.tile([P, STEP, PACK], F32, name="relu%d%d" % (j, d))
                     for pairs in parts_of(j == 0):
-                        nc.scalar.activation(rectified[:, pairs, :], banks[j][1][:, :, pairs].rearrange("p t v -> p v t"), ACT.Relu)
-                    relu1.append(rectified)
+                        nc.scalar.activation(rectified[j, d][:, pairs, :], banks[j][d][:, :, pairs].rearrange("p t v -> p v t"), ACT.Relu)
 
         for b, (words, scales) in enumerate(((w2_words, w2_scales), (w3_words, w3_scales))):
             nc.sync.dma_start(w23_words[:, b, :].bitcast(I32), words[0].bitcast(I32))
@@ -200,81 +222,79 @@ def tile_picked_haar_relu_e_kernel(
                 )
 
         out_rows = out.rearrange("(m p) v -> p m v", p=P)
-        bands = [keep.tile([P, 2, STEP * PACK], BF16, name="band%d" % j, align_bytes=64) for j in range(STEPS)]
+        bands = [keep.tile([P, 2, HALF, PACK], BF16, name="bands%d" % c, align_bytes=64) for c in range(2)]
+        band_words = [keep.tile([P, 2, HALF], U32, name="band_words%d" % c, align_bytes=64) for c in range(2)]
+        band_scales = [keep.tile([P, 2, HALF], U8, name="band_scales%d" % c, align_bytes=64) for c in range(2)]
 
-        def haar(j, b, parts):
-            for pairs in parts:
-                nc.vector.scalar_tensor_tensor(
-                    bands[j][:, b, :].rearrange("p (v t) -> p v t", t=PACK)[:, pairs, :],
-                    banks[j][0][:, :, pairs].rearrange("p t v -> p v t"),
-                    0.0,
-                    relu1[j][:, pairs, :],
-                    ALU.max,
-                    (ALU.add, ALU.subtract)[b],
-                )
+        def band_of(j, b):
+            c, within = divmod(j * STEP, HALF)
+            return bands[c][:, b, within : within + STEP, :]
 
-        def second_product(dst, m, b, words, scales):
-            nc.tensor.matmul_mx(
-                out=dst,
-                lhsT=w23_words[:, b, 2 * P * m : 2 * P * (m + 1)].bitcast(FP4X4),
-                lhsT_scale=w23_scales[:, b, P * m : P * (m + 1)],
-                rhs=words[:, b * STEP : (b + 1) * STEP].bitcast(FP8X4),
-                rhs_scale=scales[:, b * STEP : (b + 1) * STEP],
-                start=(b == 0),
-                stop=(b == 1),
+        def haar(j, b, pairs):
+            nc.vector.scalar_tensor_tensor(
+                band_of(j, b)[:, pairs, :],
+                banks[j][0][:, :, pairs].rearrange("p t v -> p v t"),
+                0.0,
+                rectified[j, 1][:, pairs, :],
+                ALU.max,
+                (ALU.add, ALU.subtract)[b],
             )
 
-        def band_codes(j):
-            words = keep.tile([P, 2 * STEP], U32, name="band_words%d" % j, align_bytes=64)
-            scales = keep.tile([P, 2 * STEP], U8, name="band_scales%d" % j, align_bytes=64)
-            return words, scales
+        def haar_turned(b, terms, tag):
+            total = psum.tile([P, PACK, STEP], F32, name="sum%d" % b, tag=tag)
+            for n, term in enumerate(terms):
+                for t in range(PACK):
+                    nc.tensor.matmul(
+                        total[:, t, :], term[:, t, :], identity[:], is_transpose=True,
+                        start=(n == 0 and t == 0), stop=(n == len(terms) - 1 and t == PACK - 1),
+                    )
+            nc.scalar.activation(band_of(TURNED, b), total[:].rearrange("p t v -> p v t"), ACT.Copy)
 
-        def multiply_bands(j, acc):
-            words, scales = band_codes(j)
-            nc.vector.quantize_mx(out=words[:].bitcast(FP8X4), scales=scales[:], in_=bands[j][:].rearrange("p b w -> p (b w)"))
-            for m in range(N // P):
-                for b in range(2):
-                    second_product(acc[:, m, :], m, b, words, scales)
+        def quantise_band(c, b, pairs):
+            quantise((band_words[c][:, b, pairs], band_scales[c][:, b, pairs]), bands[c][:, b, pairs, :].rearrange("p v t -> p (v t)"))
 
-        acc_early = psum.tile([P, N // P, 2 * STEP], F32, name="acc_early", tag="bank%d" % (2 * STEPS - 1))
-        res_early = keep.tile([P, N // P, 2 * STEP], F32, name="res_early")
+        def second_product(dst, c, m, b, pairs, last):
+            nc.tensor.matmul_mx(
+                out=dst[:, pairs],
+                lhsT=w23_words[:, b, 2 * P * m : 2 * P * (m + 1)].bitcast(FP4X4),
+                lhsT_scale=w23_scales[:, b, P * m : P * (m + 1)],
+                rhs=band_words[c][:, b, pairs].bitcast(FP8X4),
+                rhs_scale=band_scales[c][:, b, pairs],
+                start=(b == 0),
+                stop=last,
+            )
 
-        def finish(j):
-            cols = slice(j * STEP, (j + 1) * STEP)
-            if j < 2:
-                multiply_bands(j, acc_early[:, :, cols])
-                if j == 1:
-                    nc.scalar.activation(res_early[:], acc_early[:], ACT.Copy)
-                    nc.sync.dma_start(out_rows[:, :, 0 : 2 * STEP], res_early[:])
-            else:
-                acc = psum.tile([P, N // P, 2 * STEP], F32, name="acc%d" % j, tag="bank%d" % (2 * j + 1))
-                multiply_bands(j, acc[:, :, 0:STEP])
-                res = keep.tile([P, N // P, STEP], F32, name="res%d" % j)
-                nc.scalar.activation(res[:], acc[:, :, 0:STEP], ACT.Copy)
-                nc.sync.dma_start(out_rows[:, :, cols], res[:])
-
-        def finish_last():
-            j = STEPS - 1
-            cols = slice(j * STEP, (j + 1) * STEP)
-            words, scales = band_codes(j)
-            accs = [psum.tile([P, PACK * STEP], F32, name="acc_last%d" % m, tag="bank%d" % (2 * m)) for m in range(N // P)]
-            for b in range(2):
-                band_cols = slice(b * STEP, (b + 1) * STEP)
-                nc.vector.quantize_mx(out=words[:, band_cols].bitcast(FP8X4), scales=scales[:, band_cols], in_=bands[j][:, b, :])
-                for m in range(N // P):
-                    second_product(accs[m][:, 0:STEP], m, b, words, scales)
-            res_scalar = keep.tile([P, STEP], F32, name="res_last0")
-            nc.scalar.activation(res_scalar[:], accs[0][:, 0:STEP], ACT.Copy)
-            nc.scalar.dma_start(out_rows[:, 0, cols], res_scalar[:])
-            res_vector = keep.tile([P, STEP], F32, name="res_last1")
-            nc.vector.tensor_copy(res_vector[:], accs[1][:, 0:STEP])
-            nc.sync.dma_start(out_rows[:, 1, cols], res_vector[:])
-
+        whole, half = slice(0, STEP), slice(0, HALF)
+        negated = keep.tile([P, PACK, P], F32, name="negated")
+        nc.gpsimd.tensor_scalar(negated[:], rectified[TURNED, 1][:], -1.0, 0.0, ALU.mult, ALU.add)
         for pairs in parts_of(True):
-            haar(0, 0, [pairs])
-            haar(0, 1, [pairs])
-        for j in range(1, STEPS):
-            haar(j, 0, parts_of(False))
-            finish(j - 1)
-            haar(j, 1, parts_of(False))
-        finish_last()
+            haar(0, 0, pairs)
+            haar(0, 1, pairs)
+        haar(1, 0, whole)
+        haar(1, 1, whole)
+        quantise_band(0, 0, half)
+        quantise_band(0, 1, half)
+        haar_turned(0, (rectified[TURNED, 1], rectified[TURNED, 0]), "bank%d" % (2 * TURNED + 1))
+        haar_turned(1, (negated, rectified[TURNED, 0]), "bank1")
+
+        acc_early = psum.tile([P, N // P, HALF], F32, name="acc_early", tag="bank%d" % (2 * STEPS - 1))
+        for m in range(N // P):
+            for b in range(2):
+                second_product(acc_early[:, m, :], 0, m, b, half, b == 1)
+        res_early = keep.tile([P, N // P, HALF], F32, name="res_early")
+        nc.scalar.activation(res_early[:], acc_early[:], ACT.Copy)
+        nc.sync.dma_start(out_rows[:, :, 0:HALF], res_early[:])
+
+        accs = [psum.tile([P, PACK * STEP], F32, name="acc_last%d" % m, tag="bank%d" % (2 * m)) for m in range(N // P)]
+        haar(3, 0, whole)
+        haar(3, 1, whole)
+        for b, pairs, last in ((0, half, False), (1, whole, False), (1, slice(STEP, HALF), True)):
+            quantise_band(1, b, pairs)
+            for m in range(N // P):
+                second_product(accs[m], 1, m, b, pairs, last)
+        res_scalar = keep.tile([P, HALF], F32, name="res_last0")
+        nc.scalar.activation(res_scalar[:], accs[0][:, 0:HALF], ACT.Copy)
+        nc.scalar.dma_start(out_rows[:, 0, HALF:V], res_scalar[:])
+        res_vector = keep.tile([P, HALF], F32, name="res_last1")
+        nc.vector.tensor_copy(res_vector[:], accs[1][:, 0:HALF])
+        nc.sync.dma_start(out_rows[:, 1, HALF:V], res_vector[:])

@@ -100,8 +100,6 @@ def tile_picked_haar_relu_e_kernel(
                 cols = slice(first * P, last * P)
                 quantise((w_words[z][:, cols], w_scales[z][:, cols]), w_dealt[:, first:last, :, :].rearrange("p t m j -> p (t m j)"))
 
-        w_dealt0 = cast_w(0)
-
         planes0 = keep.tile([P, PACK, V], BF16, name="planes0", align_bytes=64)
         woven0 = keep.tile([P, S, PACK], BF16, name="woven0", align_bytes=64)
         for t in range(PACK):
@@ -168,7 +166,7 @@ def tile_picked_haar_relu_e_kernel(
             if t < 2:
                 quantise_pass0(t, "x_row1%d" % t)
             if t == 2:
-                quantise_w(0, w_dealt0, ((0, 2), (2, 4)), "x_row12")
+                quantise_w(0, cast_w(0), ((0, 2), (2, 4)), "w_words0")
                 for j, d in EARLY:
                     first_product(0, j, d)
 

@@ -29,6 +29,8 @@ STEP = 128
 STEPS = V // STEP
 TURNED = 2
 LEAD = 40
+ON_GPSIMD = 192
+LAST_GATHERS = ((0, 64), (64, 128), (192, 64))
 W_ON_SCALAR = (42, 42)
 EARLY = ((0, 1), (0, 0), (1, 1), (1, 0), (2, 1), (2, 0), (3, 1), (3, 0))
 
@@ -112,9 +114,9 @@ def tile_picked_haar_relu_e_kernel(
         def quantise_pass0(d, tag):
             words, scales = code_tiles("0%d" % d, V, tag)
             quantise((words[:], scales[:]), woven0[:, d * V : (d + 1) * V, :].rearrange("p e t -> p (e t)"))
-            for c in range(2):
-                cols = slice(c * HALF, (c + 1) * HALF)
-                x_codes[0, c, d] = (words[:, cols], scales[:, cols])
+            for j in range(STEPS):
+                cols = slice(j * STEP, (j + 1) * STEP)
+                x_codes[0, j, d] = (words[:, cols], scales[:, cols])
 
         banks = [
             [psum.tile([P, PACK, STEP], F32, name="h%d%d" % (j, d), tag="bank%d" % (2 * j + d)) for d in range(2)]
@@ -122,10 +124,8 @@ def tile_picked_haar_relu_e_kernel(
         ]
 
         def first_product(z, j, d):
-            c, within = divmod(j * STEP, HALF)
-            words, scales = x_codes[z, c, d]
-            patch_words = words[:, within : within + STEP].bitcast(FP8X4)
-            patch_scales = scales[:, within : within + STEP]
+            patch_words, patch_scales = x_codes[z, j, d]
+            patch_words = patch_words.bitcast(FP8X4)
             order = (0, 1) if (j, d) in EARLY else (1, 0)
             if j == TURNED:
                 nc.tensor.matmul_mx(
@@ -149,57 +149,66 @@ def tile_picked_haar_relu_e_kernel(
                     stop=(z == order[1] and t == PACK - 1),
                 )
 
-        woven1 = [[keep.tile([P, HALF, PACK], BF16, name="woven1%d%d" % (c, d), align_bytes=64) for d in range(2)] for c in range(1)]
-        woven1.append([None, keep.tile([P, HALF, PACK], BF16, name="woven111", align_bytes=64)])
-        planes1 = [keep.tile([P, PACK, HALF], BF16, name="planes1%d" % d, align_bytes=64) for d in range(2)]
+        woven1 = [keep.tile([P, HALF, PACK], BF16, name="woven1%d" % d, align_bytes=64) for d in range(2)]
+        planes1 = keep.tile([P, PACK, 2 * HALF], BF16, name="planes1", align_bytes=64)
         for t in range(PACK):
             row = load_row(1, t)
             for d in (1, 0):
-                nc.vector.tensor_copy(woven1[0][d][:, :, t], picked(row, d * V, HALF))
-                for first, count in ((0, STEP), (STEP, STEP)) if (t, d) == (PACK - 1, 1) else ((0, HALF),):
-                    part = slice(first, first + count)
-                    nc.scalar.activation(planes1[d][:, t, part], picked(row, d * V + HALF + first, count), ACT.Copy)
-                    if t % 2 == 1 and d == 1:
-                        nc.gpsimd.tensor_copy(
-                            woven1[1][1][:, part, t - 1 : t + 1], planes1[1][:, t - 1 : t + 1, part].rearrange("p t e -> p e t")
-                        )
-            if t < 2:
-                quantise_pass0(t, "x_row1%d" % t)
+                nc.vector.tensor_copy(woven1[d][:, :, t], picked(row, d * V, HALF))
+                for first, count in LAST_GATHERS if (t, d) == (PACK - 1, 1) else ((0, HALF),):
+                    at = (1 - d) * HALF + first
+                    nc.scalar.activation(planes1[:, t, at : at + count], picked(row, d * V + HALF + first, count), ACT.Copy)
+            if t in (1, 2):
+                quantise_pass0(t - 1, "x_row1%d" % t)
             if t == 2:
                 quantise_w(0, cast_w(0), ((0, 2), (2, 4)), "w_words0")
                 for j, d in EARLY:
                     first_product(0, j, d)
 
-        def quantise_pass1(c, d, woven, tag):
-            words, scales = code_tiles("1%d%d" % (c, d), HALF, tag)
-            x_codes[1, c, d] = (words[:], scales[:])
-            quantise(x_codes[1, c, d], woven[:].rearrange("p e t -> p (e t)"))
+        def quantise_pass1(name, tag, calls, owners):
+            words, scales = code_tiles(name, STEP * len(owners), tag)
+            for woven, first in calls:
+                cols = slice(first, first + woven.shape[1])
+                quantise((words[:, cols], scales[:, cols]), woven.rearrange("p e t -> p (e t)"))
+            for n, (j, d) in enumerate(owners):
+                x_codes[1, j, d] = (words[:, n * STEP : (n + 1) * STEP], scales[:, n * STEP : (n + 1) * STEP])
 
-        for d in (1, 0):
-            quantise_pass1(0, d, woven1[0][d], "x_words10%d" % d)
+        on_gpsimd = keep.tile([P, ON_GPSIMD, PACK], BF16, name="on_gpsimd", align_bytes=64)
+        for first, count in LAST_GATHERS[:-1]:
+            entries = slice(first, first + count)
+            nc.gpsimd.tensor_scalar(
+                on_gpsimd[:, entries, :], planes1[:, :, entries].rearrange("p t e -> p e t"), 1.0, 0.0, ALU.mult, ALU.add
+            )
+        quantise_pass1("1a", "x_words1a", [(woven1[1][:], 0), (woven1[0][:], HALF)], [(0, 1), (1, 1), (0, 0), (1, 0)])
 
-        def weave_late(n):
-            late = keep.tile([P, STEP, PACK], BF16, name="late%d" % n, tag=("late0", "w_raw1")[n], align_bytes=64)
-            nc.scalar.activation(*weave_views(late[:], planes1[0][:, :, n * STEP : (n + 1) * STEP]), ACT.Copy)
-            return late
+        def weave_on_scalar(first, last, tag):
+            woven = keep.tile([P, last - first, PACK], BF16, name=tag + "_woven", tag=tag, align_bytes=64)
+            nc.scalar.activation(*weave_views(woven[:], planes1[:, :, first:last]), ACT.Copy)
+            return woven
 
-        lates = [weave_late(0)]
+        ahead = weave_on_scalar(3 * STEP, 4 * STEP, "ahead")
         quantise_w(1, cast_w(1), ((0, 2), (2, 3), (3, 4)), "w_words1")
-        lates.append(weave_late(1))
-        words, scales = code_tiles("11", V, "w_dealt1")
-        for d in range(2):
-            x_codes[1, 1, d] = (words[:, d * HALF : (d + 1) * HALF], scales[:, d * HALF : (d + 1) * HALF])
-        quantise(x_codes[1, 1, 1], woven1[1][1][:].rearrange("p e t -> p (e t)"))
-        for n, late in enumerate(lates):
-            cols = slice(n * STEP, (n + 1) * STEP)
-            quantise((words[:, cols], scales[:, cols]), late[:].rearrange("p e t -> p (e t)"))
+        behind = weave_on_scalar(ON_GPSIMD, 3 * STEP, "w_raw1")
+        rest = HALF - ON_GPSIMD
+        quantise_pass1(
+            "1b",
+            "w_dealt1",
+            [
+                (on_gpsimd[:, 0:STEP, :], 0),
+                (ahead[:], 3 * STEP),
+                (on_gpsimd[:, STEP:ON_GPSIMD, :], STEP),
+                (behind[:, rest : rest + STEP, :], 2 * STEP),
+                (behind[:, 0:rest, :], ON_GPSIMD),
+            ],
+            [(2, 1), (3, 1), (2, 0), (3, 0)],
+        )
 
         def parts_of(split):
             return [slice(0, LEAD), slice(LEAD, STEP)] if split else [slice(0, STEP)]
 
         rectified = {}
-        for j in range(STEPS):
-            for d in (1, 0):
+        def close_step(j, pieces):
+            for d in pieces:
                 first_product(1, j, d)
                 if (j, d) not in EARLY:
                     first_product(0, j, d)
@@ -210,6 +219,9 @@ def tile_picked_haar_relu_e_kernel(
                     rectified[j, d] = keep.tile([P, STEP, PACK], F32, name="relu%d%d" % (j, d))
                     for pairs in parts_of(j == 0):
                         nc.scalar.activation(rectified[j, d][:, pairs, :], banks[j][d][:, :, pairs].rearrange("p t v -> p v t"), ACT.Relu)
+
+        for j in range(STEPS):
+            close_step(j, (1, 0))
 
         for b, (words, scales) in enumerate(((w2_words, w2_scales), (w3_words, w3_scales))):
             nc.sync.dma_start(w23_words[:, b, :].bitcast(I32), words[0].bitcast(I32))

@@ -263,15 +263,15 @@ def tile_picked_haar_relu_e_kernel(
         def quantise_band(c, b, pairs):
             quantise((band_words[c][:, b, pairs], band_scales[c][:, b, pairs]), bands[c][:, b, pairs, :].rearrange("p v t -> p (v t)"))
 
-        def second_product(dst, c, m, b, pairs, last):
+        def second_product(dst, c, m, b, pairs):
             nc.tensor.matmul_mx(
-                out=dst[:, pairs],
+                out=dst,
                 lhsT=w23_words[:, b, 2 * P * m : 2 * P * (m + 1)].bitcast(FP4X4),
                 lhsT_scale=w23_scales[:, b, P * m : P * (m + 1)],
                 rhs=band_words[c][:, b, pairs].bitcast(FP8X4),
                 rhs_scale=band_scales[c][:, b, pairs],
                 start=(b == 0),
-                stop=last,
+                stop=(b == 1),
             )
 
         whole, half = slice(0, STEP), slice(0, HALF)
@@ -290,21 +290,31 @@ def tile_picked_haar_relu_e_kernel(
         acc_early = psum.tile([P, N // P, HALF], F32, name="acc_early", tag="bank%d" % (2 * STEPS - 1))
         for m in range(N // P):
             for b in range(2):
-                second_product(acc_early[:, m, :], 0, m, b, half, b == 1)
+                second_product(acc_early[:, m, :], 0, m, b, half)
         res_early = keep.tile([P, N // P, HALF], F32, name="res_early")
         nc.scalar.activation(res_early[:], acc_early[:], ACT.Copy)
         nc.sync.dma_start(out_rows[:, :, 0:HALF], res_early[:])
 
         accs = [psum.tile([P, PACK * STEP], F32, name="acc_last%d" % m, tag="bank%d" % (2 * m)) for m in range(N // P)]
+        last = slice(STEP, HALF)
         haar(3, 0, whole)
+        quantise_band(1, 0, whole)
         haar(3, 1, whole)
-        for b, pairs, last in ((0, half, False), (1, whole, False), (1, slice(STEP, HALF), True)):
-            quantise_band(1, b, pairs)
+        quantise_band(1, 1, whole)
+        quantise_band(1, 0, last)
+        quantise_band(1, 1, last)
+        accs_turned = [psum.tile([P, PACK * STEP], F32, name="acc_turned%d" % m, tag="bank%d" % (3 + m)) for m in range(N // P)]
+        for b in range(2):
             for m in range(N // P):
-                second_product(accs[m], 1, m, b, pairs, last)
+                second_product(accs_turned[m][:, 0:STEP], 1, m, b, whole)
+        for b in range(2):
+            for m in range(N // P):
+                second_product(accs[m][:, 0:STEP], 1, m, b, last)
         res_scalar = keep.tile([P, HALF], F32, name="res_last0")
-        nc.scalar.activation(res_scalar[:], accs[0][:, 0:HALF], ACT.Copy)
+        nc.scalar.activation(res_scalar[:, whole], accs_turned[0][:, 0:STEP], ACT.Copy)
+        nc.scalar.activation(res_scalar[:, last], accs[0][:, 0:STEP], ACT.Copy)
         nc.scalar.dma_start(out_rows[:, 0, HALF:V], res_scalar[:])
         res_vector = keep.tile([P, HALF], F32, name="res_last1")
-        nc.vector.tensor_copy(res_vector[:], accs[1][:, 0:HALF])
+        nc.vector.tensor_copy(res_vector[:, whole], accs_turned[1][:, 0:STEP])
+        nc.vector.tensor_copy(res_vector[:, last], accs[1][:, 0:STEP])
         nc.sync.dma_start(out_rows[:, 1, HALF:V], res_vector[:])

@@ -31,7 +31,7 @@ TURNED = 2
 LEAD = 40
 ON_GPSIMD = 192
 LAST_GATHERS = ((0, 64), (64, 128), (192, 64))
-W_ON_SCALAR = (42, 42)
+W_ON_SCALAR = (66, 42)
 EARLY = ((0, 1), (0, 0), (1, 1), (1, 0), (2, 1), (2, 0), (3, 1), (3, 0))
 
 
@@ -109,7 +109,9 @@ def tile_picked_haar_relu_e_kernel(
             nc.vector.tensor_copy(woven0[:, 0:V, t], picked(row, 0, V))
             nc.scalar.activation(planes0[:, t, :], picked(row, V, V), ACT.Copy)
             if t % 2 == 1:
-                nc.gpsimd.tensor_copy(woven0[:, V:S, t - 1 : t + 1], planes0[:, t - 1 : t + 1, :].rearrange("p t e -> p e t"))
+                nc.gpsimd.tensor_scalar(
+                    woven0[:, V:S, t - 1 : t + 1], planes0[:, t - 1 : t + 1, :].rearrange("p t e -> p e t"), 1.0, 0.0, ALU.mult, ALU.add
+                )
 
         def quantise_pass0(d, tag):
             words, scales = code_tiles("0%d" % d, V, tag)
@@ -158,8 +160,8 @@ def tile_picked_haar_relu_e_kernel(
                 for first, count in LAST_GATHERS if (t, d) == (PACK - 1, 1) else ((0, HALF),):
                     at = (1 - d) * HALF + first
                     nc.scalar.activation(planes1[:, t, at : at + count], picked(row, d * V + HALF + first, count), ACT.Copy)
-            if t in (1, 2):
-                quantise_pass0(t - 1, "x_row1%d" % t)
+            if t < 2:
+                quantise_pass0(t, "x_row1%d" % t)
             if t == 2:
                 quantise_w(0, cast_w(0), ((0, 2), (2, 4)), "w_words0")
                 for j, d in EARLY:

@@ -103,22 +103,22 @@ def tile_picked_haar_relu_e_kernel(
                 quantise((w_words[z][:, cols], w_scales[z][:, cols]), w_dealt[:, first:last, :, :].rearrange("p t m j -> p (t m j)"))
 
         planes0 = keep.tile([P, PACK, V], BF16, name="planes0", align_bytes=64)
-        woven0 = keep.tile([P, S, PACK], BF16, name="woven0", align_bytes=64)
+        woven0 = keep.tile([P, V, PACK], BF16, name="woven00", tag="woven0", align_bytes=64)
         for t in range(PACK):
             row = load_row(0, t)
-            nc.vector.tensor_copy(woven0[:, 0:V, t], picked(row, 0, V))
+            nc.vector.tensor_copy(woven0[:, :, t], picked(row, 0, V))
             nc.scalar.activation(planes0[:, t, :], picked(row, V, V), ACT.Copy)
-            if t % 2 == 1:
-                nc.gpsimd.tensor_scalar(
-                    woven0[:, V:S, t - 1 : t + 1], planes0[:, t - 1 : t + 1, :].rearrange("p t e -> p e t"), 1.0, 0.0, ALU.mult, ALU.add
-                )
 
-        def quantise_pass0(d, tag):
+        def quantise_pass0(d, woven, tag):
             words, scales = code_tiles("0%d" % d, V, tag)
-            quantise((words[:], scales[:]), woven0[:, d * V : (d + 1) * V, :].rearrange("p e t -> p (e t)"))
+            quantise((words[:], scales[:]), woven[:].rearrange("p e t -> p (e t)"))
             for j in range(STEPS):
                 cols = slice(j * STEP, (j + 1) * STEP)
                 x_codes[0, j, d] = (words[:, cols], scales[:, cols])
+
+        quantise_pass0(0, woven0, "x_words00")
+        woven01 = keep.tile([P, V, PACK], BF16, name="woven01", tag="woven0", align_bytes=64)
+        nc.gpsimd.tensor_scalar(woven01[:], planes0[:].rearrange("p t e -> p e t"), 1.0, 0.0, ALU.mult, ALU.add)
 
         banks = [
             [psum.tile([P, PACK, STEP], F32, name="h%d%d" % (j, d), tag="bank%d" % (2 * j + d)) for d in range(2)]
@@ -160,8 +160,8 @@ def tile_picked_haar_relu_e_kernel(
                 for first, count in LAST_GATHERS if (t, d) == (PACK - 1, 1) else ((0, HALF),):
                     at = (1 - d) * HALF + first
                     nc.scalar.activation(planes1[:, t, at : at + count], picked(row, d * V + HALF + first, count), ACT.Copy)
-            if t < 2:
-                quantise_pass0(t, "x_row1%d" % t)
+            if t == 1:
+                quantise_pass0(1, woven01, "x_row11")
             if t == 2:
                 quantise_w(0, cast_w(0), ((0, 2), (2, 4)), "w_words0")
                 for j, d in EARLY:

@@ -31,7 +31,7 @@ TURNED = 2
 LEAD = 40
 ON_GPSIMD = 192
 LAST_GATHERS = ((0, 64), (64, 128), (192, 64))
-W_ON_SCALAR = (66, 42)
+W_ON_SCALAR = ((66, 66), (50, 42))
 EARLY = ((0, 1), (0, 0), (1, 1), (1, 0), (2, 1), (2, 0), (3, 1), (3, 0))
 
 
@@ -91,9 +91,9 @@ def tile_picked_haar_relu_e_kernel(
                     w_raw[:, :, PACK * a : PACK * b].rearrange("p j (m t) -> p m j t", t=PACK)[:, :, :, tiles],
                 )
 
-            for tiles in (slice(0, 2), slice(2, 4)):
-                nc.scalar.activation(*views(0, W_ON_SCALAR[z], tiles), ACT.Copy, scale=0.5)
-                nc.vector.tensor_scalar(*views(W_ON_SCALAR[z], P, tiles), 0.5, None, ALU.mult)
+            for tiles, share in zip((slice(0, 2), slice(2, 4)), W_ON_SCALAR[z]):
+                nc.scalar.activation(*views(0, share, tiles), ACT.Copy, scale=0.5)
+                nc.vector.tensor_scalar(*views(share, P, tiles), 0.5, None, ALU.mult)
             return w_dealt
 
         def quantise_w(z, w_dealt, groups, tag):
@@ -157,9 +157,12 @@ def tile_picked_haar_relu_e_kernel(
             row = load_row(1, t)
             for d in (1, 0):
                 nc.vector.tensor_copy(woven1[d][:, :, t], picked(row, d * V, HALF))
-                for first, count in LAST_GATHERS if (t, d) == (PACK - 1, 1) else ((0, HALF),):
-                    at = (1 - d) * HALF + first
-                    nc.scalar.activation(planes1[:, t, at : at + count], picked(row, d * V + HALF + first, count), ACT.Copy)
+            runs = [(1, 0, HALF), (0, 0, HALF)]
+            if t == PACK - 1:
+                runs = [(1,) + run for run in LAST_GATHERS[:-1]] + [(0, 0, HALF), (1,) + LAST_GATHERS[-1]]
+            for d, first, count in runs:
+                at = (1 - d) * HALF + first
+                nc.scalar.activation(planes1[:, t, at : at + count], picked(row, d * V + HALF + first, count), ACT.Copy)
             if t == 1:
                 quantise_pass0(1, woven01, "x_row11")
             if t == 2:

@@ -32,7 +32,7 @@ LEAD = 40
 ON_GPSIMD = 192
 LAST_GATHERS = ((0, 64), (64, 128), (192, 64))
 W_ON_SCALAR = ((66, 66), (50, 42))
-EARLY = ((0, 1), (0, 0), (1, 1), (1, 0), (2, 1), (2, 0), (3, 1), (3, 0))
+EARLY = ((0, 1), (0, 0), (1, 1), (1, 0), (2, 1), (3, 1), (2, 0), (3, 0))
 
 
 def tile_picked_haar_relu_e_kernel(
@@ -109,8 +109,11 @@ def tile_picked_haar_relu_e_kernel(
             nc.vector.tensor_copy(woven0[:, :, t], picked(row, 0, V))
             nc.scalar.activation(planes0[:, t, :], picked(row, V, V), ACT.Copy)
 
+        pass0_scales = {}
+
         def quantise_pass0(d, woven, tag):
             words, scales = code_tiles("0%d" % d, V, tag)
+            pass0_scales[d] = scales
             quantise((words[:], scales[:]), woven[:].rearrange("p e t -> p (e t)"))
             for j in range(STEPS):
                 cols = slice(j * STEP, (j + 1) * STEP)
@@ -167,7 +170,7 @@ def tile_picked_haar_relu_e_kernel(
                 quantise_pass0(1, woven01, "x_row11")
             if t == 2:
                 quantise_w(0, cast_w(0), ((0, 2), (2, 4)), "w_words0")
-                for j, d in EARLY:
+                for j, d in EARLY[:-2]:
                     first_product(0, j, d)
 
         def quantise_pass1(name, tag, calls, owners):
@@ -184,7 +187,14 @@ def tile_picked_haar_relu_e_kernel(
             nc.gpsimd.tensor_scalar(
                 on_gpsimd[:, entries, :], planes1[:, :, entries].rearrange("p t e -> p e t"), 1.0, 0.0, ALU.mult, ALU.add
             )
-        quantise_pass1("1a", "x_words1a", [(woven1[1][:], 0), (woven1[0][:], HALF)], [(0, 1), (1, 1), (0, 0), (1, 0)])
+        quantise_pass1("1a", "x_words1a", [(woven1[1][:], 0)], [(0, 1), (1, 1)])
+        packed_words = keep.tile([P, HALF], U32, name="x_words1p", align_bytes=64)
+        packed_scales = pass0_scales[0][SCALE_ROWS:P, HALF:V]
+        quantise((packed_words[:], packed_scales), woven1[0][:].rearrange("p e t -> p (e t)"))
+        for j in range(2):
+            x_codes[1, j, 0] = (packed_words[:, j * STEP : (j + 1) * STEP], packed_scales[:, j * STEP : (j + 1) * STEP])
+        for j, d in EARLY[-2:]:
+            first_product(0, j, d)
 
         def weave_on_scalar(first, last, tag):
             woven = keep.tile([P, last - first, PACK], BF16, name=tag + "_woven", tag=tag, align_bytes=64)

@@ -29,9 +29,10 @@ STEP = 128
 STEPS = V // STEP
 TURNED = 2
 LEAD = 40
+FIRST = 384
 ON_GPSIMD = 192
 LAST_GATHERS = ((0, 64), (64, 128), (192, 64))
-W_ON_SCALAR = ((66, 66), (50, 42))
+W_ON_SCALAR = ((60, 60), (50, 42))
 EARLY = ((0, 1), (0, 0), (1, 1), (1, 0), (2, 1), (3, 1), (2, 0), (3, 0))
 
 
@@ -59,12 +60,18 @@ def tile_picked_haar_relu_e_kernel(
             rows = xT[z * K_PASS : (z + 1) * K_PASS, :].rearrange("(p t) w -> p t w", t=PACK)
             row = keep.tile([P, T], F32, name="x_row%d%d" % (z, t), tag="x_row%d%d" % (z, t), align_bytes=64)
             nc.sync.dma_start(row[:], rows[:, t, :])
-            if (z, t) == (0, 0):
+            return row[:]
+
+        def load_pair(u):
+            rows = xT[0:K_PASS, :].rearrange("(p t) w -> p t w", t=PACK)
+            pair = keep.tile([P, 2, T], F32, name="x_pair%d" % u, align_bytes=64)
+            nc.sync.dma_start(pair[:], rows[:, 2 * u : 2 * u + 2, :])
+            if u == 0:
                 nc.sync.dma_start(offsets[:], offs)
-            return row
+            return pair
 
         def picked(row, first, count):
-            return row[:].indirect(offsets[:, first // LIST_ROWS : (first + count) // LIST_ROWS])
+            return row.indirect(offsets[:, first // LIST_ROWS : (first + count) // LIST_ROWS])
 
         def weave_views(woven, planes):
             return (
@@ -102,25 +109,30 @@ def tile_picked_haar_relu_e_kernel(
                 cols = slice(first * P, last * P)
                 quantise((w_words[z][:, cols], w_scales[z][:, cols]), w_dealt[:, first:last, :, :].rearrange("p t m j -> p (t m j)"))
 
-        planes0 = keep.tile([P, PACK, V], BF16, name="planes0", align_bytes=64)
-        woven0 = keep.tile([P, V, PACK], BF16, name="woven00", tag="woven0", align_bytes=64)
-        for t in range(PACK):
-            row = load_row(0, t)
-            nc.vector.tensor_copy(woven0[:, :, t], picked(row, 0, V))
-            nc.scalar.activation(planes0[:, t, :], picked(row, V, V), ACT.Copy)
+        planes0 = keep.tile([P, PACK, S - FIRST], F32, name="planes0", align_bytes=64)
+        woven0 = keep.tile([P, FIRST, PACK], BF16, name="woven00", align_bytes=64)
+        for u in range(2):
+            pair = load_pair(u)
+            for e in range(2):
+                nc.vector.tensor_copy(woven0[:, :, 2 * u + e], picked(pair[:, e, :], 0, FIRST))
+                nc.scalar.activation(planes0[:, 2 * u + e, :], picked(pair[:, e, :], FIRST, S - FIRST), ACT.Copy)
+        pass0_scales = keep.tile([P, S], U8, name="x_scales0", align_bytes=64)
 
-        pass0_scales = {}
+        def quantise_pass0(woven, first, tag, widths):
+            words = keep.tile([P, woven.shape[1]], U32, name="x_words0_%d" % first, tag=tag, align_bytes=64)
+            at = 0
+            for width in widths:
+                quantise(
+                    (words[:, at : at + width], pass0_scales[:, first + at : first + at + width]),
+                    woven[:, at : at + width, :].rearrange("p e t -> p (e t)"),
+                )
+                at = at + width
+            for at in range(0, woven.shape[1], STEP):
+                d, j = divmod((first + at) // STEP, STEPS)
+                x_codes[0, j, d] = (words[:, at : at + STEP], pass0_scales[:, first + at : first + at + STEP])
 
-        def quantise_pass0(d, woven, tag):
-            words, scales = code_tiles("0%d" % d, V, tag)
-            pass0_scales[d] = scales
-            quantise((words[:], scales[:]), woven[:].rearrange("p e t -> p (e t)"))
-            for j in range(STEPS):
-                cols = slice(j * STEP, (j + 1) * STEP)
-                x_codes[0, j, d] = (words[:, cols], scales[:, cols])
-
-        quantise_pass0(0, woven0, "x_words00")
-        woven01 = keep.tile([P, V, PACK], BF16, name="woven01", tag="woven0", align_bytes=64)
+        quantise_pass0(woven0, 0, "x_words00", (FIRST,))
+        woven01 = keep.tile([P, S - FIRST, PACK], BF16, name="woven01", align_bytes=64)
         nc.gpsimd.tensor_scalar(woven01[:], planes0[:].rearrange("p t e -> p e t"), 1.0, 0.0, ALU.mult, ALU.add)
 
         banks = [
@@ -166,9 +178,8 @@ def tile_picked_haar_relu_e_kernel(
             for d, first, count in runs:
                 at = (1 - d) * HALF + first
                 nc.scalar.activation(planes1[:, t, at : at + count], picked(row, d * V + HALF + first, count), ACT.Copy)
-            if t == 1:
-                quantise_pass0(1, woven01, "x_row11")
             if t == 2:
+                quantise_pass0(woven01, FIRST, "x_row12", (STEP, V))
                 quantise_w(0, cast_w(0), ((0, 2), (2, 4)), "w_words0")
                 for j, d in EARLY[:-2]:
                     first_product(0, j, d)
@@ -189,7 +200,7 @@ def tile_picked_haar_relu_e_kernel(
             )
         quantise_pass1("1a", "x_words1a", [(woven1[1][:], 0)], [(0, 1), (1, 1)])
         packed_words = keep.tile([P, HALF], U32, name="x_words1p", align_bytes=64)
-        packed_scales = pass0_scales[0][SCALE_ROWS:P, HALF:V]
+        packed_scales = pass0_scales[SCALE_ROWS:P, HALF:V]
         quantise((packed_words[:], packed_scales), woven1[0][:].rearrange("p e t -> p (e t)"))
         for j in range(2):
             x_codes[1, j, 0] = (packed_words[:, j * STEP : (j + 1) * STEP], packed_scales[:, j * STEP : (j + 1) * STEP])
@@ -302,12 +313,13 @@ def tile_picked_haar_relu_e_kernel(
         haar_turned(0, (rectified[TURNED, 1], rectified[TURNED, 0]), "bank%d" % (2 * TURNED + 1))
         haar_turned(1, (negated, rectified[TURNED, 0]), "bank1")
 
-        acc_early = psum.tile([P, N // P, HALF], F32, name="acc_early", tag="bank%d" % (2 * STEPS - 1))
-        for m in range(N // P):
-            for b in range(2):
-                second_product(acc_early[:, m, :], 0, m, b, half)
+        accs_early = [psum.tile([P, HALF], F32, name="acc_early%d" % m, tag="bank%d" % (3 + 4 * m)) for m in range(N // P)]
+        for b in range(2):
+            for m in range(N // P):
+                second_product(accs_early[m][:], 0, m, b, half)
         res_early = keep.tile([P, N // P, HALF], F32, name="res_early")
-        nc.scalar.activation(res_early[:], acc_early[:], ACT.Copy)
+        for m in range(N // P):
+            nc.scalar.activation(res_early[:, m, :], accs_early[m][:], ACT.Copy)
         nc.sync.dma_start(out_rows[:, :, 0:HALF], res_early[:])
 
         accs = [psum.tile([P, PACK * STEP], F32, name="acc_last%d" % m, tag="bank%d" % (2 * m)) for m in range(N // P)]
@@ -318,7 +330,7 @@ def tile_picked_haar_relu_e_kernel(
         quantise_band(1, 1, whole)
         quantise_band(1, 0, last)
         quantise_band(1, 1, last)
-        accs_turned = [psum.tile([P, PACK * STEP], F32, name="acc_turned%d" % m, tag="bank%d" % (3 + m)) for m in range(N // P)]
+        accs_turned = [psum.tile([P, PACK * STEP], F32, name="acc_turned%d" % m, tag="bank%d" % (4 + m)) for m in range(N // P)]
         for b in range(2):
             for m in range(N // P):
                 second_product(accs_turned[m][:, 0:STEP], 1, m, b, whole)

@@ -337,11 +337,9 @@ def tile_picked_haar_relu_e_kernel(
         for b in range(2):
             for m in range(N // P):
                 second_product(accs[m][:, 0:STEP], 1, m, b, last)
-        res_scalar = keep.tile([P, HALF], F32, name="res_last0")
-        nc.scalar.activation(res_scalar[:, whole], accs_turned[0][:, 0:STEP], ACT.Copy)
-        nc.scalar.activation(res_scalar[:, last], accs[0][:, 0:STEP], ACT.Copy)
-        nc.scalar.dma_start(out_rows[:, 0, HALF:V], res_scalar[:])
-        res_vector = keep.tile([P, HALF], F32, name="res_last1")
-        nc.vector.tensor_copy(res_vector[:, whole], accs_turned[1][:, 0:STEP])
-        nc.vector.tensor_copy(res_vector[:, last], accs[1][:, 0:STEP])
-        nc.sync.dma_start(out_rows[:, 1, HALF:V], res_vector[:])
+        res_late = keep.tile([P, N // P, HALF], F32, name="res_late")
+        nc.scalar.activation(res_late[:, 0, whole], accs_turned[0][:, 0:STEP], ACT.Copy)
+        nc.scalar.activation(res_late[:, 0, last], accs[0][:, 0:STEP], ACT.Copy)
+        nc.vector.tensor_copy(res_late[:, 1, whole], accs_turned[1][:, 0:STEP])
+        nc.vector.tensor_copy(res_late[:, 1, last], accs[1][:, 0:STEP])
+        nc.sync.dma_start(out_rows[:, :, HALF:V], res_late[:])

@@ -198,12 +198,12 @@ def tile_picked_haar_relu_e_kernel(
             nc.gpsimd.tensor_scalar(
                 on_gpsimd[:, entries, :], planes1[:, :, entries].rearrange("p t e -> p e t"), 1.0, 0.0, ALU.mult, ALU.add
             )
-        quantise_pass1("1a", "x_words1a", [(woven1[1][:], 0)], [(0, 1), (1, 1)])
         packed_words = keep.tile([P, HALF], U32, name="x_words1p", align_bytes=64)
         packed_scales = pass0_scales[SCALE_ROWS:P, HALF:V]
-        quantise((packed_words[:], packed_scales), woven1[0][:].rearrange("p e t -> p (e t)"))
+        quantise((packed_words[:], packed_scales), woven1[1][:].rearrange("p e t -> p (e t)"))
         for j in range(2):
-            x_codes[1, j, 0] = (packed_words[:, j * STEP : (j + 1) * STEP], packed_scales[:, j * STEP : (j + 1) * STEP])
+            x_codes[1, j, 1] = (packed_words[:, j * STEP : (j + 1) * STEP], packed_scales[:, j * STEP : (j + 1) * STEP])
+        quantise_pass1("1a", "x_words1a", [(woven1[0][:, 0:STEP, :], 0)], [(0, 0)])
         for j, d in EARLY[-2:]:
             first_product(0, j, d)
 
@@ -220,13 +220,14 @@ def tile_picked_haar_relu_e_kernel(
             "1b",
             "w_dealt1",
             [
+                (woven1[0][:, STEP:HALF, :], 4 * STEP),
                 (on_gpsimd[:, 0:STEP, :], 0),
                 (ahead[:], 3 * STEP),
                 (on_gpsimd[:, STEP:ON_GPSIMD, :], STEP),
                 (behind[:, rest : rest + STEP, :], 2 * STEP),
                 (behind[:, 0:rest, :], ON_GPSIMD),
             ],
-            [(2, 1), (3, 1), (2, 0), (3, 0)],
+            [(2, 1), (3, 1), (2, 0), (3, 0), (1, 0)],
         )
 
         def parts_of(split):

@@ -52,6 +52,10 @@ def tile_picked_haar_relu_e_kernel(
         nc.vector.memset(w23_scales[:].rearrange("p a n -> p (a n)").bitcast(I32), 0)
         w23_words = keep.tile([P, 2, 2 * N], U8, name="w23_words", align_bytes=64)
 
+        warm = keep.tile([P, 2], F32, name="warm")
+        nc.vector.memset(warm[:, 0:1], 0.0)
+        nc.scalar.activation(warm[:, 1:2], warm[:, 0:1], ACT.Copy)
+
         w_words = {}
         w_scales = [keep.tile([P, H], U8, name="w_scales%d" % z, align_bytes=64) for z in range(PASSES)]
         x_codes = {}

from contextlib import ExitStack

import concourse.mybir as mybir
from concourse.masks import make_identity

K, T, S, V, H, N = 1024, 2048, 1024, 512, 512, 256
FLOPS = 2 * K * H * S + 2 * 2 * H * N * V

F32 = mybir.dt.float32
BF16 = mybir.dt.bfloat16
U32 = mybir.dt.uint32
I32 = mybir.dt.int32
U16 = mybir.dt.uint16
U8 = mybir.dt.uint8
FP8X4 = mybir.dt.float8_e4m3fn_x4
FP4X4 = mybir.dt.float4_e2m1fn_x4
ACT = mybir.ActivationFunctionType
ALU = mybir.AluOpType

P = 128
PACK = 4
K_PASS = P * PACK
PASSES = K // K_PASS
LIST_ROWS = 16
SCALE_ROWS = 4
LINE = 4
HALF = V // 2
STEP = 128
STEPS = V // STEP
TURNED = 2
LEAD = 40
FIRST = 384
ON_GPSIMD = 192
LAST_GATHERS = ((0, 64), (64, 128), (192, 64))
W_ON_SCALAR = ((60, 60), (50, 42))
EARLY = ((0, 1), (0, 0), (1, 1), (1, 0), (2, 1), (3, 1), (2, 0), (3, 0))


def tile_picked_haar_relu_e_kernel(
    tc, xT, w1, w2_words, w2_scales, w3_words, w3_scales, offs, out
):
    nc = tc.nc
    with ExitStack() as ctx:
        keep = ctx.enter_context(tc.tile_pool(name="keep", bufs=1))
        psum = ctx.enter_context(tc.psum_pool(name="psum", bufs=1))

        offsets = keep.tile([P, S // LIST_ROWS], U16, name="offsets")
        identity = keep.tile([P, P], F32, name="identity")
        make_identity(nc, identity[:])

        w23_scales = keep.tile([P, 2, N], U8, name="w23_scales", align_bytes=64)
        nc.vector.memset(w23_scales[:].rearrange("p a n -> p (a n)").bitcast(I32), 0)
        w23_words = keep.tile([P, 2, 2 * N], U8, name="w23_words", align_bytes=64)

        warm = keep.tile([P, 2], F32, name="warm")
        nc.vector.memset(warm[:, 0:1], 0.0)
        nc.scalar.activation(warm[:, 1:2], warm[:, 0:1], ACT.Copy)

        w_words = {}
        w_scales = [keep.tile([P, H], U8, name="w_scales%d" % z, align_bytes=64) for z in range(PASSES)]
        x_codes = {}

        def load_row(z, t):
            rows = xT[z * K_PASS : (z + 1) * K_PASS, :].rearrange("(p t) w -> p t w", t=PACK)
            row = keep.tile([P, T], F32, name="x_row%d%d" % (z, t), tag="x_row%d%d" % (z, t), align_bytes=64)
            nc.sync.dma_start(row[:], rows[:, t, :])
            return row[:]

        def load_pair(u):
            rows = xT[0:K_PASS, :].rearrange("(p t) w -> p t w", t=PACK)
            pair = keep.tile([P, 2, T], F32, name="x_pair%d" % u, align_bytes=64)
            nc.sync.dma_start(pair[:], rows[:, 2 * u : 2 * u + 2, :])
            if u == 0:
                nc.sync.dma_start(offsets[:], offs)
            return pair

        def picked(row, first, count):
            return row.indirect(offsets[:, first // LIST_ROWS : (first + count) // LIST_ROWS])

        def weave_views(woven, planes):
            return (
                woven.rearrange("p (c i) t -> p c t i", i=LINE),
                planes.rearrange("p t (c i) -> p c t i", i=LINE),
            )

        def quantise(codes, values):
            nc.vector.quantize_mx(out=codes[0].bitcast(FP8X4), scales=codes[1], in_=values)

        def code_tiles(name, width, tag):
            words = keep.tile([P, width], U32, name="x_words" + name, tag=tag, align_bytes=64)
            scales = keep.tile([P, width], U8, name="x_scales" + name, align_bytes=64)
            return words, scales

        def cast_w(z):
            w_raw = keep.tile([P, PACK, H], F32, name="w_raw%d" % z, tag="w_raw%d" % z, align_bytes=64)
            w_dealt = keep.tile([P, PACK, P, PACK], BF16, name="w_dealt%d" % z, tag="w_dealt%d" % z, align_bytes=64)
            nc.sync.dma_start(w_raw[:], w1[z * K_PASS : (z + 1) * K_PASS, :].rearrange("(p j) c -> p j c", j=PACK))

            def views(a, b, tiles):
                return (
                    w_dealt[:, tiles, a:b, :].rearrange("p t m j -> p m j t"),
                    w_raw[:, :, PACK * a : PACK * b].rearrange("p j (m t) -> p m j t", t=PACK)[:, :, :, tiles],
                )

            for tiles, share in zip((slice(0, 2), slice(2, 4)), W_ON_SCALAR[z]):
                nc.scalar.activation(*views(0, share, tiles), ACT.Copy, scale=0.5)
                nc.vector.tensor_scalar(*views(share, P, tiles), 0.5, None, ALU.mult)
            return w_dealt

        def quantise_w(z, w_dealt, groups, tag):
            w_words[z] = keep.tile([P, H], U32, name="w_words%d" % z, tag=tag, align_bytes=64)
            for first, last in groups:
                cols = slice(first * P, last * P)
                quantise((w_words[z][:, cols], w_scales[z][:, cols]), w_dealt[:, first:last, :, :].rearrange("p t m j -> p (t m j)"))

        planes0 = keep.tile([P, PACK, S - FIRST], F32, name="planes0", align_bytes=64)
        woven0 = keep.tile([P, FIRST, PACK], BF16, name="woven00", align_bytes=64)
        for u in range(2):
            pair = load_pair(u)
            for e in range(2):
                nc.vector.tensor_copy(woven0[:, :, 2 * u + e], picked(pair[:, e, :], 0, FIRST))
                nc.scalar.activation(planes0[:, 2 * u + e, :], picked(pair[:, e, :], FIRST, S - FIRST), ACT.Copy)
        pass0_scales = keep.tile([P, S], U8, name="x_scales0", align_bytes=64)

        def quantise_pass0(woven, first, tag, widths):
            words = keep.tile([P, woven.shape[1]], U32, name="x_words0_%d" % first, tag=tag, align_bytes=64)
            at = 0
            for width in widths:
                quantise(
                    (words[:, at : at + width], pass0_scales[:, first + at : first + at + width]),
                    woven[:, at : at + width, :].rearrange("p e t -> p (e t)"),
                )
                at = at + width
            for at in range(0, woven.shape[1], STEP):
                d, j = divmod((first + at) // STEP, STEPS)
                x_codes[0, j, d] = (words[:, at : at + STEP], pass0_scales[:, first + at : first + at + STEP])

        quantise_pass0(woven0, 0, "x_words00", (FIRST,))
        woven01 = keep.tile([P, S - FIRST, PACK], BF16, name="woven01", align_bytes=64)
        nc.gpsimd.tensor_scalar(woven01[:], planes0[:].rearrange("p t e -> p e t"), 1.0, 0.0, ALU.mult, ALU.add)

        banks = [
            [psum.tile([P, PACK, STEP], F32, name="h%d%d" % (j, d), tag="bank%d" % (2 * j + d)) for d in range(2)]
            for j in range(STEPS)
        ]

        def first_product(z, j, d):
            patch_words, patch_scales = x_codes[z, j, d]
            patch_words = patch_words.bitcast(FP8X4)
            order = (0, 1) if (j, d) in EARLY else (1, 0)
            if j == TURNED:
                nc.tensor.matmul_mx(
                    out=banks[j][d][:].rearrange("p t m -> p (t m)"),
                    lhsT=patch_words,
                    lhsT_scale=patch_scales,
                    rhs=w_words[z][:].bitcast(FP8X4),
                    rhs_scale=w_scales[z][:],
                    start=(z == order[0]),
                    stop=(z == order[1]),
                )
                return
            for t in range(PACK):
                nc.tensor.matmul_mx(
                    out=banks[j][d][:, t, :],
                    lhsT=w_words[z][:, t * P : (t + 1) * P].bitcast(FP8X4),
                    lhsT_scale=w_scales[z][:, t * P : (t + 1) * P],
                    rhs=patch_words,
                    rhs_scale=patch_scales,
                    start=(z == order[0] and t == 0),
                    stop=(z == order[1] and t == PACK - 1),
                )

        woven1 = [keep.tile([P, HALF, PACK], BF16, name="woven1%d" % d, align_bytes=64) for d in range(2)]
        planes1 = keep.tile([P, PACK, 2 * HALF], BF16, name="planes1", align_bytes=64)
        for t in range(PACK):
            row = load_row(1, t)
            for d in (1, 0):
                nc.vector.tensor_copy(woven1[d][:, :, t], picked(row, d * V, HALF))
            runs = [(1, 0, HALF), (0, 0, HALF)]
            if t == PACK - 1:
                runs = [(1,) + run for run in LAST_GATHERS[:-1]] + [(0, 0, HALF), (1,) + LAST_GATHERS[-1]]
            for d, first, count in runs:
                at = (1 - d) * HALF + first
                nc.scalar.activation(planes1[:, t, at : at + count], picked(row, d * V + HALF + first, count), ACT.Copy)
            if t == 2:
                quantise_pass0(woven01, FIRST, "x_row12", (STEP, V))
                quantise_w(0, cast_w(0), ((0, 2), (2, 4)), "w_words0")
                for j, d in EARLY[:-2]:
                    first_product(0, j, d)

        def quantise_pass1(name, tag, calls, owners):
            words, scales = code_tiles(name, STEP * len(owners), tag)
            for woven, first in calls:
                cols = slice(first, first + woven.shape[1])
                quantise((words[:, cols], scales[:, cols]), woven.rearrange("p e t -> p (e t)"))
            for n, (j, d) in enumerate(owners):
                x_codes[1, j, d] = (words[:, n * STEP : (n + 1) * STEP], scales[:, n * STEP : (n + 1) * STEP])

        on_gpsimd = keep.tile([P, ON_GPSIMD, PACK], BF16, name="on_gpsimd", align_bytes=64)
        for first, count in LAST_GATHERS[:-1]:
            entries = slice(first, first + count)
            nc.gpsimd.tensor_scalar(
                on_gpsimd[:, entries, :], planes1[:, :, entries].rearrange("p t e -> p e t"), 1.0, 0.0, ALU.mult, ALU.add
            )
        packed_words = keep.tile([P, HALF], U32, name="x_words1p", align_bytes=64)
        packed_scales = pass0_scales[SCALE_ROWS:P, HALF:V]
        quantise((packed_words[:], packed_scales), woven1[1][:].rearrange("p e t -> p (e t)"))
        for j in range(2):
            x_codes[1, j, 1] = (packed_words[:, j * STEP : (j + 1) * STEP], packed_scales[:, j * STEP : (j + 1) * STEP])
        quantise_pass1("1a", "x_words1a", [(woven1[0][:, 0:STEP, :], 0)], [(0, 0)])
        for j, d in EARLY[-2:]:
            first_product(0, j, d)

        def weave_on_scalar(first, last, tag):
            woven = keep.tile([P, last - first, PACK], BF16, name=tag + "_woven", tag=tag, align_bytes=64)
            nc.scalar.activation(*weave_views(woven[:], planes1[:, :, first:last]), ACT.Copy)
            return woven

        ahead = weave_on_scalar(3 * STEP, 4 * STEP, "ahead")
        quantise_w(1, cast_w(1), ((0, 2), (2, 3), (3, 4)), "w_words1")
        behind = weave_on_scalar(ON_GPSIMD, 3 * STEP, "w_raw1")
        rest = HALF - ON_GPSIMD
        quantise_pass1(
            "1b",
            "w_dealt1",
            [
                (woven1[0][:, STEP:HALF, :], 4 * STEP),
                (on_gpsimd[:, 0:STEP, :], 0),
                (ahead[:], 3 * STEP),
                (on_gpsimd[:, STEP:ON_GPSIMD, :], STEP),
                (behind[:, rest : rest + STEP, :], 2 * STEP),
                (behind[:, 0:rest, :], ON_GPSIMD),
            ],
            [(2, 1), (3, 1), (2, 0), (3, 0), (1, 0)],
        )

        def parts_of(split):
            return [slice(0, LEAD), slice(LEAD, STEP)] if split else [slice(0, STEP)]

        rectified = {}
        def close_step(j, pieces):
            for d in pieces:
                first_product(1, j, d)
                if (j, d) not in EARLY:
                    first_product(0, j, d)
                if j == TURNED:
                    rectified[j, d] = keep.tile([P, PACK, P], F32, name="relu%d%d" % (j, d))
                    nc.scalar.activation(rectified[j, d][:], banks[j][d][:], ACT.Relu)
                elif d == 1:
                    rectified[j, d] = keep.tile([P, STEP, PACK], F32, name="relu%d%d" % (j, d))
                    for pairs in parts_of(j == 0):
                        nc.scalar.activation(rectified[j, d][:, pairs, :], banks[j][d][:, :, pairs].rearrange("p t v -> p v t"), ACT.Relu)

        for j in range(STEPS):
            close_step(j, (1, 0))

        for b, (words, scales) in enumerate(((w2_words, w2_scales), (w3_words, w3_scales))):
            nc.sync.dma_start(w23_words[:, b, :].bitcast(I32), words[0].bitcast(I32))
            for q in range(P // 32):
                nc.sync.dma_start(
                    w23_scales[32 * q : 32 * q + SCALE_ROWS, b, :].bitcast(I32),
                    scales[0, SCALE_ROWS * q : SCALE_ROWS * (q + 1), :].bitcast(I32),
                )

        out_rows = out.rearrange("(m p) v -> p m v", p=P)
        bands = [keep.tile([P, 2, HALF, PACK], BF16, name="bands%d" % c, align_bytes=64) for c in range(2)]
        band_words = [keep.tile([P, 2, HALF], U32, name="band_words%d" % c, align_bytes=64) for c in range(2)]
        band_scales = [keep.tile([P, 2, HALF], U8, name="band_scales%d" % c, align_bytes=64) for c in range(2)]

        def band_of(j, b):
            c, within = divmod(j * STEP, HALF)
            return bands[c][:, b, within : within + STEP, :]

        def haar(j, b, pairs):
            nc.vector.scalar_tensor_tensor(
                band_of(j, b)[:, pairs, :],
                banks[j][0][:, :, pairs].rearrange("p t v -> p v t"),
                0.0,
                rectified[j, 1][:, pairs, :],
                ALU.max,
                (ALU.add, ALU.subtract)[b],
            )

        def haar_turned(b, terms, tag):
            total = psum.tile([P, PACK, STEP], F32, name="sum%d" % b, tag=tag)
            for n, term in enumerate(terms):
                for t in range(PACK):
                    nc.tensor.matmul(
                        total[:, t, :], term[:, t, :], identity[:], is_transpose=True,
                        start=(n == 0 and t == 0), stop=(n == len(terms) - 1 and t == PACK - 1),
                    )
            nc.scalar.activation(band_of(TURNED, b), total[:].rearrange("p t v -> p v t"), ACT.Copy)

        def quantise_band(c, b, pairs):
            quantise((band_words[c][:, b, pairs], band_scales[c][:, b, pairs]), bands[c][:, b, pairs, :].rearrange("p v t -> p (v t)"))

        def second_product(dst, c, m, b, pairs):
            nc.tensor.matmul_mx(
                out=dst,
                lhsT=w23_words[:, b, 2 * P * m : 2 * P * (m + 1)].bitcast(FP4X4),
                lhsT_scale=w23_scales[:, b, P * m : P * (m + 1)],
                rhs=band_words[c][:, b, pairs].bitcast(FP8X4),
                rhs_scale=band_scales[c][:, b, pairs],
                start=(b == 0),
                stop=(b == 1),
            )

        whole, half = slice(0, STEP), slice(0, HALF)
        negated = keep.tile([P, PACK, P], F32, name="negated")
        nc.gpsimd.tensor_scalar(negated[:], rectified[TURNED, 1][:], -1.0, 0.0, ALU.mult, ALU.add)
        for pairs in parts_of(True):
            haar(0, 0, pairs)
            haar(0, 1, pairs)
        haar(1, 0, whole)
        haar(1, 1, whole)
        quantise_band(0, 0, half)
        quantise_band(0, 1, half)
        haar_turned(0, (rectified[TURNED, 1], rectified[TURNED, 0]), "bank%d" % (2 * TURNED + 1))
        haar_turned(1, (negated, rectified[TURNED, 0]), "bank1")

        accs_early = [psum.tile([P, HALF], F32, name="acc_early%d" % m, tag="bank%d" % (3 + 4 * m)) for m in range(N // P)]
        for b in range(2):
            for m in range(N // P):
                second_product(accs_early[m][:], 0, m, b, half)
        res_early = keep.tile([P, N // P, HALF], F32, name="res_early")
        for m in range(N // P):
            nc.scalar.activation(res_early[:, m, :], accs_early[m][:], ACT.Copy)
        nc.sync.dma_start(out_rows[:, :, 0:HALF], res_early[:])

        accs = [psum.tile([P, PACK * STEP], F32, name="acc_last%d" % m, tag="bank%d" % (2 * m)) for m in range(N // P)]
        last = slice(STEP, HALF)
        haar(3, 0, whole)
        quantise_band(1, 0, whole)
        haar(3, 1, whole)
        quantise_band(1, 1, whole)
        quantise_band(1, 0, last)
        quantise_band(1, 1, last)
        accs_turned = [psum.tile([P, PACK * STEP], F32, name="acc_turned%d" % m, tag="bank%d" % (4 + m)) for m in range(N // P)]
        for b in range(2):
            for m in range(N // P):
                second_product(accs_turned[m][:, 0:STEP], 1, m, b, whole)
        for b in range(2):
            for m in range(N // P):
                second_product(accs[m][:, 0:STEP], 1, m, b, last)
        res_late = keep.tile([P, N // P, HALF], F32, name="res_late")
        nc.scalar.activation(res_late[:, 0, whole], accs_turned[0][:, 0:STEP], ACT.Copy)
        nc.scalar.activation(res_late[:, 0, last], accs[0][:, 0:STEP], ACT.Copy)
        nc.vector.tensor_copy(res_late[:, 1, whole], accs_turned[1][:, 0:STEP])
        nc.vector.tensor_copy(res_late[:, 1, last], accs[1][:, 0:STEP])
        nc.sync.dma_start(out_rows[:, :, HALF:V], res_late[:])
